import numpy as np
import ml_dtypes


def mxq(x, axis, fmt="e4m3"):
    dtype, down = {"e4m3": (ml_dtypes.float8_e4m3fn, 7), "e5m2": (ml_dtypes.float8_e5m2, 14)}[fmt]
    v = np.moveaxis(np.asarray(x, np.float32).astype(ml_dtypes.bfloat16).astype(np.float64), axis, -1)
    blocks = v.reshape(v.shape[:-1] + (-1, 32))
    amax = np.abs(blocks).max(-1, keepdims=True)
    byte = np.maximum(np.where(amax > 0, np.frexp(amax)[1] - 1 + 127, 0) - down, 1)
    scale = np.exp2(byte - 127.0)
    codes = (blocks / scale).astype(np.float32).astype(dtype).astype(np.float64)
    return np.moveaxis((codes * scale).reshape(v.shape), -1, axis)


WIDE = False


def mx_kscale(k):
    if not WIDE:
        return np.ones(k)
    levels = np.array([24, -24, 12, -12, 0])
    if k % 512:
        return np.exp2(np.random.permutation(np.resize(levels, k // 32))).repeat(32)
    a = np.empty((k // 512, 16))
    for p in range(k // 512):
        a[p, :8] = np.random.permutation(np.resize(levels, 8))
        for g in range(8):
            far = levels[np.abs(levels - a[p, g]) >= 10]
            a[p, g + 8] = far[np.random.randint(len(far))]
    return np.exp2(a.ravel()).repeat(32)


def f64(x):
    return np.asarray(x).astype(np.float64)


def striped(idx):
    return np.tile(idx.reshape(-1, 16).T, (8, 1)).astype(np.uint16)


def unstriped(offs):
    return offs[:16].T.reshape(-1).astype(np.int64)


E2M1 = np.array([0.0, 0.5, 1.0, 1.5, 2.0, 3.0, 4.0, 6.0, -0.0, -0.5, -1.0, -1.5, -2.0, -3.0, -4.0, -6.0])


def pack_weight(w, fmt):
    k, n = w.shape
    w = f64(np.asarray(w, np.float32).astype(ml_dtypes.bfloat16)).reshape(k // 32, 32, n)
    amax = np.abs(w).max(1)
    if fmt == "e4m3":
        byte = np.frexp(amax)[1] - 1 + 127 - 7
    else:
        mant, ex = np.frexp(amax / 6.0)
        byte = np.where(mant > 0.5, ex, ex - 1) + 127
    byte = np.clip(np.where(amax > 0, byte, 1), 1, 254)
    scaled = (w * np.exp2(127.0 - byte)[:, None, :]).reshape(k, n).astype(np.float32)
    by_word = np.ascontiguousarray(scaled.reshape(k // 512, 128, 4, n).transpose(0, 1, 3, 2))
    if fmt == "e4m3":
        words = by_word.astype(ml_dtypes.float8_e4m3fn).view(np.uint8)
    else:
        c = by_word.astype(ml_dtypes.float4_e2m1fn).view(np.uint8) & 0xF
        words = (c[..., 0::2] | (c[..., 1::2] << 4)).reshape(k // 512, 128, 2 * n)
    return np.ascontiguousarray(words), np.ascontiguousarray(byte.astype(np.uint8).reshape(k // 512, 16, n))


def unpack_weight(words, scales, fmt):
    g, _, n = scales.shape
    words = np.ascontiguousarray(words).reshape(g, 128, n, -1)
    if fmt == "e4m3":
        vals = words.view(ml_dtypes.float8_e4m3fn).astype(np.float64)
    else:
        nib = np.empty((g, 128, n, 4), np.uint8)
        nib[..., 0::2] = words & 0xF
        nib[..., 1::2] = words >> 4
        vals = E2M1[nib]
    vals = vals * np.repeat(np.exp2(scales.astype(np.float64) - 127.0), 8, axis=1)[..., None]
    return vals.transpose(0, 1, 3, 2).reshape(g * 512, n)


def silu(f):
    return f / (1.0 + np.exp(-np.maximum(f, -700.0)))


K, R, N, T, J = 512, 512, 512, 2048, 1024


def setup_inputs():
    n = np.random.standard_normal
    s = mx_kscale(K)[:, None]
    u = mx_kscale(R)[:, None]
    p_tab = pack_weight(n((K, T)) * s, "e4m3")
    p_wd = pack_weight(n((R, N)) / np.sqrt(R) / u, "e4m3")
    return {
        "tab_words": p_tab[0],
        "tab_scales": p_tab[1],
        "ws": (n((K, R)) / np.sqrt(2 * K) / s).astype(np.float32),
        "wt": (n((K, R)) / np.sqrt(2 * K) / s).astype(np.float32),
        "sm": (np.random.uniform(0.5, 2.0, R) * u[:, 0]).astype(np.float32),
        "wd_words": p_wd[0],
        "wd_scales": p_wd[1],
        "gT": (n((N, T))).astype(np.float32),
        "wgo": np.tile(np.random.uniform(0.5, 2.0, J), (128, 1)).astype(np.float32),
        "offs": striped(np.random.permutation(T)[:J]),
        "offs2": striped(np.random.permutation(T)[:J]),
    }


def reference(tab_words, tab_scales, ws, wt, sm, wd_words, wd_scales, gT, wgo, offs, offs2):
    idx = unstriped(offs)
    idx2 = unstriped(offs2)
    tab_ = unpack_weight(tab_words, tab_scales, "e4m3")[:, idx]
    tabb_ = unpack_weight(tab_words, tab_scales, "e4m3")[:, idx2]
    ws_ = mxq(f64(ws), 0, "e4m3")
    wt_ = mxq(f64(wt), 0, "e4m3")
    a = ws_.T @ tab_ + wt_.T @ tabb_
    h = f64(sm)[:, None] * silu(a)
    h_ = mxq(h, 0, "e4m3")
    wd_ = unpack_weight(wd_words, wd_scales, "e4m3")
    y = wd_.T @ h_
    out = np.zeros((N, T))
    out[:, idx2] = f64(wgo)[0] * (y * f64(gT)[:, idx])
    return out

@@ -1,0 +1,225 @@
+from contextlib import ExitStack
+
+import concourse.mybir as mybir
+
+K, R, N, T, J = 512, 512, 512, 2048, 1024
+FLOPS = 2 * J * (2 * K * R + R * N)
+
+F32 = mybir.dt.float32
+BF16 = mybir.dt.bfloat16
+I32 = mybir.dt.int32
+U32 = mybir.dt.uint32
+U16 = mybir.dt.uint16
+U8 = mybir.dt.uint8
+FP8X4 = mybir.dt.float8_e4m3fn_x4
+MULT = mybir.AluOpType.mult
+ACT = mybir.ActivationFunctionType
+
+P = 128
+PACK = 4
+GROUP = 16
+CHUNK = 256
+HALF = 512
+N_TILES = N // P
+
+
+def load_scale_rows(nc, plane, rows):
+    width = plane.shape[1]
+    for q in range(4):
+        src = rows[4 * q : 4 * q + 4, :].bitcast(I32)
+        nc.sync.dma_start(
+            out=plane[32 * q : 32 * (q + 1), :],
+            in_=src.unsqueeze(0).to_broadcast([8, 4, width]),
+        )
+
+
+def tile_list_msg_silu_gate_kernel(
+    tc, tab_words, tab_scales, ws, wt, sm, wd_words, wd_scales, gT, wgo, offs, offs2, out
+):
+    nc = tc.nc
+
+    with ExitStack() as ctx:
+        keep = ctx.enter_context(tc.tile_pool(name="keep", bufs=1))
+        stage = ctx.enter_context(tc.tile_pool(name="stage", bufs=2))
+        psum = ctx.enter_context(tc.psum_pool(name="psum", bufs=2))
+
+        src_list = keep.tile([P, J // GROUP], U16, name="src_list")
+        dst_list = keep.tile([P, J // GROUP], U16, name="dst_list")
+        nc.sync.dma_start(src_list[:], offs)
+        nc.sync.dma_start(dst_list[:], offs2)
+        lists = (src_list, dst_list)
+
+        tab_plane = keep.tile([P, T // 4], I32, name="tab_plane", align_bytes=64)
+        load_scale_rows(nc, tab_plane[:], tab_scales[0])
+
+        w_raw = [keep.tile([P, PACK, R], F32, name=f"w_raw{i}", align_bytes=64) for i in range(2)]
+        tab = keep.tile([P, T], I32, name="tab", tag="tab_then_out", align_bytes=64)
+        nc.sync.dma_start(out=w_raw[0][:], in_=ws.rearrange("(p i) r -> p i r", i=PACK))
+        nc.sync.dma_start(out=tab[:], in_=tab_words[0].rearrange("p t i -> p (t i)").bitcast(I32))
+        nc.sync.dma_start(out=w_raw[1][:], in_=wt.rearrange("(p i) r -> p i r", i=PACK))
+        sm_cols = keep.tile([P, PACK], F32, name="sm_cols")
+        nc.sync.dma_start(out=sm_cols[:], in_=sm.rearrange("(p t) -> p t", t=PACK))
+        edge_w = keep.tile([P, J], F32, name="edge_w")
+        nc.sync.dma_start(out=edge_w[:], in_=wgo)
+        gates = [keep.tile([P, T], F32, name=f"gates{n}") for n in range(N_TILES)]
+        nc.sync.dma_start(out=gates[0][:], in_=gT[0:P, :])
+        wd_codes = keep.tile([P, N], I32, name="wd_codes", align_bytes=64)
+        wd_plane = keep.tile([P, N // 4], I32, name="wd_plane", align_bytes=64)
+        nc.sync.dma_start(out=wd_codes[:], in_=wd_words[0].rearrange("p n i -> p (n i)").bitcast(I32))
+        load_scale_rows(nc, wd_plane[:], wd_scales[0])
+        for n in range(1, N_TILES):
+            nc.sync.dma_start(out=gates[n][:], in_=gT[n * P : (n + 1) * P, :])
+
+        outs = [keep.tile([P, T], F32, name=f"out{n}", align_bytes=64) for n in range(2)]
+        for n in range(2):
+            nc.vector.memset(outs[n][:], 0.0)
+
+        v_codes = [keep.tile([P, J], U32, name=f"v_codes{i}", align_bytes=64) for i in range(2)]
+        v_scales = [keep.tile([P, J], U8, name=f"v_scales{i}", align_bytes=64) for i in range(2)]
+        for i in range(2):
+            nc.vector.tensor_copy(v_scales[i][:], tab_plane[:].bitcast(U8).indirect(lists[i][:]))
+
+        def gather_words(half):
+            for i in range(2):
+                nc.vector.tensor_copy(
+                    v_codes[i][:, half * HALF : (half + 1) * HALF],
+                    tab[:].bitcast(U32).indirect(
+                        lists[i][:, half * HALF // GROUP : (half + 1) * HALF // GROUP]
+                    ),
+                )
+
+        gather_words(0)
+
+        w_bf = keep.tile([P, 2, PACK * R], BF16, name="w_bf", tag="w_bf_then_out", align_bytes=64)
+        w_codes = keep.tile([P, 2, R], U32, name="w_codes", align_bytes=64)
+        w_scales = keep.tile([P, 2, R], U8, name="w_scales", align_bytes=64)
+        for i in range(2):
+            nc.scalar.copy(
+                out=w_bf[:, i, :].rearrange("p (t m i) -> p m t i", t=PACK, i=PACK),
+                in_=w_raw[i][:].rearrange("p i (m t) -> p m t i", t=PACK),
+            )
+        for i in range(2):
+            nc.vector.quantize_mx(
+                out=w_codes[:, i, :].bitcast(FP8X4), scales=w_scales[:, i, :], in_=w_bf[:, i, :]
+            )
+
+        gather_words(1)
+
+        outs.append(keep.tile([P, T], F32, name="out2", tag="w_bf_then_out", align_bytes=64))
+        outs.append(keep.tile([P, T], F32, name="out3", tag="tab_then_out", align_bytes=64))
+        for n in range(2, N_TILES):
+            nc.gpsimd.memset(outs[n][:], 0.0)
+
+        msgs = [
+            [keep.tile([P, 2, w], F32, name=f"msgs{s}_{b}") for b in range(2)]
+            for s, w in enumerate((CHUNK, CHUNK, HALF))
+        ]
+        gated = {}
+
+        def gather_gates(pieces, tag):
+            tile = keep.tile([P, sum(hi - lo for n, lo, hi in pieces)], F32, name=f"gated_{tag}", tag=tag)
+            at = 0
+            for n, lo, hi in pieces:
+                dst = tile[:, at : at + hi - lo]
+                nc.vector.tensor_tensor(
+                    dst,
+                    gates[n][:].indirect(src_list[:, lo // GROUP : hi // GROUP]),
+                    edge_w[:, lo:hi],
+                    MULT,
+                )
+                for start in range(lo, hi, CHUNK):
+                    gated[n, start] = dst[:, start - lo :]
+                at += hi - lo
+
+        def hidden(c):
+            cols = slice(c * CHUNK, (c + 1) * CHUNK)
+            act = stage.tile([P, PACK, CHUNK], F32, name="act")
+            for b in range(2):
+                acc = psum.tile([P, 2, CHUNK], F32, name=f"acc{b}")
+                for u in range(2):
+                    rows = slice((2 * b + u) * P, (2 * b + u + 1) * P)
+                    for i in range(2):
+                        nc.tensor.matmul_mx(
+                            out=acc[:, u, :],
+                            lhsT=w_codes[:, i, rows].bitcast(FP8X4),
+                            lhsT_scale=w_scales[:, i, rows],
+                            rhs=v_codes[i][:, cols].bitcast(FP8X4),
+                            rhs_scale=v_scales[i][:, cols],
+                            start=(i == 0),
+                            stop=(i == 1),
+                        )
+                nc.scalar.activation(act[:, 2 * b : 2 * b + 2, :], acc[:], ACT.Silu)
+            h_rows = keep.tile([P, PACK, CHUNK], BF16, name=f"h_rows{c}", tag=f"shared{c}")
+            for t in range(PACK):
+                nc.scalar.activation(
+                    h_rows[:, t, :], act[:, t, :], ACT.Copy, scale=sm_cols[:, t : t + 1]
+                )
+            h_bf = stage.tile([P, CHUNK, PACK], BF16, name="h_bf", align_bytes=64)
+            nc.scalar.copy(
+                out=h_bf[:].rearrange("p (c i) t -> p c t i", i=4),
+                in_=h_rows[:].rearrange("p t (c i) -> p c t i", i=4),
+            )
+            return h_bf
+
+        def message(c, h_bf):
+            h_codes = stage.tile([P, CHUNK], U32, name="h_codes", align_bytes=64)
+            h_scales = stage.tile([P, CHUNK], U8, name="h_scales", align_bytes=64)
+            nc.vector.quantize_mx(
+                out=h_codes[:].bitcast(FP8X4),
+                scales=h_scales[:],
+                in_=h_bf[:].rearrange("p c t -> p (c t)"),
+            )
+            span = min(c, 2)
+            at = (c - span) * CHUNK
+            for b in range(2):
+                acc = psum.tile([P, 2, CHUNK], F32, name=f"y_acc{b}")
+                for u in range(2):
+                    rows = slice((2 * b + u) * P, (2 * b + u + 1) * P)
+                    nc.tensor.matmul_mx(
+                        out=acc[:, u, :],
+                        lhsT=wd_codes[:, rows].bitcast(FP8X4),
+                        lhsT_scale=wd_plane[:].bitcast(U8)[:, rows],
+                        rhs=h_codes[:].bitcast(FP8X4),
+                        rhs_scale=h_scales[:],
+                        start=True,
+                        stop=True,
+                    )
+                nc.scalar.copy(out=msgs[span][b][:, :, at : at + CHUNK], in_=acc[:])
+
+        def scatter(n, lo, hi):
+            span = min(lo // CHUNK, 2)
+            at = lo - span * CHUNK
+            nc.vector.tensor_tensor(
+                outs[n][:].indirect(dst_list[:, lo // GROUP : hi // GROUP]),
+                msgs[span][n // 2][:, n % 2, at : at + hi - lo],
+                gated[n, lo][:, 0 : hi - lo],
+                MULT,
+            )
+            if hi == J:
+                nc.sync.dma_start(out=out[n * P : (n + 1) * P, :], in_=outs[n][:])
+
+        c1, c2, c3 = CHUNK, 2 * CHUNK, 3 * CHUNK
+        gather_gates([(0, 0, J), (1, 0, J)], "early")
+        message(0, hidden(0))
+        gather_gates([(2, 0, J)], "shared0")
+        h1 = hidden(1)
+        h2 = hidden(2)
+        for n in range(3):
+            scatter(n, 0, c1)
+        message(1, h1)
+        gather_gates([(3, 0, c1)], "shared1")
+        h3 = hidden(3)
+        scatter(3, 0, c1)
+        for n in range(3):
+            scatter(n, c1, c2)
+        message(2, h2)
+        gather_gates([(3, c1, c2)], "shared2")
+        scatter(3, c1, c2)
+        scatter(0, c2, c3)
+        message(3, h3)
+        gather_gates([(3, c2, J)], "shared3")
+        scatter(3, c2, c3)
+        scatter(3, c3, J)
+        scatter(0, c3, J)
+        scatter(1, c2, J)
+        scatter(2, c2, J)

@@ -21,6 +21,8 @@ GROUP = 16
 CHUNK = 256
 HALF = 512
 N_TILES = N // P
+HIDDEN_BANKS = ((0, 1), (2, 3), (4, 3), (5, 6))
+MESSAGE_BANKS = ((3, 4), (0, 1), (7, 2), (3, 4))
 
 
 def load_scale_rows(nc, plane, rows):
@@ -41,7 +43,7 @@ def tile_list_msg_silu_gate_kernel(
     with ExitStack() as ctx:
         keep = ctx.enter_context(tc.tile_pool(name="keep", bufs=1))
         stage = ctx.enter_context(tc.tile_pool(name="stage", bufs=2))
-        psum = ctx.enter_context(tc.psum_pool(name="psum", bufs=2))
+        psum = ctx.enter_context(tc.psum_pool(name="psum", bufs=1))
 
         src_list = keep.tile([P, J // GROUP], U16, name="src_list")
         dst_list = keep.tile([P, J // GROUP], U16, name="dst_list")
@@ -52,37 +54,45 @@ def tile_list_msg_silu_gate_kernel(
         tab_plane = keep.tile([P, T // 4], I32, name="tab_plane", align_bytes=64)
         load_scale_rows(nc, tab_plane[:], tab_scales[0])
 
-        w_raw = [keep.tile([P, PACK, R], F32, name=f"w_raw{i}", align_bytes=64) for i in range(2)]
+        ws_raw = keep.tile([P, PACK, R], F32, name="ws_raw", align_bytes=64)
         tab = keep.tile([P, T], I32, name="tab", tag="tab_then_out", align_bytes=64)
-        nc.sync.dma_start(out=w_raw[0][:], in_=ws.rearrange("(p i) r -> p i r", i=PACK))
+        nc.sync.dma_start(out=ws_raw[:], in_=ws.rearrange("(p i) r -> p i r", i=PACK))
         nc.sync.dma_start(out=tab[:], in_=tab_words[0].rearrange("p t i -> p (t i)").bitcast(I32))
-        nc.sync.dma_start(out=w_raw[1][:], in_=wt.rearrange("(p i) r -> p i r", i=PACK))
+        wt_raw = [keep.tile([P, PACK, R // 2], F32, name=f"wt_raw{u}", align_bytes=64) for u in range(2)]
+        for u in range(2):
+            cols = slice(u * R // 2, (u + 1) * R // 2)
+            nc.sync.dma_start(out=wt_raw[u][:], in_=wt[:, cols].rearrange("(p i) r -> p i r", i=PACK))
         sm_cols = keep.tile([P, PACK], F32, name="sm_cols")
         nc.sync.dma_start(out=sm_cols[:], in_=sm.rearrange("(p t) -> p t", t=PACK))
-        edge_w = keep.tile([P, J], F32, name="edge_w")
-        nc.sync.dma_start(out=edge_w[:], in_=wgo)
-        gates = [keep.tile([P, T], F32, name=f"gates{n}") for n in range(N_TILES)]
-        nc.sync.dma_start(out=gates[0][:], in_=gT[0:P, :])
         wd_codes = keep.tile([P, N], I32, name="wd_codes", align_bytes=64)
         wd_plane = keep.tile([P, N // 4], I32, name="wd_plane", align_bytes=64)
         nc.sync.dma_start(out=wd_codes[:], in_=wd_words[0].rearrange("p n i -> p (n i)").bitcast(I32))
         load_scale_rows(nc, wd_plane[:], wd_scales[0])
-        for n in range(1, N_TILES):
+        edge_w = keep.tile([P, J], F32, name="edge_w")
+        nc.sync.dma_start(out=edge_w[:], in_=wgo)
+        gates = [keep.tile([P, T], F32, name=f"gates{n}", align_bytes=64) for n in range(N_TILES)]
+        for n in range(2):
+            nc.sync.dma_start(out=gates[n][:], in_=gT[n * P : (n + 1) * P, :])
+        for n in range(2, N_TILES):
             nc.sync.dma_start(out=gates[n][:], in_=gT[n * P : (n + 1) * P, :])
 
         outs = [keep.tile([P, T], F32, name=f"out{n}", align_bytes=64) for n in range(2)]
         for n in range(2):
             nc.vector.memset(outs[n][:], 0.0)
 
-        v_codes = [keep.tile([P, J], U32, name=f"v_codes{i}", align_bytes=64) for i in range(2)]
+        v_codes = {}
         v_scales = [keep.tile([P, J], U8, name=f"v_scales{i}", align_bytes=64) for i in range(2)]
         for i in range(2):
             nc.vector.tensor_copy(v_scales[i][:], tab_plane[:].bitcast(U8).indirect(lists[i][:]))
 
         def gather_words(half):
             for i in range(2):
+                slot = "wt_raw1" if (half, i) == (1, 1) else f"v_codes{half}_{i}"
+                v_codes[half, i] = keep.tile(
+                    [P, HALF], U32, name=f"v_codes{half}_{i}", tag=slot, align_bytes=64
+                )
                 nc.vector.tensor_copy(
-                    v_codes[i][:, half * HALF : (half + 1) * HALF],
+                    v_codes[half, i][:],
                     tab[:].bitcast(U32).indirect(
                         lists[i][:, half * HALF // GROUP : (half + 1) * HALF // GROUP]
                     ),
@@ -93,10 +103,12 @@ def tile_list_msg_silu_gate_kernel(
         w_bf = keep.tile([P, 2, PACK * R], BF16, name="w_bf", tag="w_bf_then_out", align_bytes=64)
         w_codes = keep.tile([P, 2, R], U32, name="w_codes", align_bytes=64)
         w_scales = keep.tile([P, 2, R], U8, name="w_scales", align_bytes=64)
-        for i in range(2):
+        w_view = w_bf[:].rearrange("p w (t m i) -> p w m t i", t=PACK, i=PACK)
+        nc.scalar.copy(out=w_view[:, 0], in_=ws_raw[:].rearrange("p i (m t) -> p m t i", t=PACK))
+        for u in range(2):
             nc.scalar.copy(
-                out=w_bf[:, i, :].rearrange("p (t m i) -> p m t i", t=PACK, i=PACK),
-                in_=w_raw[i][:].rearrange("p i (m t) -> p m t i", t=PACK),
+                out=w_view[:, 1, u * P // 2 : (u + 1) * P // 2],
+                in_=wt_raw[u][:].rearrange("p i (m t) -> p m t i", t=PACK),
             )
         for i in range(2):
             nc.vector.quantize_mx(
@@ -110,14 +122,11 @@ def tile_list_msg_silu_gate_kernel(
         for n in range(2, N_TILES):
             nc.gpsimd.memset(outs[n][:], 0.0)
 
-        msgs = [
-            [keep.tile([P, 2, w], F32, name=f"msgs{s}_{b}") for b in range(2)]
-            for s, w in enumerate((CHUNK, CHUNK, HALF))
-        ]
+        msgs = {}
         gated = {}
 
         def gather_gates(pieces, tag):
-            tile = keep.tile([P, sum(hi - lo for n, lo, hi in pieces)], F32, name=f"gated_{tag}", tag=tag)
+            tile = keep.tile([P, sum(hi - lo for n, lo, hi in pieces)], F32, name=f"gated_{tag}", tag=tag, align_bytes=64)
             at = 0
             for n, lo, hi in pieces:
                 dst = tile[:, at : at + hi - lo]
@@ -135,7 +144,7 @@ def tile_list_msg_silu_gate_kernel(
             cols = slice(c * CHUNK, (c + 1) * CHUNK)
             act = stage.tile([P, PACK, CHUNK], F32, name="act")
             for b in range(2):
-                acc = psum.tile([P, 2, CHUNK], F32, name=f"acc{b}")
+                acc = psum.tile([P, 2, CHUNK], F32, name=f"acc{c}_{b}", tag=f"bank{HIDDEN_BANKS[c][b]}")
                 for u in range(2):
                     rows = slice((2 * b + u) * P, (2 * b + u + 1) * P)
                     for i in range(2):
@@ -143,26 +152,26 @@ def tile_list_msg_silu_gate_kernel(
                             out=acc[:, u, :],
                             lhsT=w_codes[:, i, rows].bitcast(FP8X4),
                             lhsT_scale=w_scales[:, i, rows],
-                            rhs=v_codes[i][:, cols].bitcast(FP8X4),
+                            rhs=v_codes[c // 2, i][:, c % 2 * CHUNK : (c % 2 + 1) * CHUNK].bitcast(FP8X4),
                             rhs_scale=v_scales[i][:, cols],
                             start=(i == 0),
                             stop=(i == 1),
                         )
                 nc.scalar.activation(act[:, 2 * b : 2 * b + 2, :], acc[:], ACT.Silu)
-            h_rows = keep.tile([P, PACK, CHUNK], BF16, name=f"h_rows{c}", tag=f"shared{c}")
+            h_rows = keep.tile([P, PACK, CHUNK], BF16, name=f"h_rows{c}", align_bytes=64)
             for t in range(PACK):
                 nc.scalar.activation(
                     h_rows[:, t, :], act[:, t, :], ACT.Copy, scale=sm_cols[:, t : t + 1]
                 )
-            h_bf = stage.tile([P, CHUNK, PACK], BF16, name="h_bf", align_bytes=64)
+            h_bf = keep.tile([P, CHUNK, PACK], BF16, name=f"h_bf{c}", align_bytes=64)
             nc.scalar.copy(
                 out=h_bf[:].rearrange("p (c i) t -> p c t i", i=4),
                 in_=h_rows[:].rearrange("p t (c i) -> p c t i", i=4),
             )
             return h_bf
 
-        def message(c, h_bf):
-            h_codes = stage.tile([P, CHUNK], U32, name="h_codes", align_bytes=64)
+        def message(c, h_bf, tag):
+            h_codes = keep.tile([P, CHUNK], U32, name=f"h_codes{c}", tag=tag, align_bytes=64)
             h_scales = stage.tile([P, CHUNK], U8, name="h_scales", align_bytes=64)
             nc.vector.quantize_mx(
                 out=h_codes[:].bitcast(FP8X4),
@@ -171,8 +180,15 @@ def tile_list_msg_silu_gate_kernel(
             )
             span = min(c, 2)
             at = (c - span) * CHUNK
+            if at == 0:
+                width = CHUNK if span < 2 else HALF
+                for b in range(2):
+                    slot = f"h_rows{c + 1}" if (c > 0 and b == 0) else f"msgs{span}_{b}"
+                    msgs[span, b] = keep.tile(
+                        [P, 2, width], F32, name=f"msgs{span}_{b}", tag=slot, align_bytes=64
+                    )
             for b in range(2):
-                acc = psum.tile([P, 2, CHUNK], F32, name=f"y_acc{b}")
+                acc = psum.tile([P, 2, CHUNK], F32, name=f"y_acc{c}_{b}", tag=f"bank{MESSAGE_BANKS[c][b]}")
                 for u in range(2):
                     rows = slice((2 * b + u) * P, (2 * b + u + 1) * P)
                     nc.tensor.matmul_mx(
@@ -184,42 +200,38 @@ def tile_list_msg_silu_gate_kernel(
                         start=True,
                         stop=True,
                     )
-                nc.scalar.copy(out=msgs[span][b][:, :, at : at + CHUNK], in_=acc[:])
+                nc.scalar.copy(out=msgs[span, b][:, :, at : at + CHUNK], in_=acc[:])
 
         def scatter(n, lo, hi):
             span = min(lo // CHUNK, 2)
             at = lo - span * CHUNK
             nc.vector.tensor_tensor(
                 outs[n][:].indirect(dst_list[:, lo // GROUP : hi // GROUP]),
-                msgs[span][n // 2][:, n % 2, at : at + hi - lo],
+                msgs[span, n // 2][:, n % 2, at : at + hi - lo],
                 gated[n, lo][:, 0 : hi - lo],
                 MULT,
             )
             if hi == J:
                 nc.sync.dma_start(out=out[n * P : (n + 1) * P, :], in_=outs[n][:])
 
-        c1, c2, c3 = CHUNK, 2 * CHUNK, 3 * CHUNK
+        c1, c2 = CHUNK, 2 * CHUNK
         gather_gates([(0, 0, J), (1, 0, J)], "early")
-        message(0, hidden(0))
-        gather_gates([(2, 0, J)], "shared0")
+        message(0, hidden(0), "gates1")
+        gather_gates([(2, 0, J)], "h_bf0")
         h1 = hidden(1)
         h2 = hidden(2)
         for n in range(3):
             scatter(n, 0, c1)
-        message(1, h1)
-        gather_gates([(3, 0, c1)], "shared1")
+        message(1, h1, "msgs0_0")
+        gather_gates([(3, 0, c1)], "h_bf1")
         h3 = hidden(3)
         scatter(3, 0, c1)
-        for n in range(3):
-            scatter(n, c1, c2)
-        message(2, h2)
-        gather_gates([(3, c1, c2)], "shared2")
+        message(2, h2, "msgs0_1")
+        scatter(0, c1, c2)
+        scatter(1, c1, c2)
+        scatter(2, c1, c2)
+        message(3, h3, "h_rows2")
+        gather_gates([(3, c1, J)], "h_bf3")
         scatter(3, c1, c2)
-        scatter(0, c2, c3)
-        message(3, h3)
-        gather_gates([(3, c2, J)], "shared3")
-        scatter(3, c2, c3)
-        scatter(3, c3, J)
-        scatter(0, c3, J)
-        scatter(1, c2, J)
-        scatter(2, c2, J)
+        for n in range(N_TILES):
+            scatter(n, c2, J)

@@ -55,7 +55,7 @@ def tile_list_msg_silu_gate_kernel(
         load_scale_rows(nc, tab_plane[:], tab_scales[0])
 
         ws_raw = keep.tile([P, PACK, R], F32, name="ws_raw", align_bytes=64)
-        tab = keep.tile([P, T], I32, name="tab", tag="tab_then_out", align_bytes=64)
+        tab = keep.tile([P, T], I32, name="tab", align_bytes=64)
         nc.sync.dma_start(out=ws_raw[:], in_=ws.rearrange("(p i) r -> p i r", i=PACK))
         nc.sync.dma_start(out=tab[:], in_=tab_words[0].rearrange("p t i -> p (t i)").bitcast(I32))
         wt_raw = [keep.tile([P, PACK, R // 2], F32, name=f"wt_raw{u}", align_bytes=64) for u in range(2)]
@@ -100,7 +100,7 @@ def tile_list_msg_silu_gate_kernel(
 
         gather_words(0)
 
-        w_bf = keep.tile([P, 2, PACK * R], BF16, name="w_bf", tag="w_bf_then_out", align_bytes=64)
+        w_bf = keep.tile([P, 2, PACK * R], BF16, name="w_bf", align_bytes=64)
         w_codes = keep.tile([P, 2, R], U32, name="w_codes", align_bytes=64)
         w_scales = keep.tile([P, 2, R], U8, name="w_scales", align_bytes=64)
         w_view = w_bf[:].rearrange("p w (t m i) -> p w m t i", t=PACK, i=PACK)
@@ -116,11 +116,6 @@ def tile_list_msg_silu_gate_kernel(
             )
 
         gather_words(1)
-
-        outs.append(keep.tile([P, T], F32, name="out2", tag="w_bf_then_out", align_bytes=64))
-        outs.append(keep.tile([P, T], F32, name="out3", tag="tab_then_out", align_bytes=64))
-        for n in range(2, N_TILES):
-            nc.gpsimd.memset(outs[n][:], 0.0)
 
         msgs = {}
         gated = {}
@@ -172,7 +167,7 @@ def tile_list_msg_silu_gate_kernel(
 
         def message(c, h_bf, tag):
             h_codes = keep.tile([P, CHUNK], U32, name=f"h_codes{c}", tag=tag, align_bytes=64)
-            h_scales = stage.tile([P, CHUNK], U8, name="h_scales", align_bytes=64)
+            h_scales = keep.tile([P, CHUNK], U8, name=f"h_scales{c}", align_bytes=64)
             nc.vector.quantize_mx(
                 out=h_codes[:].bitcast(FP8X4),
                 scales=h_scales[:],
@@ -218,6 +213,9 @@ def tile_list_msg_silu_gate_kernel(
         gather_gates([(0, 0, J), (1, 0, J)], "early")
         message(0, hidden(0), "gates1")
         gather_gates([(2, 0, J)], "h_bf0")
+        for n, slot in ((2, "gates1"), (3, "h_scales0")):
+            outs.append(keep.tile([P, T], F32, name=f"out{n}", tag=slot, align_bytes=64))
+            nc.gpsimd.memset(outs[n][:], 0.0)
         h1 = hidden(1)
         h2 = hidden(2)
         for n in range(3):

@@ -76,29 +76,26 @@ def tile_list_msg_silu_gate_kernel(
         for n in range(2, N_TILES):
             nc.sync.dma_start(out=gates[n][:], in_=gT[n * P : (n + 1) * P, :])
 
-        outs = [keep.tile([P, T], F32, name=f"out{n}", align_bytes=64) for n in range(2)]
-        for n in range(2):
-            nc.vector.memset(outs[n][:], 0.0)
+        outs = [keep.tile([P, T], F32, name=f"out{n}", align_bytes=64) for n in range(N_TILES)]
+        for n in range(N_TILES):
+            nc.vector.memset(outs[n][:].bitcast(I32), 0)
 
         v_codes = {}
         v_scales = [keep.tile([P, J], U8, name=f"v_scales{i}", align_bytes=64) for i in range(2)]
         for i in range(2):
             nc.vector.tensor_copy(v_scales[i][:], tab_plane[:].bitcast(U8).indirect(lists[i][:]))
 
-        def gather_words(half):
+        def gather_words(half, slot):
+            v_codes[half] = keep.tile([P, 2, HALF], U32, name=f"v_codes{half}", tag=slot, align_bytes=64)
             for i in range(2):
-                slot = "wt_raw1" if (half, i) == (1, 1) else f"v_codes{half}_{i}"
-                v_codes[half, i] = keep.tile(
-                    [P, HALF], U32, name=f"v_codes{half}_{i}", tag=slot, align_bytes=64
-                )
                 nc.vector.tensor_copy(
-                    v_codes[half, i][:],
+                    v_codes[half][:, i, :],
                     tab[:].bitcast(U32).indirect(
                         lists[i][:, half * HALF // GROUP : (half + 1) * HALF // GROUP]
                     ),
                 )
 
-        gather_words(0)
+        gather_words(0, "v_codes0")
 
         w_bf = keep.tile([P, 2, PACK * R], BF16, name="w_bf", align_bytes=64)
         w_codes = keep.tile([P, 2, R], U32, name="w_codes", align_bytes=64)
@@ -115,7 +112,7 @@ def tile_list_msg_silu_gate_kernel(
                 out=w_codes[:, i, :].bitcast(FP8X4), scales=w_scales[:, i, :], in_=w_bf[:, i, :]
             )
 
-        gather_words(1)
+        gather_words(1, "wt_raw1")
 
         msgs = {}
         gated = {}
@@ -147,7 +144,7 @@ def tile_list_msg_silu_gate_kernel(
                             out=acc[:, u, :],
                             lhsT=w_codes[:, i, rows].bitcast(FP8X4),
                             lhsT_scale=w_scales[:, i, rows],
-                            rhs=v_codes[c // 2, i][:, c % 2 * CHUNK : (c % 2 + 1) * CHUNK].bitcast(FP8X4),
+                            rhs=v_codes[c // 2][:, i, c % 2 * CHUNK : (c % 2 + 1) * CHUNK].bitcast(FP8X4),
                             rhs_scale=v_scales[i][:, cols],
                             start=(i == 0),
                             stop=(i == 1),
@@ -213,9 +210,6 @@ def tile_list_msg_silu_gate_kernel(
         gather_gates([(0, 0, J), (1, 0, J)], "early")
         message(0, hidden(0), "gates1")
         gather_gates([(2, 0, J)], "h_bf0")
-        for n, slot in ((2, "gates1"), (3, "h_scales0")):
-            outs.append(keep.tile([P, T], F32, name=f"out{n}", tag=slot, align_bytes=64))
-            nc.gpsimd.memset(outs[n][:], 0.0)
         h1 = hidden(1)
         h2 = hidden(2)
         for n in range(3):

@@ -26,13 +26,9 @@ MESSAGE_BANKS = ((3, 4), (0, 1), (7, 2), (3, 4))
 
 
 def load_scale_rows(nc, plane, rows):
-    width = plane.shape[1]
-    for q in range(4):
-        src = rows[4 * q : 4 * q + 4, :].bitcast(I32)
-        nc.sync.dma_start(
-            out=plane[32 * q : 32 * (q + 1), :],
-            in_=src.unsqueeze(0).to_broadcast([8, 4, width]),
-        )
+    by_place = rows.bitcast(I32).rearrange("(q r) w -> r q w", r=4)
+    for r in range(4):
+        nc.sync.dma_start(out=plane[r:P:32, :], in_=by_place[r])
 
 
 def tile_list_msg_silu_gate_kernel(
@@ -51,8 +47,14 @@ def tile_list_msg_silu_gate_kernel(
         nc.sync.dma_start(dst_list[:], offs2)
         lists = (src_list, dst_list)
 
+        sm_cols = keep.tile([P, PACK], F32, name="sm_cols")
+        nc.sync.dma_start(out=sm_cols[:], in_=sm.rearrange("(p t) -> p t", t=PACK))
+
         tab_plane = keep.tile([P, T // 4], I32, name="tab_plane", align_bytes=64)
-        load_scale_rows(nc, tab_plane[:], tab_scales[0])
+        wd_plane = keep.tile([P, N // 4], I32, name="wd_plane", align_bytes=64)
+        nc.gpsimd.memset(tab_plane[:], 0)
+        nc.gpsimd.memset(wd_plane[:], 0)
+        load_scale_rows(nc, tab_plane, tab_scales[0])
 
         ws_raw = keep.tile([P, PACK, R], F32, name="ws_raw", align_bytes=64)
         tab = keep.tile([P, T], I32, name="tab", align_bytes=64)
@@ -62,12 +64,9 @@ def tile_list_msg_silu_gate_kernel(
         for u in range(2):
             cols = slice(u * R // 2, (u + 1) * R // 2)
             nc.sync.dma_start(out=wt_raw[u][:], in_=wt[:, cols].rearrange("(p i) r -> p i r", i=PACK))
-        sm_cols = keep.tile([P, PACK], F32, name="sm_cols")
-        nc.sync.dma_start(out=sm_cols[:], in_=sm.rearrange("(p t) -> p t", t=PACK))
         wd_codes = keep.tile([P, N], I32, name="wd_codes", align_bytes=64)
-        wd_plane = keep.tile([P, N // 4], I32, name="wd_plane", align_bytes=64)
         nc.sync.dma_start(out=wd_codes[:], in_=wd_words[0].rearrange("p n i -> p (n i)").bitcast(I32))
-        load_scale_rows(nc, wd_plane[:], wd_scales[0])
+        load_scale_rows(nc, wd_plane, wd_scales[0])
         edge_w = keep.tile([P, J], F32, name="edge_w")
         nc.sync.dma_start(out=edge_w[:], in_=wgo)
         gates = [keep.tile([P, T], F32, name=f"gates{n}", align_bytes=64) for n in range(N_TILES)]
@@ -76,8 +75,8 @@ def tile_list_msg_silu_gate_kernel(
         for n in range(2, N_TILES):
             nc.sync.dma_start(out=gates[n][:], in_=gT[n * P : (n + 1) * P, :])
 
-        outs = [keep.tile([P, T], F32, name=f"out{n}", align_bytes=64) for n in range(N_TILES)]
-        for n in range(N_TILES):
+        outs = [keep.tile([P, T], F32, name=f"out{n}", align_bytes=64) for n in range(2)]
+        for n in range(2):
             nc.vector.memset(outs[n][:].bitcast(I32), 0)
 
         v_codes = {}
@@ -117,20 +116,9 @@ def tile_list_msg_silu_gate_kernel(
         msgs = {}
         gated = {}
 
-        def gather_gates(pieces, tag):
-            tile = keep.tile([P, sum(hi - lo for n, lo, hi in pieces)], F32, name=f"gated_{tag}", tag=tag, align_bytes=64)
-            at = 0
-            for n, lo, hi in pieces:
-                dst = tile[:, at : at + hi - lo]
-                nc.vector.tensor_tensor(
-                    dst,
-                    gates[n][:].indirect(src_list[:, lo // GROUP : hi // GROUP]),
-                    edge_w[:, lo:hi],
-                    MULT,
-                )
-                for start in range(lo, hi, CHUNK):
-                    gated[n, start] = dst[:, start - lo :]
-                at += hi - lo
+        def gather_gates(n, slot):
+            gated[n] = keep.tile([P, J], F32, name=f"gated{n}", tag=slot, align_bytes=64)
+            nc.vector.tensor_tensor(gated[n][:], gates[n][:].indirect(src_list[:]), edge_w[:], MULT)
 
         def hidden(c):
             cols = slice(c * CHUNK, (c + 1) * CHUNK)
@@ -170,15 +158,13 @@ def tile_list_msg_silu_gate_kernel(
                 scales=h_scales[:],
                 in_=h_bf[:].rearrange("p c t -> p (c t)"),
             )
-            span = min(c, 2)
-            at = (c - span) * CHUNK
-            if at == 0:
-                width = CHUNK if span < 2 else HALF
-                for b in range(2):
-                    slot = f"h_rows{c + 1}" if (c > 0 and b == 0) else f"msgs{span}_{b}"
-                    msgs[span, b] = keep.tile(
-                        [P, 2, width], F32, name=f"msgs{span}_{b}", tag=slot, align_bytes=64
-                    )
+            slot = f"h_rows{c + 1}" if c in (1, 2) else f"msgs_low{c}"
+            msgs[c, 0] = keep.tile([P, 2, CHUNK], F32, name=f"msgs_low{c}", tag=slot, align_bytes=64)[:]
+            if c < 3:
+                width = CHUNK if c < 2 else HALF
+                msgs[c, 1] = keep.tile([P, 2, width], F32, name=f"msgs_high{c}", align_bytes=64)[:]
+            else:
+                msgs[c, 1] = msgs[2, 1][:, :, CHUNK:]
             for b in range(2):
                 acc = psum.tile([P, 2, CHUNK], F32, name=f"y_acc{c}_{b}", tag=f"bank{MESSAGE_BANKS[c][b]}")
                 for u in range(2):
@@ -192,38 +178,40 @@ def tile_list_msg_silu_gate_kernel(
                         start=True,
                         stop=True,
                     )
-                nc.scalar.copy(out=msgs[span, b][:, :, at : at + CHUNK], in_=acc[:])
+                nc.scalar.copy(out=msgs[c, b][:, :, 0:CHUNK], in_=acc[:])
 
         def scatter(n, lo, hi):
-            span = min(lo // CHUNK, 2)
-            at = lo - span * CHUNK
             nc.vector.tensor_tensor(
                 outs[n][:].indirect(dst_list[:, lo // GROUP : hi // GROUP]),
-                msgs[span, n // 2][:, n % 2, at : at + hi - lo],
-                gated[n, lo][:, 0 : hi - lo],
+                msgs[lo // CHUNK, n // 2][:, n % 2, 0 : hi - lo],
+                gated[n][:, lo:hi],
                 MULT,
             )
             if hi == J:
                 nc.sync.dma_start(out=out[n * P : (n + 1) * P, :], in_=outs[n][:])
 
-        c1, c2 = CHUNK, 2 * CHUNK
-        gather_gates([(0, 0, J), (1, 0, J)], "early")
+        c1, c2, c3 = CHUNK, 2 * CHUNK, 3 * CHUNK
+        gather_gates(0, "gated0")
+        gather_gates(1, "gated1")
         message(0, hidden(0), "gates1")
-        gather_gates([(2, 0, J)], "h_bf0")
+        gather_gates(2, "h_bf0")
+        for n, slot in ((2, "gates1"), (3, "h_scales0")):
+            outs.append(keep.tile([P, T], F32, name=f"out{n}", tag=slot, align_bytes=64))
+            nc.gpsimd.memset(outs[n][:], 0.0)
         h1 = hidden(1)
         h2 = hidden(2)
         for n in range(3):
             scatter(n, 0, c1)
-        message(1, h1, "msgs0_0")
-        gather_gates([(3, 0, c1)], "h_bf1")
+        message(1, h1, "msgs_low0")
+        gather_gates(3, "h_bf1")
         h3 = hidden(3)
         scatter(3, 0, c1)
-        message(2, h2, "msgs0_1")
-        scatter(0, c1, c2)
-        scatter(1, c1, c2)
-        scatter(2, c1, c2)
-        message(3, h3, "h_rows2")
-        gather_gates([(3, c1, J)], "h_bf3")
-        scatter(3, c1, c2)
+        message(2, h2, "msgs_high0")
         for n in range(N_TILES):
+            scatter(n, c1, c2)
+        message(3, h3, "h_rows2")
+        for lo, hi in ((c2, c3), (c3, J)):
+            for n in range(2):
+                scatter(n, lo, hi)
+        for n in range(2, N_TILES):
             scatter(n, c2, J)

@@ -18,11 +18,9 @@ ACT = mybir.ActivationFunctionType
 P = 128
 PACK = 4
 GROUP = 16
-CHUNK = 256
-HALF = 512
+HALF = J // 2
+QUARTER = J // 4
 N_TILES = N // P
-HIDDEN_BANKS = ((0, 1), (2, 3), (4, 3), (5, 6))
-MESSAGE_BANKS = ((3, 4), (0, 1), (7, 2), (3, 4))
 
 
 def load_scale_rows(nc, plane, rows):
@@ -38,8 +36,10 @@ def tile_list_msg_silu_gate_kernel(
 
     with ExitStack() as ctx:
         keep = ctx.enter_context(tc.tile_pool(name="keep", bufs=1))
-        stage = ctx.enter_context(tc.tile_pool(name="stage", bufs=2))
         psum = ctx.enter_context(tc.psum_pool(name="psum", bufs=1))
+
+        def sbuf(shape, dtype, name, slot=None):
+            return keep.tile(shape, dtype, name=name, tag=slot or name, align_bytes=64)
 
         src_list = keep.tile([P, J // GROUP], U16, name="src_list")
         dst_list = keep.tile([P, J // GROUP], U16, name="dst_list")
@@ -47,58 +47,59 @@ def tile_list_msg_silu_gate_kernel(
         nc.sync.dma_start(dst_list[:], offs2)
         lists = (src_list, dst_list)
 
-        sm_cols = keep.tile([P, PACK], F32, name="sm_cols")
-        nc.sync.dma_start(out=sm_cols[:], in_=sm.rearrange("(p t) -> p t", t=PACK))
+        warm = sbuf([P, 2], F32, "warm")
+        nc.gpsimd.memset(warm[:, 0:1], 0.0)
+        nc.scalar.activation(warm[:, 1:2], warm[:, 0:1], ACT.Silu)
 
-        tab_plane = keep.tile([P, T // 4], I32, name="tab_plane", align_bytes=64)
-        wd_plane = keep.tile([P, N // 4], I32, name="wd_plane", align_bytes=64)
-        nc.gpsimd.memset(tab_plane[:], 0)
-        nc.gpsimd.memset(wd_plane[:], 0)
+        tab_plane = sbuf([P, T // 4], I32, "tab_plane")
+        wd_plane = sbuf([P, N // 4], I32, "wd_plane")
+        nc.vector.memset(tab_plane[:], 0)
+        nc.vector.memset(wd_plane[:], 0)
         load_scale_rows(nc, tab_plane, tab_scales[0])
 
-        ws_raw = keep.tile([P, PACK, R], F32, name="ws_raw", align_bytes=64)
-        tab = keep.tile([P, T], I32, name="tab", align_bytes=64)
+        ws_raw = sbuf([P, PACK, R], F32, "ws_raw")
+        tab = sbuf([P, T], I32, "tab")
         nc.sync.dma_start(out=ws_raw[:], in_=ws.rearrange("(p i) r -> p i r", i=PACK))
         nc.sync.dma_start(out=tab[:], in_=tab_words[0].rearrange("p t i -> p (t i)").bitcast(I32))
-        wt_raw = [keep.tile([P, PACK, R // 2], F32, name=f"wt_raw{u}", align_bytes=64) for u in range(2)]
+        wt_raw = [sbuf([P, PACK, R // 2], F32, f"wt_raw{u}") for u in range(2)]
         for u in range(2):
             cols = slice(u * R // 2, (u + 1) * R // 2)
             nc.sync.dma_start(out=wt_raw[u][:], in_=wt[:, cols].rearrange("(p i) r -> p i r", i=PACK))
-        wd_codes = keep.tile([P, N], I32, name="wd_codes", align_bytes=64)
+        edge_w = sbuf([P, J], F32, "edge_w")
+        nc.sync.dma_start(out=edge_w[:], in_=wgo)
+        gates = [sbuf([P, T], F32, f"gates{n}") for n in range(N_TILES)]
+        for n in range(2):
+            nc.sync.dma_start(out=gates[n][:], in_=gT[n * P : (n + 1) * P, :])
+        sm_cols = sbuf([P, PACK], F32, "sm_cols")
+        nc.sync.dma_start(out=sm_cols[:], in_=sm.rearrange("(p t) -> p t", t=PACK))
+        nc.sync.dma_start(out=gates[2][:], in_=gT[2 * P : 3 * P, :])
+        wd_codes = sbuf([P, N], I32, "wd_codes")
         nc.sync.dma_start(out=wd_codes[:], in_=wd_words[0].rearrange("p n i -> p (n i)").bitcast(I32))
         load_scale_rows(nc, wd_plane, wd_scales[0])
-        edge_w = keep.tile([P, J], F32, name="edge_w")
-        nc.sync.dma_start(out=edge_w[:], in_=wgo)
-        gates = [keep.tile([P, T], F32, name=f"gates{n}", align_bytes=64) for n in range(N_TILES)]
-        for n in range(2):
-            nc.sync.dma_start(out=gates[n][:], in_=gT[n * P : (n + 1) * P, :])
-        for n in range(2, N_TILES):
-            nc.sync.dma_start(out=gates[n][:], in_=gT[n * P : (n + 1) * P, :])
+        nc.sync.dma_start(out=gates[3][:], in_=gT[3 * P : 4 * P, :])
 
-        outs = [keep.tile([P, T], F32, name=f"out{n}", align_bytes=64) for n in range(2)]
+        outs = {}
         for n in range(2):
+            outs[n] = sbuf([P, T], F32, f"out{n}")
             nc.vector.memset(outs[n][:].bitcast(I32), 0)
 
-        v_codes = {}
-        v_scales = [keep.tile([P, J], U8, name=f"v_scales{i}", align_bytes=64) for i in range(2)]
+        v_scales = sbuf([P, 2, J], U8, "v_scales")
         for i in range(2):
-            nc.vector.tensor_copy(v_scales[i][:], tab_plane[:].bitcast(U8).indirect(lists[i][:]))
+            nc.vector.tensor_copy(v_scales[:, i, :], tab_plane[:].bitcast(U8).indirect(lists[i][:]))
+        v_codes = {}
 
-        def gather_words(half, slot):
-            v_codes[half] = keep.tile([P, 2, HALF], U32, name=f"v_codes{half}", tag=slot, align_bytes=64)
-            for i in range(2):
-                nc.vector.tensor_copy(
-                    v_codes[half][:, i, :],
-                    tab[:].bitcast(U32).indirect(
-                        lists[i][:, half * HALF // GROUP : (half + 1) * HALF // GROUP]
-                    ),
-                )
+        def gather_words(i, half, slot=None):
+            v_codes[i, half] = sbuf([P, HALF], U32, f"v_codes{i}_{half}", slot)
+            entries = lists[i][:, half * HALF // GROUP : (half + 1) * HALF // GROUP]
+            nc.vector.tensor_copy(v_codes[i, half][:], tab[:].bitcast(U32).indirect(entries))
 
-        gather_words(0, "v_codes0")
+        gather_words(0, 0)
+        gather_words(1, 0)
+        gather_words(0, 1)
 
-        w_bf = keep.tile([P, 2, PACK * R], BF16, name="w_bf", align_bytes=64)
-        w_codes = keep.tile([P, 2, R], U32, name="w_codes", align_bytes=64)
-        w_scales = keep.tile([P, 2, R], U8, name="w_scales", align_bytes=64)
+        w_bf = sbuf([P, 2, PACK * R], BF16, "w_bf")
+        w_codes = sbuf([P, 2, R], U32, "w_codes")
+        w_scales = sbuf([P, 2, R], U8, "w_scales")
         w_view = w_bf[:].rearrange("p w (t m i) -> p w m t i", t=PACK, i=PACK)
         nc.scalar.copy(out=w_view[:, 0], in_=ws_raw[:].rearrange("p i (m t) -> p m t i", t=PACK))
         for u in range(2):
@@ -106,112 +107,117 @@ def tile_list_msg_silu_gate_kernel(
                 out=w_view[:, 1, u * P // 2 : (u + 1) * P // 2],
                 in_=wt_raw[u][:].rearrange("p i (m t) -> p m t i", t=PACK),
             )
-        for i in range(2):
-            nc.vector.quantize_mx(
-                out=w_codes[:, i, :].bitcast(FP8X4), scales=w_scales[:, i, :], in_=w_bf[:, i, :]
-            )
+        nc.vector.quantize_mx(
+            out=w_codes[:].rearrange("p w r -> p (w r)").bitcast(FP8X4),
+            scales=w_scales[:].rearrange("p w r -> p (w r)"),
+            in_=w_bf[:].rearrange("p w c -> p (w c)"),
+        )
 
-        gather_words(1, "wt_raw1")
+        gather_words(1, 1, "wt_raw1")
 
-        msgs = {}
         gated = {}
 
-        def gather_gates(n, slot):
-            gated[n] = keep.tile([P, J], F32, name=f"gated{n}", tag=slot, align_bytes=64)
+        def gather_gates(n, slot=None):
+            gated[n] = sbuf([P, J], F32, f"gated{n}", slot)
             nc.vector.tensor_tensor(gated[n][:], gates[n][:].indirect(src_list[:]), edge_w[:], MULT)
 
-        def hidden(c):
-            cols = slice(c * CHUNK, (c + 1) * CHUNK)
-            act = stage.tile([P, PACK, CHUNK], F32, name="act")
-            for b in range(2):
-                acc = psum.tile([P, 2, CHUNK], F32, name=f"acc{c}_{b}", tag=f"bank{HIDDEN_BANKS[c][b]}")
-                for u in range(2):
-                    rows = slice((2 * b + u) * P, (2 * b + u + 1) * P)
+        def zero_out(n, slot):
+            outs[n] = sbuf([P, T], F32, f"out{n}", slot)
+            nc.gpsimd.memset(outs[n][:], 0.0)
+
+        def activate(lo, hi, banks, slot):
+            width = hi - lo
+            per_bank = PACK // len(banks)
+            act = sbuf([P, PACK, width], F32, f"act{lo}", slot)
+            for b, bank in enumerate(banks):
+                acc = psum.tile([P, per_bank, width], F32, name=f"acc{lo}_{b}", tag=f"bank{bank}")
+                for u in range(per_bank):
+                    rows = slice((per_bank * b + u) * P, (per_bank * b + u + 1) * P)
                     for i in range(2):
                         nc.tensor.matmul_mx(
                             out=acc[:, u, :],
                             lhsT=w_codes[:, i, rows].bitcast(FP8X4),
                             lhsT_scale=w_scales[:, i, rows],
-                            rhs=v_codes[c // 2][:, i, c % 2 * CHUNK : (c % 2 + 1) * CHUNK].bitcast(FP8X4),
-                            rhs_scale=v_scales[i][:, cols],
+                            rhs=v_codes[i, lo // HALF][:, lo % HALF : lo % HALF + width].bitcast(FP8X4),
+                            rhs_scale=v_scales[:, i, lo:hi],
                             start=(i == 0),
                             stop=(i == 1),
                         )
-                nc.scalar.activation(act[:, 2 * b : 2 * b + 2, :], acc[:], ACT.Silu)
-            h_rows = keep.tile([P, PACK, CHUNK], BF16, name=f"h_rows{c}", align_bytes=64)
+                nc.scalar.activation(act[:, per_bank * b : per_bank * (b + 1), :], acc[:], ACT.Silu)
+            return act
+
+        def interleave(act, lo, hi):
+            width = hi - lo
+            h_rows = sbuf([P, PACK, width], BF16, f"h_rows{lo}")
             for t in range(PACK):
-                nc.scalar.activation(
-                    h_rows[:, t, :], act[:, t, :], ACT.Copy, scale=sm_cols[:, t : t + 1]
-                )
-            h_bf = keep.tile([P, CHUNK, PACK], BF16, name=f"h_bf{c}", align_bytes=64)
+                nc.scalar.activation(h_rows[:, t, :], act[:, t, :], ACT.Copy, scale=sm_cols[:, t : t + 1])
+            h_bf = sbuf([P, width, PACK], BF16, f"h_bf{lo}")
             nc.scalar.copy(
                 out=h_bf[:].rearrange("p (c i) t -> p c t i", i=4),
                 in_=h_rows[:].rearrange("p t (c i) -> p c t i", i=4),
             )
             return h_bf
 
-        def message(c, h_bf, tag):
-            h_codes = keep.tile([P, CHUNK], U32, name=f"h_codes{c}", tag=tag, align_bytes=64)
-            h_scales = keep.tile([P, CHUNK], U8, name=f"h_scales{c}", align_bytes=64)
+        def quantise(h_bf, lo, hi):
+            h_codes = sbuf([P, hi - lo], U32, f"h_codes{lo}")
+            h_scales = sbuf([P, hi - lo], U8, f"h_scales{lo}")
             nc.vector.quantize_mx(
-                out=h_codes[:].bitcast(FP8X4),
-                scales=h_scales[:],
-                in_=h_bf[:].rearrange("p c t -> p (c t)"),
+                out=h_codes[:].bitcast(FP8X4), scales=h_scales[:], in_=h_bf[:].rearrange("p c t -> p (c t)")
             )
-            slot = f"h_rows{c + 1}" if c in (1, 2) else f"msgs_low{c}"
-            msgs[c, 0] = keep.tile([P, 2, CHUNK], F32, name=f"msgs_low{c}", tag=slot, align_bytes=64)[:]
-            if c < 3:
-                width = CHUNK if c < 2 else HALF
-                msgs[c, 1] = keep.tile([P, 2, width], F32, name=f"msgs_high{c}", align_bytes=64)[:]
-            else:
-                msgs[c, 1] = msgs[2, 1][:, :, CHUNK:]
-            for b in range(2):
-                acc = psum.tile([P, 2, CHUNK], F32, name=f"y_acc{c}_{b}", tag=f"bank{MESSAGE_BANKS[c][b]}")
-                for u in range(2):
-                    rows = slice((2 * b + u) * P, (2 * b + u + 1) * P)
-                    nc.tensor.matmul_mx(
-                        out=acc[:, u, :],
-                        lhsT=wd_codes[:, rows].bitcast(FP8X4),
-                        lhsT_scale=wd_plane[:].bitcast(U8)[:, rows],
-                        rhs=h_codes[:].bitcast(FP8X4),
-                        rhs_scale=h_scales[:],
-                        start=True,
-                        stop=True,
-                    )
-                nc.scalar.copy(out=msgs[c, b][:, :, 0:CHUNK], in_=acc[:])
+            return h_codes, h_scales
 
-        def scatter(n, lo, hi):
+        def message(h, first_tile, dest, bank):
+            h_codes, h_scales = h
+            count, width = dest.shape[1], dest.shape[2]
+            acc = psum.tile([P, count, width], F32, name=f"y_acc{first_tile}_{bank}", tag=f"bank{bank}")
+            for u in range(count):
+                rows = slice((first_tile + u) * P, (first_tile + u + 1) * P)
+                nc.tensor.matmul_mx(
+                    out=acc[:, u, :],
+                    lhsT=wd_codes[:, rows].bitcast(FP8X4),
+                    lhsT_scale=wd_plane[:].bitcast(U8)[:, rows],
+                    rhs=h_codes[:].bitcast(FP8X4),
+                    rhs_scale=h_scales[:],
+                    start=True,
+                    stop=True,
+                )
+            nc.scalar.copy(out=dest, in_=acc[:])
+
+        def scatter(n, lo, hi, msgs):
             nc.vector.tensor_tensor(
-                outs[n][:].indirect(dst_list[:, lo // GROUP : hi // GROUP]),
-                msgs[lo // CHUNK, n // 2][:, n % 2, 0 : hi - lo],
-                gated[n][:, lo:hi],
-                MULT,
+                outs[n][:].indirect(dst_list[:, lo // GROUP : hi // GROUP]), msgs, gated[n][:, lo:hi], MULT
             )
             if hi == J:
                 nc.sync.dma_start(out=out[n * P : (n + 1) * P, :], in_=outs[n][:])
 
-        c1, c2, c3 = CHUNK, 2 * CHUNK, 3 * CHUNK
-        gather_gates(0, "gated0")
-        gather_gates(1, "gated1")
-        message(0, hidden(0), "gates1")
-        gather_gates(2, "h_bf0")
-        for n, slot in ((2, "gates1"), (3, "h_scales0")):
-            outs.append(keep.tile([P, T], F32, name=f"out{n}", tag=slot, align_bytes=64))
-            nc.gpsimd.memset(outs[n][:], 0.0)
-        h1 = hidden(1)
-        h2 = hidden(2)
-        for n in range(3):
-            scatter(n, 0, c1)
-        message(1, h1, "msgs_low0")
-        gather_gates(3, "h_bf1")
-        h3 = hidden(3)
-        scatter(3, 0, c1)
-        message(2, h2, "msgs_high0")
-        for n in range(N_TILES):
-            scatter(n, c1, c2)
-        message(3, h3, "h_rows2")
-        for lo, hi in ((c2, c3), (c3, J)):
-            for n in range(2):
-                scatter(n, lo, hi)
+        q1, q2 = QUARTER, 2 * QUARTER
+        gather_gates(0)
+        zero_out(2, "tab")
+        gather_gates(1)
+        h_first = quantise(interleave(activate(0, q1, (0, 1, 2, 3), "act"), 0, q1), 0, q1)
+        gather_gates(2, "h_rows0")
+        h_second = quantise(interleave(activate(q1, q2, (4, 5), "act"), q1, q2), q1, q2)
+        zero_out(3, f"h_bf{q1}")
+        first = [sbuf([P, 1, q1], F32, f"first{n}") for n in range(2)]
+        first_high = sbuf([P, 2, q1], F32, "first_high")
+        message(h_first, 0, first[0][:], 2)
+        message(h_first, 1, first[1][:], 3)
+        message(h_first, 2, first_high[:], 4)
+        h_bf_rest = interleave(activate(q2, J, (6, 7, 0, 1), "h_codes0"), q2, J)
+        for n in range(2):
+            scatter(n, 0, q1, first[n][:, 0, :])
+        gather_gates(3, "first0")
         for n in range(2, N_TILES):
-            scatter(n, c2, J)
+            scatter(n, 0, q1, first_high[:, n - 2, :])
+        h_rest = quantise(h_bf_rest, q2, J)
+        later = sbuf([P, N_TILES, J - q1], F32, "later", f"h_rows{q2}")
+        for b, bank in enumerate((5, 2)):
+            message(h_second, 2 * b, later[:, 2 * b : 2 * b + 2, 0:q1], bank)
+        for n in range(2):
+            scatter(n, q1, q2, later[:, n, 0:q1])
+        for n in (2, 3, 0, 1):
+            message(h_rest, n, later[:, n : n + 1, q1:], (6 + n) % 8)
+        for n in range(2, N_TILES):
+            scatter(n, q1, J, later[:, n, :])
+        for n in range(2):
+            scatter(n, q2, J, later[:, n, q1:])

@@ -18,7 +18,6 @@ ACT = mybir.ActivationFunctionType
 P = 128
 PACK = 4
 GROUP = 16
-HALF = J // 2
 QUARTER = J // 4
 N_TILES = N // P
 
@@ -65,18 +64,20 @@ def tile_list_msg_silu_gate_kernel(
         for u in range(2):
             cols = slice(u * R // 2, (u + 1) * R // 2)
             nc.sync.dma_start(out=wt_raw[u][:], in_=wt[:, cols].rearrange("(p i) r -> p i r", i=PACK))
+        sm_cols = sbuf([P, PACK], F32, "sm_cols")
+        nc.sync.dma_start(out=sm_cols[:], in_=sm.rearrange("(p t) -> p t", t=PACK))
         edge_w = sbuf([P, J], F32, "edge_w")
         nc.sync.dma_start(out=edge_w[:], in_=wgo)
         gates = [sbuf([P, T], F32, f"gates{n}") for n in range(N_TILES)]
         for n in range(2):
             nc.sync.dma_start(out=gates[n][:], in_=gT[n * P : (n + 1) * P, :])
-        sm_cols = sbuf([P, PACK], F32, "sm_cols")
-        nc.sync.dma_start(out=sm_cols[:], in_=sm.rearrange("(p t) -> p t", t=PACK))
+        load_scale_rows(nc, wd_plane, wd_scales[0])
         nc.sync.dma_start(out=gates[2][:], in_=gT[2 * P : 3 * P, :])
         wd_codes = sbuf([P, N], I32, "wd_codes")
-        nc.sync.dma_start(out=wd_codes[:], in_=wd_words[0].rearrange("p n i -> p (n i)").bitcast(I32))
-        load_scale_rows(nc, wd_plane, wd_scales[0])
+        wd_packed = wd_words[0].rearrange("p n i -> p (n i)").bitcast(I32)
+        nc.sync.dma_start(out=wd_codes[:, 0 : N // 2], in_=wd_packed[:, 0 : N // 2])
         nc.sync.dma_start(out=gates[3][:], in_=gT[3 * P : 4 * P, :])
+        nc.sync.dma_start(out=wd_codes[:, N // 2 :], in_=wd_packed[:, N // 2 :])
 
         outs = {}
         for n in range(2):
@@ -86,34 +87,21 @@ def tile_list_msg_silu_gate_kernel(
         v_scales = sbuf([P, 2, J], U8, "v_scales")
         for i in range(2):
             nc.vector.tensor_copy(v_scales[:, i, :], tab_plane[:].bitcast(U8).indirect(lists[i][:]))
-        v_codes = {}
-
-        def gather_words(i, half, slot=None):
-            v_codes[i, half] = sbuf([P, HALF], U32, f"v_codes{i}_{half}", slot)
-            entries = lists[i][:, half * HALF // GROUP : (half + 1) * HALF // GROUP]
-            nc.vector.tensor_copy(v_codes[i, half][:], tab[:].bitcast(U32).indirect(entries))
-
-        gather_words(0, 0)
-        gather_words(1, 0)
-        gather_words(0, 1)
-
-        w_bf = sbuf([P, 2, PACK * R], BF16, "w_bf")
+        v_codes = sbuf([P, 2, J], U32, "v_codes")
+        w_bf = [sbuf([P, PACK * R], BF16, f"w_bf{i}") for i in range(2)]
         w_codes = sbuf([P, 2, R], U32, "w_codes")
         w_scales = sbuf([P, 2, R], U8, "w_scales")
-        w_view = w_bf[:].rearrange("p w (t m i) -> p w m t i", t=PACK, i=PACK)
-        nc.scalar.copy(out=w_view[:, 0], in_=ws_raw[:].rearrange("p i (m t) -> p m t i", t=PACK))
+        w_view = [w_bf[i][:].rearrange("p (t m i) -> p m t i", t=PACK, i=PACK) for i in range(2)]
+        nc.scalar.copy(out=w_view[0], in_=ws_raw[:].rearrange("p i (m t) -> p m t i", t=PACK))
         for u in range(2):
             nc.scalar.copy(
-                out=w_view[:, 1, u * P // 2 : (u + 1) * P // 2],
+                out=w_view[1][:, u * P // 2 : (u + 1) * P // 2],
                 in_=wt_raw[u][:].rearrange("p i (m t) -> p m t i", t=PACK),
             )
-        nc.vector.quantize_mx(
-            out=w_codes[:].rearrange("p w r -> p (w r)").bitcast(FP8X4),
-            scales=w_scales[:].rearrange("p w r -> p (w r)"),
-            in_=w_bf[:].rearrange("p w c -> p (w c)"),
-        )
-
-        gather_words(1, 1, "wt_raw1")
+        nc.vector.tensor_copy(v_codes[:, 0, :], tab[:].bitcast(U32).indirect(lists[0][:]))
+        nc.vector.quantize_mx(out=w_codes[:, 0, :].bitcast(FP8X4), scales=w_scales[:, 0, :], in_=w_bf[0][:])
+        nc.vector.tensor_copy(v_codes[:, 1, :], tab[:].bitcast(U32).indirect(lists[1][:]))
+        nc.vector.quantize_mx(out=w_codes[:, 1, :].bitcast(FP8X4), scales=w_scales[:, 1, :], in_=w_bf[1][:])
 
         gated = {}
 
@@ -125,6 +113,18 @@ def tile_list_msg_silu_gate_kernel(
             outs[n] = sbuf([P, T], F32, f"out{n}", slot)
             nc.gpsimd.memset(outs[n][:], 0.0)
 
+        def project(i, t, lo, hi, acc):
+            rows = slice(t * P, (t + 1) * P)
+            nc.tensor.matmul_mx(
+                out=acc,
+                lhsT=w_codes[:, i, rows].bitcast(FP8X4),
+                lhsT_scale=w_scales[:, i, rows],
+                rhs=v_codes[:, i, lo:hi].bitcast(FP8X4),
+                rhs_scale=v_scales[:, i, lo:hi],
+                start=(i == 0),
+                stop=(i == 1),
+            )
+
         def activate(lo, hi, banks, slot):
             width = hi - lo
             per_bank = PACK // len(banks)
@@ -132,18 +132,19 @@ def tile_list_msg_silu_gate_kernel(
             for b, bank in enumerate(banks):
                 acc = psum.tile([P, per_bank, width], F32, name=f"acc{lo}_{b}", tag=f"bank{bank}")
                 for u in range(per_bank):
-                    rows = slice((per_bank * b + u) * P, (per_bank * b + u + 1) * P)
                     for i in range(2):
-                        nc.tensor.matmul_mx(
-                            out=acc[:, u, :],
-                            lhsT=w_codes[:, i, rows].bitcast(FP8X4),
-                            lhsT_scale=w_scales[:, i, rows],
-                            rhs=v_codes[i, lo // HALF][:, lo % HALF : lo % HALF + width].bitcast(FP8X4),
-                            rhs_scale=v_scales[:, i, lo:hi],
-                            start=(i == 0),
-                            stop=(i == 1),
-                        )
+                        project(i, per_bank * b + u, lo, hi, acc[:, u, :])
                 nc.scalar.activation(act[:, per_bank * b : per_bank * (b + 1), :], acc[:], ACT.Silu)
+            return act
+
+        def activate_first(hi):
+            act = sbuf([P, PACK, hi], F32, "act0", "act")
+            accs = [psum.tile([P, hi], F32, name=f"acc0_{t}", tag=f"bank{t}") for t in range(PACK)]
+            for t in range(PACK):
+                project(0, t, 0, hi, accs[t][:])
+            for t in range(PACK):
+                project(1, t, 0, hi, accs[t][:])
+                nc.scalar.activation(act[:, t, :], accs[t][:], ACT.Silu)
             return act
 
         def interleave(act, lo, hi):
@@ -158,11 +159,10 @@ def tile_list_msg_silu_gate_kernel(
             )
             return h_bf
 
-        def quantise(h_bf, lo, hi):
+        def quantise(h_bf, lo, hi, h_scales):
             h_codes = sbuf([P, hi - lo], U32, f"h_codes{lo}")
-            h_scales = sbuf([P, hi - lo], U8, f"h_scales{lo}")
             nc.vector.quantize_mx(
-                out=h_codes[:].bitcast(FP8X4), scales=h_scales[:], in_=h_bf[:].rearrange("p c t -> p (c t)")
+                out=h_codes[:].bitcast(FP8X4), scales=h_scales, in_=h_bf[:].rearrange("p c t -> p (c t)")
             )
             return h_codes, h_scales
 
@@ -177,7 +177,7 @@ def tile_list_msg_silu_gate_kernel(
                     lhsT=wd_codes[:, rows].bitcast(FP8X4),
                     lhsT_scale=wd_plane[:].bitcast(U8)[:, rows],
                     rhs=h_codes[:].bitcast(FP8X4),
-                    rhs_scale=h_scales[:],
+                    rhs_scale=h_scales,
                     start=True,
                     stop=True,
                 )
@@ -191,17 +191,19 @@ def tile_list_msg_silu_gate_kernel(
                 nc.sync.dma_start(out=out[n * P : (n + 1) * P, :], in_=outs[n][:])
 
         q1, q2 = QUARTER, 2 * QUARTER
+        rest_scales = sbuf([P, J - q2], U8, "rest_scales")
         gather_gates(0)
-        zero_out(2, "tab")
+        zero_out(2, "w_bf1")
         gather_gates(1)
-        h_first = quantise(interleave(activate(0, q1, (0, 1, 2, 3), "act"), 0, q1), 0, q1)
+        h_first = quantise(interleave(activate_first(q1), 0, q1), 0, q1, wd_plane[:].bitcast(U8)[4:P, 0:q1])
         gather_gates(2, "h_rows0")
-        h_second = quantise(interleave(activate(q1, q2, (4, 5), "act"), q1, q2), q1, q2)
-        zero_out(3, f"h_bf{q1}")
+        h_bf_second = interleave(activate(q1, q2, (4, 5), "act"), q1, q2)
         first = [sbuf([P, 1, q1], F32, f"first{n}") for n in range(2)]
         first_high = sbuf([P, 2, q1], F32, "first_high")
         message(h_first, 0, first[0][:], 2)
         message(h_first, 1, first[1][:], 3)
+        h_second = quantise(h_bf_second, q1, q2, wd_plane[:].bitcast(U8)[8:P, 0:q1])
+        zero_out(3, f"h_bf{q1}")
         message(h_first, 2, first_high[:], 4)
         h_bf_rest = interleave(activate(q2, J, (6, 7, 0, 1), "h_codes0"), q2, J)
         for n in range(2):
@@ -209,7 +211,7 @@ def tile_list_msg_silu_gate_kernel(
         gather_gates(3, "first0")
         for n in range(2, N_TILES):
             scatter(n, 0, q1, first_high[:, n - 2, :])
-        h_rest = quantise(h_bf_rest, q2, J)
+        h_rest = quantise(h_bf_rest, q2, J, rest_scales[:])
         later = sbuf([P, N_TILES, J - q1], F32, "later", f"h_rows{q2}")
         for b, bank in enumerate((5, 2)):
             message(h_second, 2 * b, later[:, 2 * b : 2 * b + 2, 0:q1], bank)

@@ -74,10 +74,8 @@ def tile_list_msg_silu_gate_kernel(
         load_scale_rows(nc, wd_plane, wd_scales[0])
         nc.sync.dma_start(out=gates[2][:], in_=gT[2 * P : 3 * P, :])
         wd_codes = sbuf([P, N], I32, "wd_codes")
-        wd_packed = wd_words[0].rearrange("p n i -> p (n i)").bitcast(I32)
-        nc.sync.dma_start(out=wd_codes[:, 0 : N // 2], in_=wd_packed[:, 0 : N // 2])
+        nc.sync.dma_start(out=wd_codes[:], in_=wd_words[0].rearrange("p n i -> p (n i)").bitcast(I32))
         nc.sync.dma_start(out=gates[3][:], in_=gT[3 * P : 4 * P, :])
-        nc.sync.dma_start(out=wd_codes[:, N // 2 :], in_=wd_packed[:, N // 2 :])
 
         outs = {}
         for n in range(2):
@@ -202,24 +200,29 @@ def tile_list_msg_silu_gate_kernel(
         first_high = sbuf([P, 2, q1], F32, "first_high")
         message(h_first, 0, first[0][:], 2)
         message(h_first, 1, first[1][:], 3)
+        message(h_first, 2, first_high[:], 4)
         h_second = quantise(h_bf_second, q1, q2, wd_plane[:].bitcast(U8)[8:P, 0:q1])
         zero_out(3, f"h_bf{q1}")
-        message(h_first, 2, first_high[:], 4)
+        second_low = sbuf([P, 2, q1], F32, "second_low")
+        message(h_second, 0, second_low[:], 5)
         h_bf_rest = interleave(activate(q2, J, (6, 7, 0, 1), "h_codes0"), q2, J)
         for n in range(2):
             scatter(n, 0, q1, first[n][:, 0, :])
         gather_gates(3, "first0")
         for n in range(2, N_TILES):
             scatter(n, 0, q1, first_high[:, n - 2, :])
+        for n in range(2):
+            scatter(n, q1, q2, second_low[:, n, :])
         h_rest = quantise(h_bf_rest, q2, J, rest_scales[:])
-        later = sbuf([P, N_TILES, J - q1], F32, "later", f"h_rows{q2}")
-        for b, bank in enumerate((5, 2)):
-            message(h_second, 2 * b, later[:, 2 * b : 2 * b + 2, 0:q1], bank)
+        later_high = sbuf([P, 2, J - q1], F32, "later_high", f"h_rows{q2}")
+        later_low = sbuf([P, 2, J - q2], F32, "later_low")
+        message(h_second, 2, later_high[:, :, 0:q1], 2)
+        scatter(2, q1, q2, later_high[:, 0, 0:q1])
+        for n in (3, 2):
+            message(h_rest, n, later_high[:, n - 2 : n - 1, q1:], n - 2)
         for n in range(2):
-            scatter(n, q1, q2, later[:, n, 0:q1])
-        for n in (2, 3, 0, 1):
-            message(h_rest, n, later[:, n : n + 1, q1:], (6 + n) % 8)
-        for n in range(2, N_TILES):
-            scatter(n, q1, J, later[:, n, :])
+            message(h_rest, n, later_low[:, n : n + 1, :], 6 + n)
+        scatter(3, q1, J, later_high[:, 1, :])
+        scatter(2, q2, J, later_high[:, 0, q1:])
         for n in range(2):
-            scatter(n, q2, J, later[:, n, q1:])
+            scatter(n, q2, J, later_low[:, n, :])

@@ -1,6 +1,7 @@
 from contextlib import ExitStack
 
 import concourse.mybir as mybir
+from concourse.masks import make_identity
 
 K, R, N, T, J = 512, 512, 512, 2048, 1024
 FLOPS = 2 * J * (2 * K * R + R * N)
@@ -18,6 +19,7 @@ ACT = mybir.ActivationFunctionType
 P = 128
 PACK = 4
 GROUP = 16
+HALF = J // 2
 QUARTER = J // 4
 N_TILES = N // P
 
@@ -50,24 +52,30 @@ def tile_list_msg_silu_gate_kernel(
         nc.gpsimd.memset(warm[:, 0:1], 0.0)
         nc.scalar.activation(warm[:, 1:2], warm[:, 0:1], ACT.Silu)
 
+        ws_raw = sbuf([P, PACK, R], F32, "ws_raw")
+        ws_rows = ws.rearrange("(p i) r -> p i r", i=PACK)
+        nc.sync.dma_start(out=ws_raw[:, 0:2, :], in_=ws_rows[:, 0:2, :])
+
         tab_plane = sbuf([P, T // 4], I32, "tab_plane")
         wd_plane = sbuf([P, N // 4], I32, "wd_plane")
+        identity = sbuf([P, P], F32, "identity")
         nc.vector.memset(tab_plane[:], 0)
         nc.vector.memset(wd_plane[:], 0)
+        nc.vector.memset(identity[:], 0.0)
+        make_identity(nc, identity[:], nomemset=True)
         load_scale_rows(nc, tab_plane, tab_scales[0])
 
-        ws_raw = sbuf([P, PACK, R], F32, "ws_raw")
+        nc.sync.dma_start(out=ws_raw[:, 2:4, :], in_=ws_rows[:, 2:4, :])
+        edge_cols = sbuf([P, J // P], F32, "edge_cols")
+        nc.sync.dma_start(out=edge_cols[:], in_=wgo[0].rearrange("(p c) -> p c", p=P))
+        sm_cols = sbuf([P, PACK], F32, "sm_cols")
+        nc.sync.dma_start(out=sm_cols[:], in_=sm.rearrange("(p t) -> p t", t=PACK))
         tab = sbuf([P, T], I32, "tab")
-        nc.sync.dma_start(out=ws_raw[:], in_=ws.rearrange("(p i) r -> p i r", i=PACK))
         nc.sync.dma_start(out=tab[:], in_=tab_words[0].rearrange("p t i -> p (t i)").bitcast(I32))
         wt_raw = [sbuf([P, PACK, R // 2], F32, f"wt_raw{u}") for u in range(2)]
         for u in range(2):
             cols = slice(u * R // 2, (u + 1) * R // 2)
             nc.sync.dma_start(out=wt_raw[u][:], in_=wt[:, cols].rearrange("(p i) r -> p i r", i=PACK))
-        sm_cols = sbuf([P, PACK], F32, "sm_cols")
-        nc.sync.dma_start(out=sm_cols[:], in_=sm.rearrange("(p t) -> p t", t=PACK))
-        edge_w = sbuf([P, J], F32, "edge_w")
-        nc.sync.dma_start(out=edge_w[:], in_=wgo)
         gates = [sbuf([P, T], F32, f"gates{n}") for n in range(N_TILES)]
         for n in range(2):
             nc.sync.dma_start(out=gates[n][:], in_=gT[n * P : (n + 1) * P, :])
@@ -85,21 +93,39 @@ def tile_list_msg_silu_gate_kernel(
         v_scales = sbuf([P, 2, J], U8, "v_scales")
         for i in range(2):
             nc.vector.tensor_copy(v_scales[:, i, :], tab_plane[:].bitcast(U8).indirect(lists[i][:]))
-        v_codes = sbuf([P, 2, J], U32, "v_codes")
+        v_codes = {}
+
+        def gather_words(i, half, slot=None):
+            v_codes[i, half] = sbuf([P, HALF], U32, f"v_codes{i}_{half}", slot)
+            entries = lists[i][:, half * HALF // GROUP : (half + 1) * HALF // GROUP]
+            nc.vector.tensor_copy(v_codes[i, half][:], tab[:].bitcast(U32).indirect(entries))
+
         w_bf = [sbuf([P, PACK * R], BF16, f"w_bf{i}") for i in range(2)]
         w_codes = sbuf([P, 2, R], U32, "w_codes")
         w_scales = sbuf([P, 2, R], U8, "w_scales")
         w_view = [w_bf[i][:].rearrange("p (t m i) -> p m t i", t=PACK, i=PACK) for i in range(2)]
         nc.scalar.copy(out=w_view[0], in_=ws_raw[:].rearrange("p i (m t) -> p m t i", t=PACK))
+
+        edge_w = sbuf([P, J], F32, "edge_w")
+        edge_view = edge_w[:].rearrange("p (m b c) -> p b m c", b=2, c=4)
+        for b in range(2):
+            spread = psum.tile([P, 4, P], F32, name=f"spread{b}", tag=f"bank{6 + b}")
+            for c in range(4):
+                column = edge_cols[:, 4 * b + c : 4 * b + c + 1].to_broadcast([P, P])
+                nc.tensor.transpose(spread[:, c, :], column, identity[:])
+            nc.scalar.copy(out=edge_view[:, b], in_=spread[:].rearrange("p c m -> p m c"))
+
         for u in range(2):
             nc.scalar.copy(
                 out=w_view[1][:, u * P // 2 : (u + 1) * P // 2],
                 in_=wt_raw[u][:].rearrange("p i (m t) -> p m t i", t=PACK),
             )
-        nc.vector.tensor_copy(v_codes[:, 0, :], tab[:].bitcast(U32).indirect(lists[0][:]))
+        gather_words(0, 0)
+        gather_words(1, 0)
         nc.vector.quantize_mx(out=w_codes[:, 0, :].bitcast(FP8X4), scales=w_scales[:, 0, :], in_=w_bf[0][:])
-        nc.vector.tensor_copy(v_codes[:, 1, :], tab[:].bitcast(U32).indirect(lists[1][:]))
+        gather_words(0, 1)
         nc.vector.quantize_mx(out=w_codes[:, 1, :].bitcast(FP8X4), scales=w_scales[:, 1, :], in_=w_bf[1][:])
+        gather_words(1, 1, "wt_raw1")
 
         gated = {}
 
@@ -117,7 +143,7 @@ def tile_list_msg_silu_gate_kernel(
                 out=acc,
                 lhsT=w_codes[:, i, rows].bitcast(FP8X4),
                 lhsT_scale=w_scales[:, i, rows],
-                rhs=v_codes[:, i, lo:hi].bitcast(FP8X4),
+                rhs=v_codes[i, lo // HALF][:, lo % HALF : lo % HALF + hi - lo].bitcast(FP8X4),
                 rhs_scale=v_scales[:, i, lo:hi],
                 start=(i == 0),
                 stop=(i == 1),
@@ -191,7 +217,7 @@ def tile_list_msg_silu_gate_kernel(
         q1, q2 = QUARTER, 2 * QUARTER
         rest_scales = sbuf([P, J - q2], U8, "rest_scales")
         gather_gates(0)
-        zero_out(2, "w_bf1")
+        zero_out(2, "tab")
         gather_gates(1)
         h_first = quantise(interleave(activate_first(q1), 0, q1), 0, q1, wd_plane[:].bitcast(U8)[4:P, 0:q1])
         gather_gates(2, "h_rows0")

@@ -52,10 +52,6 @@ def tile_list_msg_silu_gate_kernel(
         nc.gpsimd.memset(warm[:, 0:1], 0.0)
         nc.scalar.activation(warm[:, 1:2], warm[:, 0:1], ACT.Silu)
 
-        ws_raw = sbuf([P, PACK, R], F32, "ws_raw")
-        ws_rows = ws.rearrange("(p i) r -> p i r", i=PACK)
-        nc.sync.dma_start(out=ws_raw[:, 0:2, :], in_=ws_rows[:, 0:2, :])
-
         tab_plane = sbuf([P, T // 4], I32, "tab_plane")
         wd_plane = sbuf([P, N // 4], I32, "wd_plane")
         identity = sbuf([P, P], F32, "identity")
@@ -65,7 +61,8 @@ def tile_list_msg_silu_gate_kernel(
         make_identity(nc, identity[:], nomemset=True)
         load_scale_rows(nc, tab_plane, tab_scales[0])
 
-        nc.sync.dma_start(out=ws_raw[:, 2:4, :], in_=ws_rows[:, 2:4, :])
+        ws_raw = sbuf([P, PACK, R], F32, "ws_raw")
+        nc.sync.dma_start(out=ws_raw[:], in_=ws.rearrange("(p i) r -> p i r", i=PACK))
         edge_cols = sbuf([P, J // P], F32, "edge_cols")
         nc.sync.dma_start(out=edge_cols[:], in_=wgo[0].rearrange("(p c) -> p c", p=P))
         sm_cols = sbuf([P, PACK], F32, "sm_cols")
@@ -222,33 +219,33 @@ def tile_list_msg_silu_gate_kernel(
         h_first = quantise(interleave(activate_first(q1), 0, q1), 0, q1, wd_plane[:].bitcast(U8)[4:P, 0:q1])
         gather_gates(2, "h_rows0")
         h_bf_second = interleave(activate(q1, q2, (4, 5), "act"), q1, q2)
-        first = [sbuf([P, 1, q1], F32, f"first{n}") for n in range(2)]
-        first_high = sbuf([P, 2, q1], F32, "first_high")
+        first = [sbuf([P, 1, q1], F32, f"first{n}") for n in range(3)]
+        last_tile = sbuf([P, 1, J], F32, "last_tile")
         message(h_first, 0, first[0][:], 2)
         message(h_first, 1, first[1][:], 3)
-        message(h_first, 2, first_high[:], 4)
+        message(h_first, 2, first[2][:], 4)
+        message(h_first, 3, last_tile[:, :, 0:q1], 5)
         h_second = quantise(h_bf_second, q1, q2, wd_plane[:].bitcast(U8)[8:P, 0:q1])
-        zero_out(3, f"h_bf{q1}")
-        second_low = sbuf([P, 2, q1], F32, "second_low")
-        message(h_second, 0, second_low[:], 5)
+        second = [sbuf([P, 1, q1], F32, f"second{n}") for n in range(2)]
+        for n in range(2):
+            message(h_second, n, second[n][:], 2 + n)
         h_bf_rest = interleave(activate(q2, J, (6, 7, 0, 1), "h_codes0"), q2, J)
-        for n in range(2):
+        for n in range(3):
             scatter(n, 0, q1, first[n][:, 0, :])
-        gather_gates(3, "first0")
-        for n in range(2, N_TILES):
-            scatter(n, 0, q1, first_high[:, n - 2, :])
         for n in range(2):
-            scatter(n, q1, q2, second_low[:, n, :])
+            scatter(n, q1, q2, second[n][:, 0, :])
+        gather_gates(3, "second0")
         h_rest = quantise(h_bf_rest, q2, J, rest_scales[:])
-        later_high = sbuf([P, 2, J - q1], F32, "later_high", f"h_rows{q2}")
-        later_low = sbuf([P, 2, J - q2], F32, "later_low")
-        message(h_second, 2, later_high[:, :, 0:q1], 2)
-        scatter(2, q1, q2, later_high[:, 0, 0:q1])
-        for n in (3, 2):
-            message(h_rest, n, later_high[:, n - 2 : n - 1, q1:], n - 2)
+        second_filler = sbuf([P, 1, q1], F32, "second_filler", f"h_rows{q2}")
+        later = sbuf([P, 3, J - q2], F32, "later")
+        message(h_second, 2, second_filler[:], 5)
+        scatter(2, q1, q2, second_filler[:, 0, :])
+        for n in range(3):
+            message(h_rest, n, later[:, n : n + 1, :], (6 + n) % 8)
+        message(h_second, 3, last_tile[:, :, q1:q2], 4)
+        message(h_rest, 3, last_tile[:, :, q2:], 1)
         for n in range(2):
-            message(h_rest, n, later_low[:, n : n + 1, :], 6 + n)
-        scatter(3, q1, J, later_high[:, 1, :])
-        scatter(2, q2, J, later_high[:, 0, q1:])
-        for n in range(2):
-            scatter(n, q2, J, later_low[:, n, :])
+            scatter(n, q2, J, later[:, n, :])
+        scatter(2, q2, J, later[:, 2, :])
+        outs[3] = outs[0]
+        scatter(3, 0, J, last_tile[:, 0, :])

@@ -83,9 +83,8 @@ def tile_list_msg_silu_gate_kernel(
         nc.sync.dma_start(out=gates[3][:], in_=gT[3 * P : 4 * P, :])
 
         outs = {}
-        for n in range(2):
-            outs[n] = sbuf([P, T], F32, f"out{n}")
-            nc.vector.memset(outs[n][:].bitcast(I32), 0)
+        outs[0] = sbuf([P, T], F32, "out0")
+        nc.vector.memset(outs[0][:].bitcast(I32), 0)
 
         v_scales = sbuf([P, 2, J], U8, "v_scales")
         for i in range(2):
@@ -214,7 +213,7 @@ def tile_list_msg_silu_gate_kernel(
         q1, q2 = QUARTER, 2 * QUARTER
         rest_scales = sbuf([P, J - q2], U8, "rest_scales")
         gather_gates(0)
-        zero_out(2, "tab")
+        zero_out(1, "tab")
         gather_gates(1)
         h_first = quantise(interleave(activate_first(q1), 0, q1), 0, q1, wd_plane[:].bitcast(U8)[4:P, 0:q1])
         gather_gates(2, "h_rows0")
@@ -226,6 +225,7 @@ def tile_list_msg_silu_gate_kernel(
         message(h_first, 2, first[2][:], 4)
         message(h_first, 3, last_tile[:, :, 0:q1], 5)
         h_second = quantise(h_bf_second, q1, q2, wd_plane[:].bitcast(U8)[8:P, 0:q1])
+        zero_out(2, f"h_bf{q1}")
         second = [sbuf([P, 1, q1], F32, f"second{n}") for n in range(2)]
         for n in range(2):
             message(h_second, n, second[n][:], 2 + n)

@@ -48,10 +48,6 @@ def tile_list_msg_silu_gate_kernel(
         nc.sync.dma_start(dst_list[:], offs2)
         lists = (src_list, dst_list)
 
-        warm = sbuf([P, 2], F32, "warm")
-        nc.gpsimd.memset(warm[:, 0:1], 0.0)
-        nc.scalar.activation(warm[:, 1:2], warm[:, 0:1], ACT.Silu)
-
         tab_plane = sbuf([P, T // 4], I32, "tab_plane")
         wd_plane = sbuf([P, N // 4], I32, "wd_plane")
         identity = sbuf([P, P], F32, "identity")

@@ -22,6 +22,7 @@ GROUP = 16
 HALF = J // 2
 QUARTER = J // 4
 N_TILES = N // P
+ROW0 = P - K // 32
 
 
 def load_scale_rows(nc, plane, rows):
@@ -42,49 +43,57 @@ def tile_list_msg_silu_gate_kernel(
         def sbuf(shape, dtype, name, slot=None):
             return keep.tile(shape, dtype, name=name, tag=slot or name, align_bytes=64)
 
+        placed = ctx.enter_context(tc.tile_pool(name="placed", bufs=1))
+
         src_list = keep.tile([P, J // GROUP], U16, name="src_list")
         dst_list = keep.tile([P, J // GROUP], U16, name="dst_list")
+        tab_rows = placed.tile([P, T // 4], I32, name="tab_rows", offset=4 * T - T // 2)
+        nc.sync.dma_start(out=tab_rows[ROW0:P, :], in_=tab_scales[0].bitcast(I32))
         nc.sync.dma_start(src_list[:], offs)
         nc.sync.dma_start(dst_list[:], offs2)
         lists = (src_list, dst_list)
+        edge_cols = sbuf([P, J // P], F32, "edge_cols")
+        nc.scalar.dma_start(out=edge_cols[:], in_=wgo[0].rearrange("(p c) -> p c", p=P))
 
-        tab_plane = sbuf([P, T // 4], I32, "tab_plane")
-        wd_plane = sbuf([P, N // 4], I32, "wd_plane")
         identity = sbuf([P, P], F32, "identity")
-        nc.vector.memset(tab_plane[:], 0)
-        nc.vector.memset(wd_plane[:], 0)
+        v_plane = sbuf([P, 2 * J // 4], I32, "v_plane")
+        nc.vector.memset(tab_rows[0:ROW0, :], 0)
         nc.vector.memset(identity[:], 0.0)
+        nc.vector.memset(v_plane[:], 0)
         make_identity(nc, identity[:], nomemset=True)
-        load_scale_rows(nc, tab_plane, tab_scales[0])
 
         ws_raw = sbuf([P, PACK, R], F32, "ws_raw")
         nc.sync.dma_start(out=ws_raw[:], in_=ws.rearrange("(p i) r -> p i r", i=PACK))
-        edge_cols = sbuf([P, J // P], F32, "edge_cols")
-        nc.sync.dma_start(out=edge_cols[:], in_=wgo[0].rearrange("(p c) -> p c", p=P))
-        sm_cols = sbuf([P, PACK], F32, "sm_cols")
-        nc.sync.dma_start(out=sm_cols[:], in_=sm.rearrange("(p t) -> p t", t=PACK))
         tab = sbuf([P, T], I32, "tab")
         nc.sync.dma_start(out=tab[:], in_=tab_words[0].rearrange("p t i -> p (t i)").bitcast(I32))
         wt_raw = [sbuf([P, PACK, R // 2], F32, f"wt_raw{u}") for u in range(2)]
         for u in range(2):
             cols = slice(u * R // 2, (u + 1) * R // 2)
             nc.sync.dma_start(out=wt_raw[u][:], in_=wt[:, cols].rearrange("(p i) r -> p i r", i=PACK))
-        gates = [sbuf([P, T], F32, f"gates{n}") for n in range(N_TILES)]
-        for n in range(2):
-            nc.sync.dma_start(out=gates[n][:], in_=gT[n * P : (n + 1) * P, :])
-        load_scale_rows(nc, wd_plane, wd_scales[0])
-        nc.sync.dma_start(out=gates[2][:], in_=gT[2 * P : 3 * P, :])
-        wd_codes = sbuf([P, N], I32, "wd_codes")
-        nc.sync.dma_start(out=wd_codes[:], in_=wd_words[0].rearrange("p n i -> p (n i)").bitcast(I32))
-        nc.sync.dma_start(out=gates[3][:], in_=gT[3 * P : 4 * P, :])
+        sm_cols = sbuf([P, PACK], F32, "sm_cols")
+        nc.sync.dma_start(out=sm_cols[:], in_=sm.rearrange("(p t) -> p t", t=PACK))
 
         outs = {}
-        outs[0] = sbuf([P, T], F32, "out0")
-        nc.vector.memset(outs[0][:].bitcast(I32), 0)
 
-        v_scales = sbuf([P, 2, J], U8, "v_scales")
+        picked = sbuf([P, 2 * J], U8, "picked")
         for i in range(2):
-            nc.vector.tensor_copy(v_scales[:, i, :], tab_plane[:].bitcast(U8).indirect(lists[i][:]))
+            nc.vector.tensor_copy(picked[:, i * J : (i + 1) * J], tab_rows[:].bitcast(U8).indirect(lists[i][:]))
+        for q in range(4):
+            nc.sync.dma_start(
+                out=v_plane[32 * q : 32 * q + 4, :], in_=picked[ROW0 + 4 * q : ROW0 + 4 * q + 4, :].bitcast(I32)
+            )
+        v_scales = v_plane[:].bitcast(U8)
+        gates = {}
+
+        def load_gates(n, tile):
+            gates[n] = tile
+            nc.sync.dma_start(out=tile[:], in_=gT[n * P : (n + 1) * P, :])
+
+        for n in range(2):
+            load_gates(n, placed.tile([P, T], F32, name=f"gates{n}", offset=n * 4 * T))
+        wd_plane = sbuf([P, N // 4], I32, "wd_plane", "picked")
+        nc.gpsimd.memset(wd_plane[:], 0)
+        load_scale_rows(nc, wd_plane, wd_scales[0])
         v_codes = {}
 
         def gather_words(i, half, slot=None):
@@ -96,8 +105,6 @@ def tile_list_msg_silu_gate_kernel(
         w_codes = sbuf([P, 2, R], U32, "w_codes")
         w_scales = sbuf([P, 2, R], U8, "w_scales")
         w_view = [w_bf[i][:].rearrange("p (t m i) -> p m t i", t=PACK, i=PACK) for i in range(2)]
-        nc.scalar.copy(out=w_view[0], in_=ws_raw[:].rearrange("p i (m t) -> p m t i", t=PACK))
-
         edge_w = sbuf([P, J], F32, "edge_w")
         edge_view = edge_w[:].rearrange("p (m b c) -> p b m c", b=2, c=4)
         for b in range(2):
@@ -107,14 +114,20 @@ def tile_list_msg_silu_gate_kernel(
                 nc.tensor.transpose(spread[:, c, :], column, identity[:])
             nc.scalar.copy(out=edge_view[:, b], in_=spread[:].rearrange("p c m -> p m c"))
 
+        nc.scalar.copy(out=w_view[0], in_=ws_raw[:].rearrange("p i (m t) -> p m t i", t=PACK))
+        load_gates(2, sbuf([P, T], F32, "gates2", "ws_raw"))
+
         for u in range(2):
             nc.scalar.copy(
                 out=w_view[1][:, u * P // 2 : (u + 1) * P // 2],
                 in_=wt_raw[u][:].rearrange("p i (m t) -> p m t i", t=PACK),
             )
+        load_gates(3, sbuf([P, T], F32, "gates3", "wt_raw0"))
         gather_words(0, 0)
         gather_words(1, 0)
         nc.vector.quantize_mx(out=w_codes[:, 0, :].bitcast(FP8X4), scales=w_scales[:, 0, :], in_=w_bf[0][:])
+        wd_codes = sbuf([P, N], I32, "wd_codes", "w_bf0")
+        nc.sync.dma_start(out=wd_codes[:], in_=wd_words[0].rearrange("p n i -> p (n i)").bitcast(I32))
         gather_words(0, 1)
         nc.vector.quantize_mx(out=w_codes[:, 1, :].bitcast(FP8X4), scales=w_scales[:, 1, :], in_=w_bf[1][:])
         gather_words(1, 1, "wt_raw1")
@@ -136,7 +149,7 @@ def tile_list_msg_silu_gate_kernel(
                 lhsT=w_codes[:, i, rows].bitcast(FP8X4),
                 lhsT_scale=w_scales[:, i, rows],
                 rhs=v_codes[i, lo // HALF][:, lo % HALF : lo % HALF + hi - lo].bitcast(FP8X4),
-                rhs_scale=v_scales[:, i, lo:hi],
+                rhs_scale=v_scales[:, i * J + lo : i * J + hi],
                 start=(i == 0),
                 stop=(i == 1),
             )
@@ -208,8 +221,10 @@ def tile_list_msg_silu_gate_kernel(
 
         q1, q2 = QUARTER, 2 * QUARTER
         rest_scales = sbuf([P, J - q2], U8, "rest_scales")
+        zero_out(0, "tab")
         gather_gates(0)
-        zero_out(1, "tab")
+        outs[1] = placed.tile([P, T], F32, name="out1", offset=0)
+        nc.gpsimd.memset(outs[1][:], 0.0)
         gather_gates(1)
         h_first = quantise(interleave(activate_first(q1), 0, q1), 0, q1, wd_plane[:].bitcast(U8)[4:P, 0:q1])
         gather_gates(2, "h_rows0")

@@ -66,7 +66,10 @@ def tile_list_msg_silu_gate_kernel(
         nc.sync.dma_start(out=ws_raw[:], in_=ws.rearrange("(p i) r -> p i r", i=PACK))
         tab = sbuf([P, T], I32, "tab")
         nc.sync.dma_start(out=tab[:], in_=tab_words[0].rearrange("p t i -> p (t i)").bitcast(I32))
-        wt_raw = [sbuf([P, PACK, R // 2], F32, f"wt_raw{u}") for u in range(2)]
+        wt_raw = [
+            sbuf([P, PACK, R // 2], F32, "wt_raw0"),
+            placed.tile([P, PACK, R // 2], F32, name="wt_raw1", offset=8 * T),
+        ]
         for u in range(2):
             cols = slice(u * R // 2, (u + 1) * R // 2)
             nc.sync.dma_start(out=wt_raw[u][:], in_=wt[:, cols].rearrange("(p i) r -> p i r", i=PACK))
@@ -91,13 +94,12 @@ def tile_list_msg_silu_gate_kernel(
 
         for n in range(2):
             load_gates(n, placed.tile([P, T], F32, name=f"gates{n}", offset=n * 4 * T))
-        wd_plane = sbuf([P, N // 4], I32, "wd_plane", "picked")
-        nc.gpsimd.memset(wd_plane[:], 0)
-        load_scale_rows(nc, wd_plane, wd_scales[0])
         v_codes = {}
 
-        def gather_words(i, half, slot=None):
-            v_codes[i, half] = sbuf([P, HALF], U32, f"v_codes{i}_{half}", slot)
+        def gather_words(i, half, tile=None):
+            if tile is None:
+                tile = sbuf([P, HALF], U32, f"v_codes{i}_{half}")
+            v_codes[i, half] = tile
             entries = lists[i][:, half * HALF // GROUP : (half + 1) * HALF // GROUP]
             nc.vector.tensor_copy(v_codes[i, half][:], tab[:].bitcast(U32).indirect(entries))
 
@@ -122,15 +124,18 @@ def tile_list_msg_silu_gate_kernel(
                 out=w_view[1][:, u * P // 2 : (u + 1) * P // 2],
                 in_=wt_raw[u][:].rearrange("p i (m t) -> p m t i", t=PACK),
             )
-        load_gates(3, sbuf([P, T], F32, "gates3", "wt_raw0"))
+        load_gates(3, placed.tile([P, T], F32, name="gates3", offset=9 * T))
         gather_words(0, 0)
         gather_words(1, 0)
         nc.vector.quantize_mx(out=w_codes[:, 0, :].bitcast(FP8X4), scales=w_scales[:, 0, :], in_=w_bf[0][:])
-        wd_codes = sbuf([P, N], I32, "wd_codes", "w_bf0")
-        nc.sync.dma_start(out=wd_codes[:], in_=wd_words[0].rearrange("p n i -> p (n i)").bitcast(I32))
+        wd_plane = sbuf([P, N // 4], I32, "wd_plane", "w_bf0")
+        nc.gpsimd.memset(wd_plane[:], 0)
+        load_scale_rows(nc, wd_plane, wd_scales[0])
         gather_words(0, 1)
         nc.vector.quantize_mx(out=w_codes[:, 1, :].bitcast(FP8X4), scales=w_scales[:, 1, :], in_=w_bf[1][:])
-        gather_words(1, 1, "wt_raw1")
+        wd_codes = sbuf([P, N], I32, "wd_codes", "w_bf1")
+        nc.sync.dma_start(out=wd_codes[:], in_=wd_words[0].rearrange("p n i -> p (n i)").bitcast(I32))
+        gather_words(1, 1, placed.tile([P, HALF], U32, name="v_codes1_1", offset=8 * T, align_bytes=64))
 
         gated = {}
 
@@ -138,9 +143,9 @@ def tile_list_msg_silu_gate_kernel(
             gated[n] = sbuf([P, J], F32, f"gated{n}", slot)
             nc.vector.tensor_tensor(gated[n][:], gates[n][:].indirect(src_list[:]), edge_w[:], MULT)
 
-        def zero_out(n, slot):
-            outs[n] = sbuf([P, T], F32, f"out{n}", slot)
-            nc.gpsimd.memset(outs[n][:], 0.0)
+        def zero_out(n, tile):
+            outs[n] = tile
+            nc.gpsimd.memset(tile[:], 0.0)
 
         def project(i, t, lo, hi, acc):
             rows = slice(t * P, (t + 1) * P)
@@ -176,9 +181,9 @@ def tile_list_msg_silu_gate_kernel(
                 nc.scalar.activation(act[:, t, :], accs[t][:], ACT.Silu)
             return act
 
-        def interleave(act, lo, hi):
+        def interleave(act, lo, hi, slot=None):
             width = hi - lo
-            h_rows = sbuf([P, PACK, width], BF16, f"h_rows{lo}")
+            h_rows = sbuf([P, PACK, width], BF16, f"h_rows{lo}", slot)
             for t in range(PACK):
                 nc.scalar.activation(h_rows[:, t, :], act[:, t, :], ACT.Copy, scale=sm_cols[:, t : t + 1])
             h_bf = sbuf([P, width, PACK], BF16, f"h_bf{lo}")
@@ -221,42 +226,34 @@ def tile_list_msg_silu_gate_kernel(
 
         q1, q2 = QUARTER, 2 * QUARTER
         rest_scales = sbuf([P, J - q2], U8, "rest_scales")
-        zero_out(0, "tab")
-        gather_gates(0)
-        outs[1] = placed.tile([P, T], F32, name="out1", offset=0)
-        nc.gpsimd.memset(outs[1][:], 0.0)
-        gather_gates(1)
+        zero_out(0, sbuf([P, T], F32, "out0", "tab"))
+        for n in range(3):
+            gather_gates(n)
+            if n < 2:
+                zero_out(n + 1, placed.tile([P, T], F32, name=f"out{n + 1}", offset=n * 4 * T))
         h_first = quantise(interleave(activate_first(q1), 0, q1), 0, q1, wd_plane[:].bitcast(U8)[4:P, 0:q1])
-        gather_gates(2, "h_rows0")
+        gather_gates(3, "h_bf0")
         h_bf_second = interleave(activate(q1, q2, (4, 5), "act"), q1, q2)
-        first = [sbuf([P, 1, q1], F32, f"first{n}") for n in range(3)]
-        last_tile = sbuf([P, 1, J], F32, "last_tile")
-        message(h_first, 0, first[0][:], 2)
-        message(h_first, 1, first[1][:], 3)
-        message(h_first, 2, first[2][:], 4)
-        message(h_first, 3, last_tile[:, :, 0:q1], 5)
+        first = [sbuf([P, 1, q1], F32, f"first{n}") for n in range(N_TILES)]
+        for n in range(N_TILES):
+            message(h_first, n, first[n][:], 2 + n)
         h_second = quantise(h_bf_second, q1, q2, wd_plane[:].bitcast(U8)[8:P, 0:q1])
-        zero_out(2, f"h_bf{q1}")
+        zero_out(3, sbuf([P, T], F32, "out3", f"h_bf{q1}"))
         second = [sbuf([P, 1, q1], F32, f"second{n}") for n in range(2)]
         for n in range(2):
             message(h_second, n, second[n][:], 2 + n)
-        h_bf_rest = interleave(activate(q2, J, (6, 7, 0, 1), "h_codes0"), q2, J)
-        for n in range(3):
+        h_bf_rest = interleave(activate(q2, J, (6, 7, 0, 1), "act"), q2, J, "h_codes0")
+        for n in range(N_TILES):
             scatter(n, 0, q1, first[n][:, 0, :])
         for n in range(2):
             scatter(n, q1, q2, second[n][:, 0, :])
-        gather_gates(3, "second0")
         h_rest = quantise(h_bf_rest, q2, J, rest_scales[:])
-        second_filler = sbuf([P, 1, q1], F32, "second_filler", f"h_rows{q2}")
-        later = sbuf([P, 3, J - q2], F32, "later")
+        second_filler = sbuf([P, 2, q1], F32, "second_filler", "h_codes0")
+        later = sbuf([P, N_TILES, J - q2], F32, "later")
         message(h_second, 2, second_filler[:], 5)
-        scatter(2, q1, q2, second_filler[:, 0, :])
-        for n in range(3):
+        for n in range(2, N_TILES):
+            scatter(n, q1, q2, second_filler[:, n - 2, :])
+        for n in range(N_TILES):
             message(h_rest, n, later[:, n : n + 1, :], (6 + n) % 8)
-        message(h_second, 3, last_tile[:, :, q1:q2], 4)
-        message(h_rest, 3, last_tile[:, :, q2:], 1)
-        for n in range(2):
+        for n in range(N_TILES):
             scatter(n, q2, J, later[:, n, :])
-        scatter(2, q2, J, later[:, 2, :])
-        outs[3] = outs[0]
-        scatter(3, 0, J, last_tile[:, 0, :])

@@ -106,7 +106,7 @@ def tile_list_msg_silu_gate_kernel(
         w_bf = [sbuf([P, PACK * R], BF16, f"w_bf{i}") for i in range(2)]
         w_codes = sbuf([P, 2, R], U32, "w_codes")
         w_scales = sbuf([P, 2, R], U8, "w_scales")
-        w_view = [w_bf[i][:].rearrange("p (t m i) -> p m t i", t=PACK, i=PACK) for i in range(2)]
+        w_view = [w_bf[i][:].rearrange("p (t m i) -> p m i t", t=PACK, i=PACK) for i in range(2)]
         edge_w = sbuf([P, J], F32, "edge_w")
         edge_view = edge_w[:].rearrange("p (m b c) -> p b m c", b=2, c=4)
         for b in range(2):
@@ -116,13 +116,13 @@ def tile_list_msg_silu_gate_kernel(
                 nc.tensor.transpose(spread[:, c, :], column, identity[:])
             nc.scalar.copy(out=edge_view[:, b], in_=spread[:].rearrange("p c m -> p m c"))
 
-        nc.scalar.copy(out=w_view[0], in_=ws_raw[:].rearrange("p i (m t) -> p m t i", t=PACK))
+        nc.scalar.copy(out=w_view[0], in_=ws_raw[:].rearrange("p i (m t) -> p m i t", t=PACK))
         load_gates(2, sbuf([P, T], F32, "gates2", "ws_raw"))
 
         for u in range(2):
             nc.scalar.copy(
                 out=w_view[1][:, u * P // 2 : (u + 1) * P // 2],
-                in_=wt_raw[u][:].rearrange("p i (m t) -> p m t i", t=PACK),
+                in_=wt_raw[u][:].rearrange("p i (m t) -> p m i t", t=PACK),
             )
         load_gates(3, placed.tile([P, T], F32, name="gates3", offset=9 * T))
         gather_words(0, 0)
@@ -132,10 +132,10 @@ def tile_list_msg_silu_gate_kernel(
         nc.gpsimd.memset(wd_plane[:], 0)
         load_scale_rows(nc, wd_plane, wd_scales[0])
         gather_words(0, 1)
+        gather_words(1, 1)
         nc.vector.quantize_mx(out=w_codes[:, 1, :].bitcast(FP8X4), scales=w_scales[:, 1, :], in_=w_bf[1][:])
         wd_codes = sbuf([P, N], I32, "wd_codes", "w_bf1")
         nc.sync.dma_start(out=wd_codes[:], in_=wd_words[0].rearrange("p n i -> p (n i)").bitcast(I32))
-        gather_words(1, 1, placed.tile([P, HALF], U32, name="v_codes1_1", offset=8 * T, align_bytes=64))
 
         gated = {}
 
@@ -181,9 +181,9 @@ def tile_list_msg_silu_gate_kernel(
                 nc.scalar.activation(act[:, t, :], accs[t][:], ACT.Silu)
             return act
 
-        def interleave(act, lo, hi, slot=None):
+        def interleave(act, lo, hi):
             width = hi - lo
-            h_rows = sbuf([P, PACK, width], BF16, f"h_rows{lo}", slot)
+            h_rows = sbuf([P, PACK, width], BF16, f"h_rows{lo}")
             for t in range(PACK):
                 nc.scalar.activation(h_rows[:, t, :], act[:, t, :], ACT.Copy, scale=sm_cols[:, t : t + 1])
             h_bf = sbuf([P, width, PACK], BF16, f"h_bf{lo}")
@@ -242,13 +242,13 @@ def tile_list_msg_silu_gate_kernel(
         second = [sbuf([P, 1, q1], F32, f"second{n}") for n in range(2)]
         for n in range(2):
             message(h_second, n, second[n][:], 2 + n)
-        h_bf_rest = interleave(activate(q2, J, (6, 7, 0, 1), "act"), q2, J, "h_codes0")
+        h_bf_rest = interleave(activate(q2, J, (6, 7, 0, 1), "h_codes0"), q2, J)
         for n in range(N_TILES):
             scatter(n, 0, q1, first[n][:, 0, :])
         for n in range(2):
             scatter(n, q1, q2, second[n][:, 0, :])
         h_rest = quantise(h_bf_rest, q2, J, rest_scales[:])
-        second_filler = sbuf([P, 2, q1], F32, "second_filler", "h_codes0")
+        second_filler = sbuf([P, 2, q1], F32, "second_filler", f"h_rows{q2}")
         later = sbuf([P, N_TILES, J - q2], F32, "later")
         message(h_second, 2, second_filler[:], 5)
         for n in range(2, N_TILES):

@@ -96,12 +96,9 @@ def tile_list_msg_silu_gate_kernel(
             load_gates(n, placed.tile([P, T], F32, name=f"gates{n}", offset=n * 4 * T))
         v_codes = {}
 
-        def gather_words(i, half, tile=None):
-            if tile is None:
-                tile = sbuf([P, HALF], U32, f"v_codes{i}_{half}")
-            v_codes[i, half] = tile
-            entries = lists[i][:, half * HALF // GROUP : (half + 1) * HALF // GROUP]
-            nc.vector.tensor_copy(v_codes[i, half][:], tab[:].bitcast(U32).indirect(entries))
+        def gather_words(i):
+            v_codes[i] = sbuf([P, J], U32, f"v_codes{i}")
+            nc.vector.tensor_copy(v_codes[i][:], tab[:].bitcast(U32).indirect(lists[i][:]))
 
         w_bf = [sbuf([P, PACK * R], BF16, f"w_bf{i}") for i in range(2)]
         w_codes = sbuf([P, 2, R], U32, "w_codes")
@@ -125,14 +122,12 @@ def tile_list_msg_silu_gate_kernel(
                 in_=wt_raw[u][:].rearrange("p i (m t) -> p m i t", t=PACK),
             )
         load_gates(3, placed.tile([P, T], F32, name="gates3", offset=9 * T))
-        gather_words(0, 0)
-        gather_words(1, 0)
+        gather_words(0)
         nc.vector.quantize_mx(out=w_codes[:, 0, :].bitcast(FP8X4), scales=w_scales[:, 0, :], in_=w_bf[0][:])
         wd_plane = sbuf([P, N // 4], I32, "wd_plane", "w_bf0")
         nc.gpsimd.memset(wd_plane[:], 0)
         load_scale_rows(nc, wd_plane, wd_scales[0])
-        gather_words(0, 1)
-        gather_words(1, 1)
+        gather_words(1)
         nc.vector.quantize_mx(out=w_codes[:, 1, :].bitcast(FP8X4), scales=w_scales[:, 1, :], in_=w_bf[1][:])
         wd_codes = sbuf([P, N], I32, "wd_codes", "w_bf1")
         nc.sync.dma_start(out=wd_codes[:], in_=wd_words[0].rearrange("p n i -> p (n i)").bitcast(I32))
@@ -153,7 +148,7 @@ def tile_list_msg_silu_gate_kernel(
                 out=acc,
                 lhsT=w_codes[:, i, rows].bitcast(FP8X4),
                 lhsT_scale=w_scales[:, i, rows],
-                rhs=v_codes[i, lo // HALF][:, lo % HALF : lo % HALF + hi - lo].bitcast(FP8X4),
+                rhs=v_codes[i][:, lo:hi].bitcast(FP8X4),
                 rhs_scale=v_scales[:, i * J + lo : i * J + hi],
                 start=(i == 0),
                 stop=(i == 1),
@@ -234,26 +229,23 @@ def tile_list_msg_silu_gate_kernel(
         h_first = quantise(interleave(activate_first(q1), 0, q1), 0, q1, wd_plane[:].bitcast(U8)[4:P, 0:q1])
         gather_gates(3, "h_bf0")
         h_bf_second = interleave(activate(q1, q2, (4, 5), "act"), q1, q2)
-        first = [sbuf([P, 1, q1], F32, f"first{n}") for n in range(N_TILES)]
+        early = [sbuf([P, 1, q1 if n < 2 else q2], F32, f"early{n}") for n in range(N_TILES)]
         for n in range(N_TILES):
-            message(h_first, n, first[n][:], 2 + n)
+            message(h_first, n, early[n][:, :, 0:q1], 2 + n)
         h_second = quantise(h_bf_second, q1, q2, wd_plane[:].bitcast(U8)[8:P, 0:q1])
         zero_out(3, sbuf([P, T], F32, "out3", f"h_bf{q1}"))
-        second = [sbuf([P, 1, q1], F32, f"second{n}") for n in range(2)]
-        for n in range(2):
-            message(h_second, n, second[n][:], 2 + n)
+        for n in range(2, N_TILES):
+            message(h_second, n, early[n][:, :, q1:q2], n)
         h_bf_rest = interleave(activate(q2, J, (6, 7, 0, 1), "h_codes0"), q2, J)
         for n in range(N_TILES):
-            scatter(n, 0, q1, first[n][:, 0, :])
-        for n in range(2):
-            scatter(n, q1, q2, second[n][:, 0, :])
+            scatter(n, 0, early[n].shape[2], early[n][:, 0, :])
         h_rest = quantise(h_bf_rest, q2, J, rest_scales[:])
         second_filler = sbuf([P, 2, q1], F32, "second_filler", f"h_rows{q2}")
         later = sbuf([P, N_TILES, J - q2], F32, "later")
-        message(h_second, 2, second_filler[:], 5)
-        for n in range(2, N_TILES):
-            scatter(n, q1, q2, second_filler[:, n - 2, :])
-        for n in range(N_TILES):
-            message(h_rest, n, later[:, n : n + 1, :], (6 + n) % 8)
-        for n in range(N_TILES):
+        message(h_second, 0, second_filler[:], 5)
+        for n in range(2):
+            scatter(n, q1, q2, second_filler[:, n, :])
+        for n in (2, 3, 0, 1):
+            message(h_rest, n, later[:, n : n + 1, :], (4 + n) % 8)
+        for n in (2, 3, 0, 1):
             scatter(n, q2, J, later[:, n, :])

@@ -48,7 +48,7 @@ def tile_list_msg_silu_gate_kernel(
         src_list = keep.tile([P, J // GROUP], U16, name="src_list")
         dst_list = keep.tile([P, J // GROUP], U16, name="dst_list")
         tab_rows = placed.tile([P, T // 4], I32, name="tab_rows", offset=4 * T - T // 2)
-        nc.sync.dma_start(out=tab_rows[ROW0:P, :], in_=tab_scales[0].bitcast(I32))
+        nc.scalar.dma_start(out=tab_rows[ROW0:P, :], in_=tab_scales[0].bitcast(I32))
         nc.sync.dma_start(src_list[:], offs)
         nc.sync.dma_start(dst_list[:], offs2)
         lists = (src_list, dst_list)
@@ -100,7 +100,10 @@ def tile_list_msg_silu_gate_kernel(
             v_codes[i] = sbuf([P, J], U32, f"v_codes{i}")
             nc.vector.tensor_copy(v_codes[i][:], tab[:].bitcast(U32).indirect(lists[i][:]))
 
-        w_bf = [sbuf([P, PACK * R], BF16, f"w_bf{i}") for i in range(2)]
+        w_bf = [
+            sbuf([P, PACK * R], BF16, "w_bf0"),
+            placed.tile([P, PACK * R], BF16, name="w_bf1", offset=13 * T, align_bytes=64),
+        ]
         w_codes = sbuf([P, 2, R], U32, "w_codes")
         w_scales = sbuf([P, 2, R], U8, "w_scales")
         w_view = [w_bf[i][:].rearrange("p (t m i) -> p m i t", t=PACK, i=PACK) for i in range(2)]
@@ -115,6 +118,9 @@ def tile_list_msg_silu_gate_kernel(
 
         nc.scalar.copy(out=w_view[0], in_=ws_raw[:].rearrange("p i (m t) -> p m i t", t=PACK))
         load_gates(2, sbuf([P, T], F32, "gates2", "ws_raw"))
+        wd_plane = sbuf([P, N // 4], I32, "wd_plane", "picked")
+        nc.gpsimd.memset(wd_plane[:], 0)
+        load_scale_rows(nc, wd_plane, wd_scales[0])
 
         for u in range(2):
             nc.scalar.copy(
@@ -124,18 +130,15 @@ def tile_list_msg_silu_gate_kernel(
         load_gates(3, placed.tile([P, T], F32, name="gates3", offset=9 * T))
         gather_words(0)
         nc.vector.quantize_mx(out=w_codes[:, 0, :].bitcast(FP8X4), scales=w_scales[:, 0, :], in_=w_bf[0][:])
-        wd_plane = sbuf([P, N // 4], I32, "wd_plane", "w_bf0")
-        nc.gpsimd.memset(wd_plane[:], 0)
-        load_scale_rows(nc, wd_plane, wd_scales[0])
         gather_words(1)
         nc.vector.quantize_mx(out=w_codes[:, 1, :].bitcast(FP8X4), scales=w_scales[:, 1, :], in_=w_bf[1][:])
-        wd_codes = sbuf([P, N], I32, "wd_codes", "w_bf1")
+        wd_codes = placed.tile([P, N], I32, name="wd_codes", offset=13 * T, align_bytes=64)
         nc.sync.dma_start(out=wd_codes[:], in_=wd_words[0].rearrange("p n i -> p (n i)").bitcast(I32))
 
         gated = {}
 
-        def gather_gates(n, slot=None):
-            gated[n] = sbuf([P, J], F32, f"gated{n}", slot)
+        def gather_gates(n):
+            gated[n] = sbuf([P, J], F32, f"gated{n}")
             nc.vector.tensor_tensor(gated[n][:], gates[n][:].indirect(src_list[:]), edge_w[:], MULT)
 
         def zero_out(n, tile):
@@ -221,24 +224,26 @@ def tile_list_msg_silu_gate_kernel(
 
         q1, q2 = QUARTER, 2 * QUARTER
         rest_scales = sbuf([P, J - q2], U8, "rest_scales")
-        zero_out(0, sbuf([P, T], F32, "out0", "tab"))
-        for n in range(3):
-            gather_gates(n)
-            if n < 2:
-                zero_out(n + 1, placed.tile([P, T], F32, name=f"out{n + 1}", offset=n * 4 * T))
+        zero_out(0, placed.tile([P, T], F32, name="out0", offset=14 * T))
+        gather_gates(0)
+        zero_out(1, placed.tile([P, T], F32, name="out1", offset=0))
+        gather_gates(1)
+        gather_gates(2)
         h_first = quantise(interleave(activate_first(q1), 0, q1), 0, q1, wd_plane[:].bitcast(U8)[4:P, 0:q1])
-        gather_gates(3, "h_bf0")
+        gather_gates(3)
         h_bf_second = interleave(activate(q1, q2, (4, 5), "act"), q1, q2)
         early = [sbuf([P, 1, q1 if n < 2 else q2], F32, f"early{n}") for n in range(N_TILES)]
         for n in range(N_TILES):
             message(h_first, n, early[n][:, :, 0:q1], 2 + n)
         h_second = quantise(h_bf_second, q1, q2, wd_plane[:].bitcast(U8)[8:P, 0:q1])
-        zero_out(3, sbuf([P, T], F32, "out3", f"h_bf{q1}"))
+        zero_out(2, sbuf([P, T], F32, "out2", f"h_bf{q1}"))
         for n in range(2, N_TILES):
             message(h_second, n, early[n][:, :, q1:q2], n)
         h_bf_rest = interleave(activate(q2, J, (6, 7, 0, 1), "h_codes0"), q2, J)
         for n in range(N_TILES):
             scatter(n, 0, early[n].shape[2], early[n][:, 0, :])
+            if n == 0:
+                zero_out(3, sbuf([P, T], F32, "out3", "early0"))
         h_rest = quantise(h_bf_rest, q2, J, rest_scales[:])
         second_filler = sbuf([P, 2, q1], F32, "second_filler", f"h_rows{q2}")
         later = sbuf([P, N_TILES, J - q2], F32, "later")

@@ -57,10 +57,19 @@ def tile_list_msg_silu_gate_kernel(
 
         identity = sbuf([P, P], F32, "identity")
         v_plane = sbuf([P, 2 * J // 4], I32, "v_plane")
-        nc.vector.memset(tab_rows[0:ROW0, :], 0)
-        nc.vector.memset(identity[:], 0.0)
-        nc.vector.memset(v_plane[:], 0)
+        nc.gpsimd.memset(tab_rows[0:ROW0, :], 0)
+        nc.gpsimd.memset(identity[:], 0.0)
+        nc.gpsimd.memset(v_plane[:], 0)
         make_identity(nc, identity[:], nomemset=True)
+
+        outs = {}
+
+        def zero_out(n, tile):
+            outs[n] = tile
+            nc.gpsimd.memset(tile[:], 0.0)
+
+        for n in range(1, N_TILES):
+            zero_out(n, sbuf([P, T], F32, f"out{n}"))
 
         ws_raw = sbuf([P, PACK, R], F32, "ws_raw")
         nc.sync.dma_start(out=ws_raw[:], in_=ws.rearrange("(p i) r -> p i r", i=PACK))
@@ -75,8 +84,6 @@ def tile_list_msg_silu_gate_kernel(
             nc.sync.dma_start(out=wt_raw[u][:], in_=wt[:, cols].rearrange("(p i) r -> p i r", i=PACK))
         sm_cols = sbuf([P, PACK], F32, "sm_cols")
         nc.sync.dma_start(out=sm_cols[:], in_=sm.rearrange("(p t) -> p t", t=PACK))
-
-        outs = {}
 
         picked = sbuf([P, 2 * J], U8, "picked")
         for i in range(2):
@@ -141,10 +148,6 @@ def tile_list_msg_silu_gate_kernel(
             gated[n] = sbuf([P, J], F32, f"gated{n}")
             nc.vector.tensor_tensor(gated[n][:], gates[n][:].indirect(src_list[:]), edge_w[:], MULT)
 
-        def zero_out(n, tile):
-            outs[n] = tile
-            nc.gpsimd.memset(tile[:], 0.0)
-
         def project(i, t, lo, hi, acc):
             rows = slice(t * P, (t + 1) * P)
             nc.tensor.matmul_mx(
@@ -198,21 +201,22 @@ def tile_list_msg_silu_gate_kernel(
             )
             return h_codes, h_scales
 
-        def message(h, first_tile, dest, bank):
+        def multiply(h, n, acc):
             h_codes, h_scales = h
-            count, width = dest.shape[1], dest.shape[2]
-            acc = psum.tile([P, count, width], F32, name=f"y_acc{first_tile}_{bank}", tag=f"bank{bank}")
-            for u in range(count):
-                rows = slice((first_tile + u) * P, (first_tile + u + 1) * P)
-                nc.tensor.matmul_mx(
-                    out=acc[:, u, :],
-                    lhsT=wd_codes[:, rows].bitcast(FP8X4),
-                    lhsT_scale=wd_plane[:].bitcast(U8)[:, rows],
-                    rhs=h_codes[:].bitcast(FP8X4),
-                    rhs_scale=h_scales,
-                    start=True,
-                    stop=True,
-                )
+            rows = slice(n * P, (n + 1) * P)
+            nc.tensor.matmul_mx(
+                out=acc,
+                lhsT=wd_codes[:, rows].bitcast(FP8X4),
+                lhsT_scale=wd_plane[:].bitcast(U8)[:, rows],
+                rhs=h_codes[:].bitcast(FP8X4),
+                rhs_scale=h_scales,
+                start=True,
+                stop=True,
+            )
+
+        def message(h, n, dest, bank):
+            acc = psum.tile([P, dest.shape[1]], F32, name=f"y_acc{n}_{bank}", tag=f"bank{bank}")
+            multiply(h, n, acc[:])
             nc.scalar.copy(out=dest, in_=acc[:])
 
         def scatter(n, lo, hi, msgs):
@@ -226,31 +230,33 @@ def tile_list_msg_silu_gate_kernel(
         rest_scales = sbuf([P, J - q2], U8, "rest_scales")
         zero_out(0, placed.tile([P, T], F32, name="out0", offset=14 * T))
         gather_gates(0)
-        zero_out(1, placed.tile([P, T], F32, name="out1", offset=0))
         gather_gates(1)
         gather_gates(2)
         h_first = quantise(interleave(activate_first(q1), 0, q1), 0, q1, wd_plane[:].bitcast(U8)[4:P, 0:q1])
         gather_gates(3)
         h_bf_second = interleave(activate(q1, q2, (4, 5), "act"), q1, q2)
-        early = [sbuf([P, 1, q1 if n < 2 else q2], F32, f"early{n}") for n in range(N_TILES)]
-        for n in range(N_TILES):
-            message(h_first, n, early[n][:, :, 0:q1], 2 + n)
+        early = [sbuf([P, q1 if n == 0 else q2], F32, f"early{n}") for n in range(3)]
+        for n in range(3):
+            message(h_first, n, early[n][:, 0:q1], 2 + n)
+        held = psum.tile([P, q2], F32, name="held", tag="bank5")
+        multiply(h_first, 3, held[:, 0:q1])
         h_second = quantise(h_bf_second, q1, q2, wd_plane[:].bitcast(U8)[8:P, 0:q1])
-        zero_out(2, sbuf([P, T], F32, "out2", f"h_bf{q1}"))
-        for n in range(2, N_TILES):
-            message(h_second, n, early[n][:, :, q1:q2], n)
+        for n in (1, 2):
+            message(h_second, n, early[n][:, q1:q2], 1 + n)
+        second0 = sbuf([P, q1], F32, "second0")
+        message(h_second, 0, second0[:], 4)
+        multiply(h_second, 3, held[:, q1:q2])
         h_bf_rest = interleave(activate(q2, J, (6, 7, 0, 1), "h_codes0"), q2, J)
-        for n in range(N_TILES):
-            scatter(n, 0, early[n].shape[2], early[n][:, 0, :])
-            if n == 0:
-                zero_out(3, sbuf([P, T], F32, "out3", "early0"))
+        scatter(0, 0, q1, early[0][:])
+        for n in (1, 2):
+            scatter(n, 0, q2, early[n][:])
+        scatter(0, q1, q2, second0[:])
         h_rest = quantise(h_bf_rest, q2, J, rest_scales[:])
-        second_filler = sbuf([P, 2, q1], F32, "second_filler", f"h_rows{q2}")
+        filler = sbuf([P, q2], F32, "filler", f"h_rows{q2}")
+        nc.scalar.copy(out=filler[:], in_=held[:])
+        scatter(3, 0, q2, filler[:])
         later = sbuf([P, N_TILES, J - q2], F32, "later")
-        message(h_second, 0, second_filler[:], 5)
-        for n in range(2):
-            scatter(n, q1, q2, second_filler[:, n, :])
-        for n in (2, 3, 0, 1):
-            message(h_rest, n, later[:, n : n + 1, :], (4 + n) % 8)
-        for n in (2, 3, 0, 1):
+        for n in (1, 2, 3, 0):
+            message(h_rest, n, later[:, n, :], (5 + n) % 8 if n else 1)
+        for n in (1, 2, 3, 0):
             scatter(n, q2, J, later[:, n, :])

@@ -170,7 +170,7 @@ def tile_list_msg_silu_gate_kernel(
                     for i in range(2):
                         project(i, per_bank * b + u, lo, hi, acc[:, u, :])
                 nc.scalar.activation(act[:, per_bank * b : per_bank * (b + 1), :], acc[:], ACT.Silu)
-            return act
+            return [act[:, t, :] for t in range(PACK)]
 
         def activate_first(hi):
             act = sbuf([P, PACK, hi], F32, "act0", "act")
@@ -180,13 +180,13 @@ def tile_list_msg_silu_gate_kernel(
             for t in range(PACK):
                 project(1, t, 0, hi, accs[t][:])
                 nc.scalar.activation(act[:, t, :], accs[t][:], ACT.Silu)
-            return act
+            return [act[:, t, :] for t in range(PACK)]
 
         def interleave(act, lo, hi):
             width = hi - lo
             h_rows = sbuf([P, PACK, width], BF16, f"h_rows{lo}")
             for t in range(PACK):
-                nc.scalar.activation(h_rows[:, t, :], act[:, t, :], ACT.Copy, scale=sm_cols[:, t : t + 1])
+                nc.scalar.activation(h_rows[:, t, :], act[t], ACT.Copy, scale=sm_cols[:, t : t + 1])
             h_bf = sbuf([P, width, PACK], BF16, f"h_bf{lo}")
             nc.scalar.copy(
                 out=h_bf[:].rearrange("p (c i) t -> p c t i", i=4),
@@ -241,22 +241,39 @@ def tile_list_msg_silu_gate_kernel(
         held = psum.tile([P, q2], F32, name="held", tag="bank5")
         multiply(h_first, 3, held[:, 0:q1])
         h_second = quantise(h_bf_second, q1, q2, wd_plane[:].bitcast(U8)[8:P, 0:q1])
-        for n in (1, 2):
-            message(h_second, n, early[n][:, q1:q2], 1 + n)
-        second0 = sbuf([P, q1], F32, "second0")
-        message(h_second, 0, second0[:], 4)
+        act_head = sbuf([P, 1, J - q2], F32, "act_head", "h_codes0")
+        act_tail = sbuf([P, PACK - 1, J - q2], F32, "act_tail", f"h_bf{q1}")
+        act_rest = [act_head[:, 0, :]] + [act_tail[:, t, :] for t in range(PACK - 1)]
+
+        def activate_rest(t, bank):
+            acc = psum.tile([P, J - q2], F32, name=f"acc_rest{t}", tag=f"bank{bank}")
+            for i in range(2):
+                project(i, t, q2, J, acc[:])
+            nc.scalar.activation(act_rest[t], acc[:], ACT.Silu)
+
+        for t, bank in enumerate((6, 7)):
+            activate_rest(t, bank)
+        message(h_second, 1, early[1][:, q1:q2], 2)
+        for t, bank in ((2, 0), (3, 1)):
+            activate_rest(t, bank)
+        message(h_second, 2, early[2][:, q1:q2], 3)
+        held0 = psum.tile([P, q1], F32, name="held0", tag="bank4")
+        multiply(h_second, 0, held0[:])
         multiply(h_second, 3, held[:, q1:q2])
-        h_bf_rest = interleave(activate(q2, J, (6, 7, 0, 1), "h_codes0"), q2, J)
+        h_bf_rest = interleave(act_rest, q2, J)
         scatter(0, 0, q1, early[0][:])
         for n in (1, 2):
             scatter(n, 0, q2, early[n][:])
-        scatter(0, q1, q2, second0[:])
         h_rest = quantise(h_bf_rest, q2, J, rest_scales[:])
         filler = sbuf([P, q2], F32, "filler", f"h_rows{q2}")
         nc.scalar.copy(out=filler[:], in_=held[:])
         scatter(3, 0, q2, filler[:])
-        later = sbuf([P, N_TILES, J - q2], F32, "later")
-        for n in (1, 2, 3, 0):
-            message(h_rest, n, later[:, n, :], (5 + n) % 8 if n else 1)
-        for n in (1, 2, 3, 0):
-            scatter(n, q2, J, later[:, n, :])
+        later = sbuf([P, N_TILES - 1, J - q2], F32, "later")
+        for n in (1, 2, 3):
+            message(h_rest, n, later[:, n - 1, :], (5 + n) % 8)
+        last = sbuf([P, J - q1], F32, "last", f"h_bf{q2}")
+        nc.scalar.copy(out=last[:, 0:q1], in_=held0[:])
+        message(h_rest, 0, last[:, q1 : J - q1], 1)
+        for n in (1, 2, 3):
+            scatter(n, q2, J, later[:, n - 1, :])
+        scatter(0, q1, J, last[:])

@@ -223,8 +223,11 @@ def tile_list_msg_silu_gate_kernel(
             nc.vector.tensor_tensor(
                 outs[n][:].indirect(dst_list[:, lo // GROUP : hi // GROUP]), msgs, gated[n][:, lo:hi], MULT
             )
-            if hi == J:
+            if hi == J and n > 0:
                 nc.sync.dma_start(out=out[n * P : (n + 1) * P, :], in_=outs[n][:])
+            elif hi == J:
+                nc.sync.dma_start(out=out[0:P, 0 : T // 2], in_=outs[0][:, 0 : T // 2])
+                nc.scalar.dma_start(out=out[0:P, T // 2 : T], in_=outs[0][:, T // 2 : T])
 
         q1, q2 = QUARTER, 2 * QUARTER
         rest_scales = sbuf([P, J - q2], U8, "rest_scales")

@@ -226,8 +226,9 @@ def tile_list_msg_silu_gate_kernel(
             if hi == J and n > 0:
                 nc.sync.dma_start(out=out[n * P : (n + 1) * P, :], in_=outs[n][:])
             elif hi == J:
-                nc.sync.dma_start(out=out[0:P, 0 : T // 2], in_=outs[0][:, 0 : T // 2])
-                nc.scalar.dma_start(out=out[0:P, T // 2 : T], in_=outs[0][:, T // 2 : T])
+                cut = 3 * T // 8
+                nc.sync.dma_start(out=out[0:P, 0:cut], in_=outs[0][:, 0:cut])
+                nc.scalar.dma_start(out=out[0:P, cut:T], in_=outs[0][:, cut:T])
 
         q1, q2 = QUARTER, 2 * QUARTER
         rest_scales = sbuf([P, J - q2], U8, "rest_scales")

@@ -23,6 +23,8 @@ HALF = J // 2
 QUARTER = J // 4
 N_TILES = N // P
 ROW0 = P - K // 32
+LAST = N_TILES - 1
+PIECE_STARTS = (608, 672, 736, 832, 928, J)
 
 
 def load_scale_rows(nc, plane, rows):
@@ -134,7 +136,7 @@ def tile_list_msg_silu_gate_kernel(
                 out=w_view[1][:, u * P // 2 : (u + 1) * P // 2],
                 in_=wt_raw[u][:].rearrange("p i (m t) -> p m i t", t=PACK),
             )
-        load_gates(3, placed.tile([P, T], F32, name="gates3", offset=9 * T))
+        load_gates(LAST, placed.tile([P, T], F32, name="gates3", offset=9 * T))
         gather_words(0)
         nc.vector.quantize_mx(out=w_codes[:, 0, :].bitcast(FP8X4), scales=w_scales[:, 0, :], in_=w_bf[0][:])
         gather_words(1)
@@ -142,11 +144,14 @@ def tile_list_msg_silu_gate_kernel(
         wd_codes = placed.tile([P, N], I32, name="wd_codes", offset=13 * T, align_bytes=64)
         nc.sync.dma_start(out=wd_codes[:], in_=wd_words[0].rearrange("p n i -> p (n i)").bitcast(I32))
 
-        gated = {}
+        gated = [sbuf([P, J + (QUARTER if n == LAST else 0)], F32, f"gated{n}") for n in range(N_TILES)]
 
-        def gather_gates(n):
-            gated[n] = sbuf([P, J], F32, f"gated{n}")
-            nc.vector.tensor_tensor(gated[n][:], gates[n][:].indirect(src_list[:]), edge_w[:], MULT)
+        def gather_gates(n, lo, hi):
+            offsets = src_list[:, lo // GROUP : hi // GROUP]
+            nc.vector.tensor_tensor(gated[n][:, lo:hi], gates[n][:].indirect(offsets), edge_w[:, lo:hi], MULT)
+
+        def gather_piece(k):
+            gather_gates(LAST, PIECE_STARTS[k], PIECE_STARTS[k + 1])
 
         def project(i, t, lo, hi, acc):
             rows = slice(t * P, (t + 1) * P)
@@ -177,17 +182,19 @@ def tile_list_msg_silu_gate_kernel(
             accs = [psum.tile([P, hi], F32, name=f"acc0_{t}", tag=f"bank{t}") for t in range(PACK)]
             for t in range(PACK):
                 project(0, t, 0, hi, accs[t][:])
-            for t in range(PACK):
                 project(1, t, 0, hi, accs[t][:])
                 nc.scalar.activation(act[:, t, :], accs[t][:], ACT.Silu)
             return [act[:, t, :] for t in range(PACK)]
 
-        def interleave(act, lo, hi):
-            width = hi - lo
-            h_rows = sbuf([P, PACK, width], BF16, f"h_rows{lo}")
+        def scale(act, lo, hi):
+            h_rows = sbuf([P, PACK, hi - lo], BF16, f"h_rows{lo}")
             for t in range(PACK):
                 nc.scalar.activation(h_rows[:, t, :], act[t], ACT.Copy, scale=sm_cols[:, t : t + 1])
-            h_bf = sbuf([P, width, PACK], BF16, f"h_bf{lo}")
+            return h_rows
+
+        def interleave(h_rows, lo, hi, slot=None):
+            width = hi - lo
+            h_bf = sbuf([P, width, PACK], BF16, f"h_bf{lo}", slot)
             nc.scalar.copy(
                 out=h_bf[:].rearrange("p (c i) t -> p c t i", i=4),
                 in_=h_rows[:].rearrange("p t (c i) -> p c t i", i=4),
@@ -199,85 +206,90 @@ def tile_list_msg_silu_gate_kernel(
             nc.vector.quantize_mx(
                 out=h_codes[:].bitcast(FP8X4), scales=h_scales, in_=h_bf[:].rearrange("p c t -> p (c t)")
             )
-            return h_codes, h_scales
+            return h_codes[:], h_scales
 
-        def multiply(h, n, acc):
-            h_codes, h_scales = h
-            rows = slice(n * P, (n + 1) * P)
-            nc.tensor.matmul_mx(
-                out=acc,
-                lhsT=wd_codes[:, rows].bitcast(FP8X4),
-                lhsT_scale=wd_plane[:].bitcast(U8)[:, rows],
-                rhs=h_codes[:].bitcast(FP8X4),
-                rhs_scale=h_scales,
-                start=True,
-                stop=True,
-            )
+        def messages(parts, dest, bank):
+            width = parts[0][2] - parts[0][1]
+            acc = psum.tile([P, len(parts), width], F32, name=f"y_acc{parts[0][0]}_{parts[0][1]}", tag=f"bank{bank}")
+            for at, (n, lo, hi) in enumerate(parts):
+                start = max(s for s in h if s <= lo)
+                h_codes, h_scales = h[start]
+                rows = slice(n * P, (n + 1) * P)
+                nc.tensor.matmul_mx(
+                    out=acc[:, at, :],
+                    lhsT=wd_codes[:, rows].bitcast(FP8X4),
+                    lhsT_scale=wd_plane[:].bitcast(U8)[:, rows],
+                    rhs=h_codes[:, lo - start : hi - start].bitcast(FP8X4),
+                    rhs_scale=h_scales[:, lo - start : hi - start],
+                    start=True,
+                    stop=True,
+                )
+                msgs[n, lo] = dest[:, at * width : (at + 1) * width]
+            return lambda: nc.scalar.copy(out=dest, in_=acc[:].rearrange("p a w -> p (a w)"))
 
-        def message(h, n, dest, bank):
-            acc = psum.tile([P, dest.shape[1]], F32, name=f"y_acc{n}_{bank}", tag=f"bank{bank}")
-            multiply(h, n, acc[:])
-            nc.scalar.copy(out=dest, in_=acc[:])
-
-        def scatter(n, lo, hi, msgs):
+        def scatter(n, lo, hi):
             nc.vector.tensor_tensor(
-                outs[n][:].indirect(dst_list[:, lo // GROUP : hi // GROUP]), msgs, gated[n][:, lo:hi], MULT
+                outs[n][:].indirect(dst_list[:, lo // GROUP : hi // GROUP]), msgs[n, lo], gated[n][:, lo:hi], MULT
             )
-            if hi == J and n > 0:
+            if hi == J and n < LAST:
                 nc.sync.dma_start(out=out[n * P : (n + 1) * P, :], in_=outs[n][:])
             elif hi == J:
                 cut = 3 * T // 8
-                nc.sync.dma_start(out=out[0:P, 0:cut], in_=outs[0][:, 0:cut])
-                nc.scalar.dma_start(out=out[0:P, cut:T], in_=outs[0][:, cut:T])
+                nc.sync.dma_start(out=out[n * P : (n + 1) * P, 0:cut], in_=outs[n][:, 0:cut])
+                nc.scalar.dma_start(out=out[n * P : (n + 1) * P, cut:T], in_=outs[n][:, cut:T])
 
-        q1, q2 = QUARTER, 2 * QUARTER
+        q1, q2, q3 = QUARTER, 2 * QUARTER, 3 * QUARTER
+        h, msgs = {}, {}
+
+        def ahead_of_piece(k):
+            return gated[LAST][:, PIECE_STARTS[k] : PIECE_STARTS[k] + HALF]
+
         rest_scales = sbuf([P, J - q2], U8, "rest_scales")
         zero_out(0, placed.tile([P, T], F32, name="out0", offset=14 * T))
-        gather_gates(0)
-        gather_gates(1)
-        gather_gates(2)
-        h_first = quantise(interleave(activate_first(q1), 0, q1), 0, q1, wd_plane[:].bitcast(U8)[4:P, 0:q1])
-        gather_gates(3)
-        h_bf_second = interleave(activate(q1, q2, (4, 5), "act"), q1, q2)
-        early = [sbuf([P, q1 if n == 0 else q2], F32, f"early{n}") for n in range(3)]
-        for n in range(3):
-            message(h_first, n, early[n][:, 0:q1], 2 + n)
-        held = psum.tile([P, q2], F32, name="held", tag="bank5")
-        multiply(h_first, 3, held[:, 0:q1])
-        h_second = quantise(h_bf_second, q1, q2, wd_plane[:].bitcast(U8)[8:P, 0:q1])
-        act_head = sbuf([P, 1, J - q2], F32, "act_head", "h_codes0")
-        act_tail = sbuf([P, PACK - 1, J - q2], F32, "act_tail", f"h_bf{q1}")
-        act_rest = [act_head[:, 0, :]] + [act_tail[:, t, :] for t in range(PACK - 1)]
-
-        def activate_rest(t, bank):
+        gather_gates(0, 0, J)
+        gather_gates(1, 0, J)
+        gather_gates(2, 0, J)
+        h[0] = quantise(interleave(scale(activate_first(q1), 0, q1), 0, q1), 0, q1, wd_plane[:].bitcast(U8)[4:P, 0:q1])
+        gather_gates(LAST, 0, PIECE_STARTS[0])
+        h_rows_second = scale(activate(q1, q2, (4, 5), "act"), q1, q2)
+        first = ahead_of_piece(0)[:, 0:q1]
+        for lo, bank in ((0, 0), (P, 3)):
+            messages([(0, lo, lo + P)], first[:, lo : lo + P], bank)()
+        msgs[0, 0] = first
+        messages([(1, 0, q1)], sbuf([P, q1], F32, "msg_second")[:], 1)()
+        empty_pair = messages([(2, 0, q1), (LAST, 0, q1)], ahead_of_piece(1), 2)
+        h_bf_second = interleave(h_rows_second, q1, q2, "h_codes0")
+        scatter(0, 0, q1)
+        scatter(1, 0, q1)
+        gather_piece(0)
+        h[q1] = quantise(h_bf_second, q1, q2, wd_plane[:].bitcast(U8)[8:P, 0:q1])
+        act_all = sbuf([P, PACK, J - q2], F32, "act_rest", f"h_rows{q1}")
+        act_rest = [act_all[:, t, :] for t in range(PACK)]
+        for t, bank in enumerate((6, 7, 0, 1)):
             acc = psum.tile([P, J - q2], F32, name=f"acc_rest{t}", tag=f"bank{bank}")
             for i in range(2):
                 project(i, t, q2, J, acc[:])
             nc.scalar.activation(act_rest[t], acc[:], ACT.Silu)
-
-        for t, bank in enumerate((6, 7)):
-            activate_rest(t, bank)
-        message(h_second, 1, early[1][:, q1:q2], 2)
-        for t, bank in ((2, 0), (3, 1)):
-            activate_rest(t, bank)
-        message(h_second, 2, early[2][:, q1:q2], 3)
-        held0 = psum.tile([P, q1], F32, name="held0", tag="bank4")
-        multiply(h_second, 0, held0[:])
-        multiply(h_second, 3, held[:, q1:q2])
-        h_bf_rest = interleave(act_rest, q2, J)
-        scatter(0, 0, q1, early[0][:])
-        for n in (1, 2):
-            scatter(n, 0, q2, early[n][:])
-        h_rest = quantise(h_bf_rest, q2, J, rest_scales[:])
-        filler = sbuf([P, q2], F32, "filler", f"h_rows{q2}")
-        nc.scalar.copy(out=filler[:], in_=held[:])
-        scatter(3, 0, q2, filler[:])
-        later = sbuf([P, N_TILES - 1, J - q2], F32, "later")
-        for n in (1, 2, 3):
-            message(h_rest, n, later[:, n - 1, :], (5 + n) % 8)
-        last = sbuf([P, J - q1], F32, "last", f"h_bf{q2}")
-        nc.scalar.copy(out=last[:, 0:q1], in_=held0[:])
-        message(h_rest, 0, last[:, q1 : J - q1], 1)
-        for n in (1, 2, 3):
-            scatter(n, q2, J, later[:, n - 1, :])
-        scatter(0, q1, J, last[:])
+            if t == 0:
+                empty_pair()
+        scatter(2, 0, q1)
+        scatter(LAST, 0, q1)
+        gather_piece(1)
+        messages([(0, q1, q2), (1, q1, q2)], sbuf([P, HALF], F32, "msg_q1")[:], 3)()
+        h_bf_rest = interleave(scale(act_rest, q2, J), q2, J)
+        messages([(2, q1, q2), (LAST, q1, q2)], sbuf([P, HALF], F32, "msg_cover", f"h_rows{q2}")[:], 4)()
+        scatter(0, q1, q2)
+        scatter(1, q1, q2)
+        h[q2] = quantise(h_bf_rest, q2, J, rest_scales[:])
+        scatter(2, q1, q2)
+        scatter(LAST, q1, q2)
+        messages([(0, q3, J), (1, q3, J)], sbuf([P, HALF], F32, "msg_q3")[:], 5)()
+        messages([(0, q2, q3), (1, q2, q3)], ahead_of_piece(2), 6)()
+        for n, bank in ((2, 7), (LAST, 0)):
+            messages([(n, q2, J)], sbuf([P, HALF], F32, f"msg_half{n}")[:], bank)()
+        scatter(0, q2, q3)
+        for k, (n, lo) in enumerate(((1, q2), (0, q3), (1, q3))):
+            scatter(n, lo, lo + QUARTER)
+            gather_piece(2 + k)
+        for n in (2, LAST):
+            scatter(n, q2, J)

@@ -24,7 +24,9 @@ QUARTER = J // 4
 N_TILES = N // P
 ROW0 = P - K // 32
 LAST = N_TILES - 1
-PIECE_STARTS = (608, 672, 736, 832, 928, J)
+PIECE_STARTS = (608, 736, 832, 928, J)
+UPPER_STARTS = (HALF, HALF + 160, HALF + 320, J)
+SHIFT = 64
 
 
 def load_scale_rows(nc, plane, rows):
@@ -144,11 +146,18 @@ def tile_list_msg_silu_gate_kernel(
         wd_codes = placed.tile([P, N], I32, name="wd_codes", offset=13 * T, align_bytes=64)
         nc.sync.dma_start(out=wd_codes[:], in_=wd_words[0].rearrange("p n i -> p (n i)").bitcast(I32))
 
-        gated = [sbuf([P, J + (QUARTER if n == LAST else 0)], F32, f"gated{n}") for n in range(N_TILES)]
+        gated = [sbuf([P, J + (QUARTER if n >= 2 else 0)], F32, f"gated{n}") for n in range(N_TILES)]
+
+        def gated_cols(n, lo, hi):
+            shift = SHIFT if n == 2 and lo >= HALF else 0
+            return gated[n][:, lo - shift : hi - shift]
 
         def gather_gates(n, lo, hi):
             offsets = src_list[:, lo // GROUP : hi // GROUP]
-            nc.vector.tensor_tensor(gated[n][:, lo:hi], gates[n][:].indirect(offsets), edge_w[:, lo:hi], MULT)
+            nc.vector.tensor_tensor(gated_cols(n, lo, hi), gates[n][:].indirect(offsets), edge_w[:, lo:hi], MULT)
+
+        def gather_upper(k):
+            gather_gates(2, UPPER_STARTS[k], UPPER_STARTS[k + 1])
 
         def gather_piece(k):
             gather_gates(LAST, PIECE_STARTS[k], PIECE_STARTS[k + 1])
@@ -182,6 +191,7 @@ def tile_list_msg_silu_gate_kernel(
             accs = [psum.tile([P, hi], F32, name=f"acc0_{t}", tag=f"bank{t}") for t in range(PACK)]
             for t in range(PACK):
                 project(0, t, 0, hi, accs[t][:])
+            for t in range(PACK):
                 project(1, t, 0, hi, accs[t][:])
                 nc.scalar.activation(act[:, t, :], accs[t][:], ACT.Silu)
             return [act[:, t, :] for t in range(PACK)]
@@ -229,7 +239,7 @@ def tile_list_msg_silu_gate_kernel(
 
         def scatter(n, lo, hi):
             nc.vector.tensor_tensor(
-                outs[n][:].indirect(dst_list[:, lo // GROUP : hi // GROUP]), msgs[n, lo], gated[n][:, lo:hi], MULT
+                outs[n][:].indirect(dst_list[:, lo // GROUP : hi // GROUP]), msgs[n, lo], gated_cols(n, lo, hi), MULT
             )
             if hi == J and n < LAST:
                 nc.sync.dma_start(out=out[n * P : (n + 1) * P, :], in_=outs[n][:])
@@ -248,20 +258,20 @@ def tile_list_msg_silu_gate_kernel(
         zero_out(0, placed.tile([P, T], F32, name="out0", offset=14 * T))
         gather_gates(0, 0, J)
         gather_gates(1, 0, J)
-        gather_gates(2, 0, J)
+        gather_gates(2, 0, HALF)
         h[0] = quantise(interleave(scale(activate_first(q1), 0, q1), 0, q1), 0, q1, wd_plane[:].bitcast(U8)[4:P, 0:q1])
         gather_gates(LAST, 0, PIECE_STARTS[0])
         h_rows_second = scale(activate(q1, q2, (4, 5), "act"), q1, q2)
-        first = ahead_of_piece(0)[:, 0:q1]
+        first = gated_cols(2, UPPER_STARTS[1], UPPER_STARTS[1] + q1)
         for lo, bank in ((0, 0), (P, 3)):
             messages([(0, lo, lo + P)], first[:, lo : lo + P], bank)()
         msgs[0, 0] = first
         messages([(1, 0, q1)], sbuf([P, q1], F32, "msg_second")[:], 1)()
-        empty_pair = messages([(2, 0, q1), (LAST, 0, q1)], ahead_of_piece(1), 2)
+        empty_pair = messages([(2, 0, q1), (LAST, 0, q1)], ahead_of_piece(0), 2)
         h_bf_second = interleave(h_rows_second, q1, q2, "h_codes0")
         scatter(0, 0, q1)
         scatter(1, 0, q1)
-        gather_piece(0)
+        gather_upper(1)
         h[q1] = quantise(h_bf_second, q1, q2, wd_plane[:].bitcast(U8)[8:P, 0:q1])
         act_all = sbuf([P, PACK, J - q2], F32, "act_rest", f"h_rows{q1}")
         act_rest = [act_all[:, t, :] for t in range(PACK)]
@@ -274,22 +284,24 @@ def tile_list_msg_silu_gate_kernel(
                 empty_pair()
         scatter(2, 0, q1)
         scatter(LAST, 0, q1)
-        gather_piece(1)
-        messages([(0, q1, q2), (1, q1, q2)], sbuf([P, HALF], F32, "msg_q1")[:], 3)()
+        gather_piece(0)
+        messages([(0, q1, q2), (1, q1, q2)], gated_cols(2, UPPER_STARTS[2], UPPER_STARTS[2] + HALF), 3)()
         h_bf_rest = interleave(scale(act_rest, q2, J), q2, J)
         messages([(2, q1, q2), (LAST, q1, q2)], sbuf([P, HALF], F32, "msg_cover", f"h_rows{q2}")[:], 4)()
         scatter(0, q1, q2)
         scatter(1, q1, q2)
+        gather_upper(2)
         h[q2] = quantise(h_bf_rest, q2, J, rest_scales[:])
         scatter(2, q1, q2)
         scatter(LAST, q1, q2)
+        gather_upper(0)
         messages([(0, q3, J), (1, q3, J)], sbuf([P, HALF], F32, "msg_q3")[:], 5)()
-        messages([(0, q2, q3), (1, q2, q3)], ahead_of_piece(2), 6)()
+        messages([(0, q2, q3), (1, q2, q3)], ahead_of_piece(1), 6)()
         for n, bank in ((2, 7), (LAST, 0)):
             messages([(n, q2, J)], sbuf([P, HALF], F32, f"msg_half{n}")[:], bank)()
         scatter(0, q2, q3)
         for k, (n, lo) in enumerate(((1, q2), (0, q3), (1, q3))):
             scatter(n, lo, lo + QUARTER)
-            gather_piece(2 + k)
+            gather_piece(1 + k)
         for n in (2, LAST):
             scatter(n, q2, J)

@@ -20,19 +20,12 @@ P = 128
 PACK = 4
 GROUP = 16
 HALF = J // 2
-QUARTER = J // 4
+Q = J // 4
+E = J // 8
 N_TILES = N // P
 ROW0 = P - K // 32
 LAST = N_TILES - 1
-PIECE_STARTS = (608, 736, 832, 928, J)
-UPPER_STARTS = (HALF, HALF + 160, HALF + 320, J)
-SHIFT = 64
-
-
-def load_scale_rows(nc, plane, rows):
-    by_place = rows.bitcast(I32).rearrange("(q r) w -> r q w", r=4)
-    for r in range(4):
-        nc.sync.dma_start(out=plane[r:P:32, :], in_=by_place[r])
+KIB = 1024
 
 
 def tile_list_msg_silu_gate_kernel(
@@ -43,19 +36,28 @@ def tile_list_msg_silu_gate_kernel(
     with ExitStack() as ctx:
         keep = ctx.enter_context(tc.tile_pool(name="keep", bufs=1))
         psum = ctx.enter_context(tc.psum_pool(name="psum", bufs=1))
+        placed = ctx.enter_context(tc.tile_pool(name="placed", bufs=1))
 
         def sbuf(shape, dtype, name, slot=None):
             return keep.tile(shape, dtype, name=name, tag=slot or name, align_bytes=64)
 
-        placed = ctx.enter_context(tc.tile_pool(name="placed", bufs=1))
+        def at(offset, shape, dtype, name):
+            return placed.tile(shape, dtype, name=name, offset=offset, align_bytes=64)
+
+        def bank(b, shape, name):
+            return psum.tile(shape, F32, name=name, tag=f"bank{b}")
 
         src_list = keep.tile([P, J // GROUP], U16, name="src_list")
         dst_list = keep.tile([P, J // GROUP], U16, name="dst_list")
-        tab_rows = placed.tile([P, T // 4], I32, name="tab_rows", offset=4 * T - T // 2)
+        tab_rows = at(7 * KIB, [P, T // 4], I32, "tab_rows")
         nc.scalar.dma_start(out=tab_rows[ROW0:P, :], in_=tab_scales[0].bitcast(I32))
         nc.sync.dma_start(src_list[:], offs)
         nc.sync.dma_start(dst_list[:], offs2)
         lists = (src_list, dst_list)
+
+        def entries(i, lo, hi):
+            return lists[i][:, lo // GROUP : hi // GROUP]
+
         edge_cols = sbuf([P, J // P], F32, "edge_cols")
         nc.scalar.dma_start(out=edge_cols[:], in_=wgo[0].rearrange("(p c) -> p c", p=P))
 
@@ -72,236 +74,275 @@ def tile_list_msg_silu_gate_kernel(
             outs[n] = tile
             nc.gpsimd.memset(tile[:], 0.0)
 
-        for n in range(1, N_TILES):
+        for n in range(2):
             zero_out(n, sbuf([P, T], F32, f"out{n}"))
 
-        ws_raw = sbuf([P, PACK, R], F32, "ws_raw")
+        ws_raw = at(16 * KIB, [P, PACK, R], F32, "ws_raw")
         nc.sync.dma_start(out=ws_raw[:], in_=ws.rearrange("(p i) r -> p i r", i=PACK))
         tab = sbuf([P, T], I32, "tab")
         nc.sync.dma_start(out=tab[:], in_=tab_words[0].rearrange("p t i -> p (t i)").bitcast(I32))
-        wt_raw = [
-            sbuf([P, PACK, R // 2], F32, "wt_raw0"),
-            placed.tile([P, PACK, R // 2], F32, name="wt_raw1", offset=8 * T),
-        ]
+        wt_raw = [at(32 * KIB, [P, PACK, R // 2], F32, "wt_raw0"), sbuf([P, PACK, R // 2], F32, "wt_raw1")]
         for u in range(2):
             cols = slice(u * R // 2, (u + 1) * R // 2)
             nc.sync.dma_start(out=wt_raw[u][:], in_=wt[:, cols].rearrange("(p i) r -> p i r", i=PACK))
         sm_cols = sbuf([P, PACK], F32, "sm_cols")
         nc.sync.dma_start(out=sm_cols[:], in_=sm.rearrange("(p t) -> p t", t=PACK))
 
-        picked = sbuf([P, 2 * J], U8, "picked")
-        for i in range(2):
-            nc.vector.tensor_copy(picked[:, i * J : (i + 1) * J], tab_rows[:].bitcast(U8).indirect(lists[i][:]))
-        for q in range(4):
-            nc.sync.dma_start(
-                out=v_plane[32 * q : 32 * q + 4, :], in_=picked[ROW0 + 4 * q : ROW0 + 4 * q + 4, :].bitcast(I32)
-            )
-        v_scales = v_plane[:].bitcast(U8)
+        picked = [sbuf([P, J], U8, "picked0"), at(61 * KIB, [P, J], U8, "picked1")]
+        for half in range(2):
+            for i in range(2):
+                nc.vector.tensor_copy(
+                    picked[half][:, i * HALF : (i + 1) * HALF],
+                    tab_rows[:].bitcast(U8).indirect(entries(i, half * HALF, (half + 1) * HALF)),
+                )
+
+        def move_scale_rows(half):
+            for q in range(4):
+                nc.sync.dma_start(
+                    out=v_plane[32 * q : 32 * q + 4, half * Q : (half + 1) * Q],
+                    in_=picked[half][ROW0 + 4 * q : ROW0 + 4 * q + 4, :].bitcast(I32),
+                )
+
+        move_scale_rows(0)
         gates = {}
 
-        def load_gates(n, tile):
-            gates[n] = tile
-            nc.sync.dma_start(out=tile[:], in_=gT[n * P : (n + 1) * P, :])
+        def load_gates(n, offset):
+            gates[n] = at(offset, [P, T], F32, f"gates{n}")
+            nc.sync.dma_start(out=gates[n][:], in_=gT[n * P : (n + 1) * P, :])
 
         for n in range(2):
-            load_gates(n, placed.tile([P, T], F32, name=f"gates{n}", offset=n * 4 * T))
-        v_codes = {}
+            load_gates(n, n * 8 * KIB)
 
-        def gather_words(i):
-            v_codes[i] = sbuf([P, J], U32, f"v_codes{i}")
-            nc.vector.tensor_copy(v_codes[i][:], tab[:].bitcast(U32).indirect(lists[i][:]))
-
-        w_bf = [
-            sbuf([P, PACK * R], BF16, "w_bf0"),
-            placed.tile([P, PACK * R], BF16, name="w_bf1", offset=13 * T, align_bytes=64),
-        ]
-        w_codes = sbuf([P, 2, R], U32, "w_codes")
-        w_scales = sbuf([P, 2, R], U8, "w_scales")
-        w_view = [w_bf[i][:].rearrange("p (t m i) -> p m i t", t=PACK, i=PACK) for i in range(2)]
         edge_w = sbuf([P, J], F32, "edge_w")
         edge_view = edge_w[:].rearrange("p (m b c) -> p b m c", b=2, c=4)
         for b in range(2):
-            spread = psum.tile([P, 4, P], F32, name=f"spread{b}", tag=f"bank{6 + b}")
+            spread = bank(6 + b, [P, 4, P], f"spread{b}")
             for c in range(4):
                 column = edge_cols[:, 4 * b + c : 4 * b + c + 1].to_broadcast([P, P])
                 nc.tensor.transpose(spread[:, c, :], column, identity[:])
             nc.scalar.copy(out=edge_view[:, b], in_=spread[:].rearrange("p c m -> p m c"))
 
+        w_bf = [sbuf([P, PACK * R], BF16, "w_bf0"), at(40 * KIB, [P, PACK * R], BF16, "w_bf1")]
+        w_codes = sbuf([P, 2, R], U32, "w_codes")
+        w_scales = sbuf([P, 2, R], U8, "w_scales")
+        w_view = [w_bf[i][:].rearrange("p (t m i) -> p m i t", t=PACK, i=PACK) for i in range(2)]
         nc.scalar.copy(out=w_view[0], in_=ws_raw[:].rearrange("p i (m t) -> p m i t", t=PACK))
-        load_gates(2, sbuf([P, T], F32, "gates2", "ws_raw"))
-        wd_plane = sbuf([P, N // 4], I32, "wd_plane", "picked")
+        wd_plane = at(16 * KIB, [P, N // 4], I32, "wd_plane")
         nc.gpsimd.memset(wd_plane[:], 0)
-        load_scale_rows(nc, wd_plane, wd_scales[0])
-
+        by_place = wd_scales[0].bitcast(I32).rearrange("(q r) w -> r q w", r=4)
+        for r in range(4):
+            nc.sync.dma_start(out=wd_plane[r:P:32, :], in_=by_place[r])
+        load_gates(2, 24 * KIB - 64)
+        wd_codes = at(16 * KIB + N, [P, N], I32, "wd_codes")
+        nc.sync.dma_start(out=wd_codes[:], in_=wd_words[0].rearrange("p n i -> p (n i)").bitcast(I32))
         for u in range(2):
             nc.scalar.copy(
                 out=w_view[1][:, u * P // 2 : (u + 1) * P // 2],
                 in_=wt_raw[u][:].rearrange("p i (m t) -> p m i t", t=PACK),
             )
-        load_gates(LAST, placed.tile([P, T], F32, name="gates3", offset=9 * T))
-        gather_words(0)
-        nc.vector.quantize_mx(out=w_codes[:, 0, :].bitcast(FP8X4), scales=w_scales[:, 0, :], in_=w_bf[0][:])
-        gather_words(1)
-        nc.vector.quantize_mx(out=w_codes[:, 1, :].bitcast(FP8X4), scales=w_scales[:, 1, :], in_=w_bf[1][:])
-        wd_codes = placed.tile([P, N], I32, name="wd_codes", offset=13 * T, align_bytes=64)
-        nc.sync.dma_start(out=wd_codes[:], in_=wd_words[0].rearrange("p n i -> p (n i)").bitcast(I32))
+        load_gates(LAST, 32 * KIB)
+        move_scale_rows(1)
 
-        gated = [sbuf([P, J + (QUARTER if n >= 2 else 0)], F32, f"gated{n}") for n in range(N_TILES)]
+        v_codes = {}
 
-        def gated_cols(n, lo, hi):
-            shift = SHIFT if n == 2 and lo >= HALF else 0
-            return gated[n][:, lo - shift : hi - shift]
+        def gather_words(i, lo, hi, tile):
+            v_codes[i, lo] = tile
+            nc.vector.tensor_copy(tile[:], tab[:].bitcast(U32).indirect(entries(i, lo, hi)))
 
-        def gather_gates(n, lo, hi):
-            offsets = src_list[:, lo // GROUP : hi // GROUP]
-            nc.vector.tensor_tensor(gated_cols(n, lo, hi), gates[n][:].indirect(offsets), edge_w[:, lo:hi], MULT)
+        def quantise_weight(i):
+            nc.vector.quantize_mx(out=w_codes[:, i, :].bitcast(FP8X4), scales=w_scales[:, i, :], in_=w_bf[i][:])
 
-        def gather_upper(k):
-            gather_gates(2, UPPER_STARTS[k], UPPER_STARTS[k + 1])
-
-        def gather_piece(k):
-            gather_gates(LAST, PIECE_STARTS[k], PIECE_STARTS[k + 1])
+        gather_words(0, 0, J, sbuf([P, J], U32, "v_src"))
+        quantise_weight(0)
+        gather_words(1, 0, Q, sbuf([P, Q], U32, "v_dst_first"))
+        quantise_weight(1)
+        gather_words(1, Q, J, at(40 * KIB, [P, J - Q], U32, "v_dst_rest"))
 
         def project(i, t, lo, hi, acc):
             rows = slice(t * P, (t + 1) * P)
+            start = max(s for j, s in v_codes if j == i and s <= lo)
+            plane = (lo // HALF) * J + i * HALF + lo % HALF
             nc.tensor.matmul_mx(
                 out=acc,
                 lhsT=w_codes[:, i, rows].bitcast(FP8X4),
                 lhsT_scale=w_scales[:, i, rows],
-                rhs=v_codes[i][:, lo:hi].bitcast(FP8X4),
-                rhs_scale=v_scales[:, i * J + lo : i * J + hi],
+                rhs=v_codes[i, start][:, lo - start : hi - start].bitcast(FP8X4),
+                rhs_scale=v_plane[:].bitcast(U8)[:, plane : plane + hi - lo],
                 start=(i == 0),
                 stop=(i == 1),
             )
 
-        def activate(lo, hi, banks, slot):
-            width = hi - lo
-            per_bank = PACK // len(banks)
-            act = sbuf([P, PACK, width], F32, f"act{lo}", slot)
-            for b, bank in enumerate(banks):
-                acc = psum.tile([P, per_bank, width], F32, name=f"acc{lo}_{b}", tag=f"bank{bank}")
-                for u in range(per_bank):
-                    for i in range(2):
-                        project(i, per_bank * b + u, lo, hi, acc[:, u, :])
-                nc.scalar.activation(act[:, per_bank * b : per_bank * (b + 1), :], acc[:], ACT.Silu)
-            return [act[:, t, :] for t in range(PACK)]
+        def sums(ts, lo, hi, b):
+            acc = bank(b, [P, len(ts), hi - lo], f"acc{lo}_{ts[0]}")
+            for u, t in enumerate(ts):
+                for i in range(2):
+                    project(i, t, lo, hi, acc[:, u, :])
+            return acc
 
-        def activate_first(hi):
-            act = sbuf([P, PACK, hi], F32, "act0", "act")
-            accs = [psum.tile([P, hi], F32, name=f"acc0_{t}", tag=f"bank{t}") for t in range(PACK)]
-            for t in range(PACK):
-                project(0, t, 0, hi, accs[t][:])
-            for t in range(PACK):
-                project(1, t, 0, hi, accs[t][:])
-                nc.scalar.activation(act[:, t, :], accs[t][:], ACT.Silu)
-            return [act[:, t, :] for t in range(PACK)]
+        def activate(acc, act, h_rows, ts):
+            nc.scalar.activation(act, acc[:], ACT.Silu)
+            for u, t in enumerate(ts):
+                scale(act[:, u, :], h_rows, t)
 
-        def scale(act, lo, hi):
-            h_rows = sbuf([P, PACK, hi - lo], BF16, f"h_rows{lo}")
-            for t in range(PACK):
-                nc.scalar.activation(h_rows[:, t, :], act[t], ACT.Copy, scale=sm_cols[:, t : t + 1])
-            return h_rows
+        def hidden(act, h_rows, ts, lo, hi, b):
+            activate(sums(ts, lo, hi, b), act[:, ts[0] : ts[-1] + 1, :], h_rows, ts)
 
-        def interleave(h_rows, lo, hi, slot=None):
-            width = hi - lo
-            h_bf = sbuf([P, width, PACK], BF16, f"h_bf{lo}", slot)
+        def scale(act_row, h_rows, t):
+            nc.scalar.activation(h_rows[:, t, :], act_row, ACT.Copy, scale=sm_cols[:, t : t + 1])
+
+        def interleave(h_rows, h_bf):
             nc.scalar.copy(
-                out=h_bf[:].rearrange("p (c i) t -> p c t i", i=4),
+                out=h_bf.rearrange("p (c i t) -> p c t i", i=4, t=PACK),
                 in_=h_rows[:].rearrange("p t (c i) -> p c t i", i=4),
             )
-            return h_bf
 
-        def quantise(h_bf, lo, hi, h_scales):
-            h_codes = sbuf([P, hi - lo], U32, f"h_codes{lo}")
-            nc.vector.quantize_mx(
-                out=h_codes[:].bitcast(FP8X4), scales=h_scales, in_=h_bf[:].rearrange("p c t -> p (c t)")
+        h = {}
+
+        def quantise(h_bf, lo, h_codes, h_scales):
+            nc.vector.quantize_mx(out=h_codes.bitcast(FP8X4), scales=h_scales, in_=h_bf)
+            h[lo] = h_codes, h_scales
+
+        msgs, gated = {}, {}
+
+        def message(n, lo, acc):
+            h_codes, h_scales = h[lo]
+            rows = slice(n * P, (n + 1) * P)
+            nc.tensor.matmul_mx(
+                out=acc,
+                lhsT=wd_codes[:, rows].bitcast(FP8X4),
+                lhsT_scale=wd_plane[:].bitcast(U8)[:, rows],
+                rhs=h_codes.bitcast(FP8X4),
+                rhs_scale=h_scales,
+                start=True,
+                stop=True,
             )
-            return h_codes[:], h_scales
 
-        def messages(parts, dest, bank):
-            width = parts[0][2] - parts[0][1]
-            acc = psum.tile([P, len(parts), width], F32, name=f"y_acc{parts[0][0]}_{parts[0][1]}", tag=f"bank{bank}")
-            for at, (n, lo, hi) in enumerate(parts):
-                start = max(s for s in h if s <= lo)
-                h_codes, h_scales = h[start]
-                rows = slice(n * P, (n + 1) * P)
-                nc.tensor.matmul_mx(
-                    out=acc[:, at, :],
-                    lhsT=wd_codes[:, rows].bitcast(FP8X4),
-                    lhsT_scale=wd_plane[:].bitcast(U8)[:, rows],
-                    rhs=h_codes[:, lo - start : hi - start].bitcast(FP8X4),
-                    rhs_scale=h_scales[:, lo - start : hi - start],
-                    start=True,
-                    stop=True,
-                )
-                msgs[n, lo] = dest[:, at * width : (at + 1) * width]
-            return lambda: nc.scalar.copy(out=dest, in_=acc[:].rearrange("p a w -> p (a w)"))
+        def empty(acc, dest):
+            nc.scalar.copy(out=dest, in_=acc[:].rearrange("p a w -> p (a w)"))
 
-        def scatter(n, lo, hi):
-            nc.vector.tensor_tensor(
-                outs[n][:].indirect(dst_list[:, lo // GROUP : hi // GROUP]), msgs[n, lo], gated_cols(n, lo, hi), MULT
-            )
-            if hi == J and n < LAST:
+        def messages(parts, dest, b):
+            acc = bank(b, [P, len(parts), Q], f"y_acc{parts[0][0]}_{parts[0][1]}")
+            for place, (n, lo) in enumerate(parts):
+                message(n, lo, acc[:, place, :])
+                msgs[n, lo] = dest[:, place * Q : (place + 1) * Q]
+            return lambda: empty(acc, dest)
+
+        def gather_gates(n, lo, hi, dest, factor=None):
+            factor = edge_w[:, lo:hi] if factor is None else factor
+            nc.vector.tensor_tensor(dest, gates[n][:].indirect(entries(0, lo, hi)), factor, MULT)
+
+        def scatter(n, lo, hi, a, b):
+            nc.vector.tensor_tensor(outs[n][:].indirect(entries(1, lo, hi)), a, b, MULT)
+            if hi == J and n != 2:
                 nc.sync.dma_start(out=out[n * P : (n + 1) * P, :], in_=outs[n][:])
             elif hi == J:
                 cut = 3 * T // 8
                 nc.sync.dma_start(out=out[n * P : (n + 1) * P, 0:cut], in_=outs[n][:, 0:cut])
                 nc.scalar.dma_start(out=out[n * P : (n + 1) * P, cut:T], in_=outs[n][:, cut:T])
 
-        q1, q2, q3 = QUARTER, 2 * QUARTER, 3 * QUARTER
-        h, msgs = {}, {}
+        q1, q2, q3 = Q, 2 * Q, 3 * Q
 
-        def ahead_of_piece(k):
-            return gated[LAST][:, PIECE_STARTS[k] : PIECE_STARTS[k] + HALF]
-
-        rest_scales = sbuf([P, J - q2], U8, "rest_scales")
-        zero_out(0, placed.tile([P, T], F32, name="out0", offset=14 * T))
-        gather_gates(0, 0, J)
-        gather_gates(1, 0, J)
-        gather_gates(2, 0, HALF)
-        h[0] = quantise(interleave(scale(activate_first(q1), 0, q1), 0, q1), 0, q1, wd_plane[:].bitcast(U8)[4:P, 0:q1])
-        gather_gates(LAST, 0, PIECE_STARTS[0])
-        h_rows_second = scale(activate(q1, q2, (4, 5), "act"), q1, q2)
-        first = gated_cols(2, UPPER_STARTS[1], UPPER_STARTS[1] + q1)
-        for lo, bank in ((0, 0), (P, 3)):
-            messages([(0, lo, lo + P)], first[:, lo : lo + P], bank)()
-        msgs[0, 0] = first
-        messages([(1, 0, q1)], sbuf([P, q1], F32, "msg_second")[:], 1)()
-        empty_pair = messages([(2, 0, q1), (LAST, 0, q1)], ahead_of_piece(0), 2)
-        h_bf_second = interleave(h_rows_second, q1, q2, "h_codes0")
-        scatter(0, 0, q1)
-        scatter(1, 0, q1)
-        gather_upper(1)
-        h[q1] = quantise(h_bf_second, q1, q2, wd_plane[:].bitcast(U8)[8:P, 0:q1])
-        act_all = sbuf([P, PACK, J - q2], F32, "act_rest", f"h_rows{q1}")
-        act_rest = [act_all[:, t, :] for t in range(PACK)]
-        for t, bank in enumerate((6, 7, 0, 1)):
-            acc = psum.tile([P, J - q2], F32, name=f"acc_rest{t}", tag=f"bank{bank}")
-            for i in range(2):
-                project(i, t, q2, J, acc[:])
-            nc.scalar.activation(act_rest[t], acc[:], ACT.Silu)
-            if t == 0:
-                empty_pair()
-        scatter(2, 0, q1)
-        scatter(LAST, 0, q1)
-        gather_piece(0)
-        messages([(0, q1, q2), (1, q1, q2)], gated_cols(2, UPPER_STARTS[2], UPPER_STARTS[2] + HALF), 3)()
-        h_bf_rest = interleave(scale(act_rest, q2, J), q2, J)
-        messages([(2, q1, q2), (LAST, q1, q2)], sbuf([P, HALF], F32, "msg_cover", f"h_rows{q2}")[:], 4)()
-        scatter(0, q1, q2)
-        scatter(1, q1, q2)
-        gather_upper(2)
-        h[q2] = quantise(h_bf_rest, q2, J, rest_scales[:])
-        scatter(2, q1, q2)
-        scatter(LAST, q1, q2)
-        gather_upper(0)
-        messages([(0, q3, J), (1, q3, J)], sbuf([P, HALF], F32, "msg_q3")[:], 5)()
-        messages([(0, q2, q3), (1, q2, q3)], ahead_of_piece(1), 6)()
-        for n, bank in ((2, 7), (LAST, 0)):
-            messages([(n, q2, J)], sbuf([P, HALF], F32, f"msg_half{n}")[:], bank)()
-        scatter(0, q2, q3)
-        for k, (n, lo) in enumerate(((1, q2), (0, q3), (1, q3))):
-            scatter(n, lo, lo + QUARTER)
-            gather_piece(1 + k)
+        gated0 = sbuf([P, J], F32, "gated0")
+        gather_gates(0, 0, J, gated0[:])
+        act0 = sbuf([P, PACK, Q], F32, "act0")
+        rows0 = sbuf([P, PACK, Q], BF16, "rows0", "rows0_act1")
+        accs = [bank(t, [P, Q], f"acc0_{t}") for t in range(PACK)]
+        for t in range(PACK):
+            project(0, t, 0, Q, accs[t][:])
+        for t in range(PACK):
+            project(1, t, 0, Q, accs[t][:])
+            nc.scalar.activation(act0[:, t, :], accs[t][:], ACT.Silu)
+        for t in range(PACK):
+            scale(act0[:, t, :], rows0, t)
+        h_bf0 = at(51 * KIB, [P, PACK * Q], BF16, "h_bf0")
+        interleave(rows0, h_bf0[:])
+        gated1 = sbuf([P, HALF], F32, "gated1")
+        gather_gates(1, q1, q3, gated1[:])
+        quantise(h_bf0[:], 0, sbuf([P, Q], U32, "h_codes0")[:], wd_plane[:].bitcast(U8)[4:P, 0:Q])
+        gated20 = sbuf([P, Q], F32, "gated20")
+        gather_gates(2, 0, q1, gated20[:])
+        upper2 = sbuf([P, 3 * Q], F32, "upper2")
+        gather_gates(2, q2, q3, upper2[:, 0:Q])
         for n in (2, LAST):
-            scatter(n, q2, J)
+            zero_out(n, at((44 + 8 * (n - 2)) * KIB, [P, T], F32, f"out{n}"))
+
+        act1 = sbuf([P, PACK, Q], F32, "act1", "rows0_act1")
+        rows1 = sbuf([P, PACK, Q], BF16, "rows1")
+        hidden(act1, rows1, (0,), q1, q2, 4)
+        messages([(0, 0)], sbuf([P, Q], F32, "msg00")[:], 5)()
+        messages([(1, 0), (2, 0)], upper2[:, Q : 3 * Q], 6)()
+        empty_last = messages([(LAST, 0)], at(61 * KIB + HALF, [P, Q], F32, "msg30")[:], 7)
+        scatter(0, 0, q1, msgs[0, 0], gated0[:, 0:q1])
+        product10 = sbuf([P, Q], F32, "product10")
+        gather_gates(1, 0, q1, product10[:], msgs[1, 0])
+        scatter(2, 0, q1, msgs[2, 0], gated20[:])
+        gather_gates(2, q3, J, upper2[:, Q:HALF])
+        scatter(1, 0, q1, product10[:], edge_w[:, 0:q1])
+        gated30 = sbuf([P, Q], F32, "gated30")
+        gather_gates(LAST, 0, q1, gated30[:])
+
+        hidden(act1, rows1, (1,), q1, q2, 5)
+        hidden(act1, rows1, (2, 3), q1, q2, 6)
+        h_bf1 = sbuf([P, PACK * Q], BF16, "h_bf1")
+        interleave(rows1, h_bf1[:])
+        empty_last()
+        quantise(h_bf1[:], q1, at(61 * KIB - HALF, [P, Q], U32, "h_codes1")[:], sbuf([P, Q], U8, "h_scales1")[:])
+        scatter(LAST, 0, q1, msgs[LAST, 0], gated30[:])
+        rows2 = at(66 * KIB, [P, PACK, Q], BF16, "rows2")
+        rows3 = at(72 * KIB, [P, PACK, Q], BF16, "rows3")
+        act2 = sbuf([P, PACK, Q], F32, "act2")
+        pairs = ((0, 1), (2, 3))
+        accs2 = [sums(ts, q2, q3, b) for b, ts in enumerate(pairs)]
+        accs3 = [sums(ts, q3, J, 2 + b) for b, ts in enumerate(pairs)]
+        for acc, ts in zip(accs2, pairs):
+            activate(acc, act2[:, ts[0] : ts[1] + 1, :], rows2, ts)
+        late = sbuf([P, HALF + 64 + Q], F32, "late", "act2")
+        first = HALF - 64
+        messages([(0, q1), (2, q1)], late[:, 0:HALF], 4)()
+        messages([(1, q1)], late[:, first + E : first + E + Q], 5)()
+        cover = bank(6, [P, 1, Q], "y_acc3_cover")
+        message(LAST, q1, cover[:, 0, :])
+        gated31 = at(61 * KIB - HALF, [P, Q], F32, "gated31")
+        gather_gates(LAST, q1, q2, gated31[:])
+        scatter(0, q1, q2, msgs[0, q1], gated0[:, q1:q2])
+        product21 = at(63 * KIB, [P, Q], F32, "product21")
+        gather_gates(2, q1, q2, product21[:], msgs[2, q1])
+        scatter(1, q1, q2, msgs[1, q1], gated1[:, 0:Q])
+        gather_gates(LAST, q3, q3 + E, late[:, first : first + E])
+        scatter(2, q1, q2, product21[:], edge_w[:, q1:q2])
+        gather_gates(LAST, q3 + E, J, late[:, first + E : first + Q])
+
+        h_bf2 = sbuf([P, PACK * Q], BF16, "h_bf2")
+        interleave(rows2, h_bf2[:])
+        msg31 = at(65 * KIB + HALF, [P, Q], F32, "msg31")
+        empty(cover, msg31[:])
+        quantise(h_bf2[:], q2, at(63 * KIB, [P, Q], U32, "h_codes2")[:], sbuf([P, Q], U8, "h_scales2")[:])
+        scatter(LAST, q1, q2, msg31[:], gated31[:])
+        act3 = at(67 * KIB, [P, PACK, Q], F32, "act3")
+        for acc, ts in zip(accs3, pairs):
+            activate(acc, act3[:, ts[0] : ts[1] + 1, :], rows3, ts)
+        h_bf3 = sbuf([P, PACK * Q], BF16, "h_bf3")
+        interleave(rows3, h_bf3[:])
+        messages([(0, q2), (LAST, q2)], at(71 * KIB, [P, HALF], F32, "msg02")[:], 7)()
+        empty_single = messages([(1, q2)], at(73 * KIB, [P, Q], F32, "msg12")[:], 4)
+        last_acc = bank(1, [P, 2, Q], "y_acc_last")
+        message(2, q2, last_acc[:, 0, :])
+        gated13 = at(63 * KIB, [P, Q], F32, "gated13")
+        gather_gates(1, q3, J, gated13[:])
+        empty_single()
+        quantise(h_bf3[:], q3, sbuf([P, Q], U32, "h_codes3")[:], sbuf([P, Q], U8, "h_scales3")[:])
+        scatter(0, q2, q3, msgs[0, q2], gated0[:, q2:q3])
+        product32 = sbuf([P, Q], F32, "product32")
+        gather_gates(LAST, q2, q3, product32[:], msgs[LAST, q2])
+
+        messages([(0, q3), (1, q3)], sbuf([P, HALF], F32, "msg03")[:], 5)()
+        messages([(LAST, q3)], sbuf([P, Q], F32, "msg33")[:], 0)()
+        message(2, q3, last_acc[:, 1, :])
+        msg22 = sbuf([P, HALF], F32, "msg22")
+        empty(last_acc, msg22[:])
+        scatter(1, q2, q3, msgs[1, q2], gated1[:, Q:HALF])
+        scatter(0, q3, J, msgs[0, q3], gated0[:, q3:J])
+        scatter(LAST, q2, q3, product32[:], edge_w[:, q2:q3])
+        scatter(1, q3, J, msgs[1, q3], gated13[:])
+        scatter(LAST, q3, J, msgs[LAST, q3], late[:, first : first + Q])
+        scatter(2, q2, J, msg22[:], upper2[:, 0:HALF])

@@ -61,6 +61,11 @@ def tile_list_msg_silu_gate_kernel(
         edge_cols = sbuf([P, J // P], F32, "edge_cols")
         nc.scalar.dma_start(out=edge_cols[:], in_=wgo[0].rearrange("(p c) -> p c", p=P))
 
+        warm_in = sbuf([P, 1], F32, "warm_in")
+        warm_out = sbuf([P, 1], F32, "warm_out")
+        nc.gpsimd.memset(warm_in[:], 0.0)
+        nc.scalar.activation(warm_out[:], warm_in[:], ACT.Silu)
+
         identity = sbuf([P, P], F32, "identity")
         v_plane = sbuf([P, 2 * J // 4], I32, "v_plane")
         nc.gpsimd.memset(tab_rows[0:ROW0, :], 0)

@@ -159,9 +159,8 @@ def tile_list_msg_silu_gate_kernel(
 
         gather_words(0, 0, J, sbuf([P, J], U32, "v_src"))
         quantise_weight(0)
-        gather_words(1, 0, Q, sbuf([P, Q], U32, "v_dst_first"))
+        gather_words(1, 0, HALF, sbuf([P, HALF], U32, "v_dst_first"))
         quantise_weight(1)
-        gather_words(1, Q, J, at(40 * KIB, [P, J - Q], U32, "v_dst_rest"))
 
         def project(i, t, lo, hi, acc):
             rows = slice(t * P, (t + 1) * P)
@@ -249,16 +248,17 @@ def tile_list_msg_silu_gate_kernel(
 
         gated0 = sbuf([P, J], F32, "gated0")
         gather_gates(0, 0, J, gated0[:])
-        act0 = sbuf([P, PACK, Q], F32, "act0")
+        act0 = [sbuf([P, Q], F32, f"act0_{t}") for t in range(PACK)]
         rows0 = sbuf([P, PACK, Q], BF16, "rows0", "rows0_act1")
         accs = [bank(t, [P, Q], f"acc0_{t}") for t in range(PACK)]
         for t in range(PACK):
             project(0, t, 0, Q, accs[t][:])
         for t in range(PACK):
             project(1, t, 0, Q, accs[t][:])
-            nc.scalar.activation(act0[:, t, :], accs[t][:], ACT.Silu)
+            nc.scalar.activation(act0[t][:], accs[t][:], ACT.Silu)
         for t in range(PACK):
-            scale(act0[:, t, :], rows0, t)
+            scale(act0[t][:], rows0, t)
+        gather_words(1, HALF, J, sbuf([P, HALF], U32, "v_dst_rest", "act0_0"))
         h_bf0 = at(51 * KIB, [P, PACK * Q], BF16, "h_bf0")
         interleave(rows0, h_bf0[:])
         gated1 = sbuf([P, HALF], F32, "gated1")
@@ -266,8 +266,8 @@ def tile_list_msg_silu_gate_kernel(
         quantise(h_bf0[:], 0, sbuf([P, Q], U32, "h_codes0")[:], wd_plane[:].bitcast(U8)[4:P, 0:Q])
         gated20 = sbuf([P, Q], F32, "gated20")
         gather_gates(2, 0, q1, gated20[:])
-        upper2 = sbuf([P, 3 * Q], F32, "upper2")
-        gather_gates(2, q2, q3, upper2[:, 0:Q])
+        upper2 = sbuf([P, 3 * Q + E], F32, "upper2")
+        gather_gates(2, q2, q3 + E, upper2[:, 0 : Q + E])
         for n in (2, LAST):
             zero_out(n, at((44 + 8 * (n - 2)) * KIB, [P, T], F32, f"out{n}"))
 
@@ -275,13 +275,13 @@ def tile_list_msg_silu_gate_kernel(
         rows1 = sbuf([P, PACK, Q], BF16, "rows1")
         hidden(act1, rows1, (0,), q1, q2, 4)
         messages([(0, 0)], sbuf([P, Q], F32, "msg00")[:], 5)()
-        messages([(1, 0), (2, 0)], upper2[:, Q : 3 * Q], 6)()
+        messages([(1, 0), (2, 0)], upper2[:, Q + E : 3 * Q + E], 6)()
         empty_last = messages([(LAST, 0)], at(61 * KIB + HALF, [P, Q], F32, "msg30")[:], 7)
         scatter(0, 0, q1, msgs[0, 0], gated0[:, 0:q1])
         product10 = sbuf([P, Q], F32, "product10")
         gather_gates(1, 0, q1, product10[:], msgs[1, 0])
         scatter(2, 0, q1, msgs[2, 0], gated20[:])
-        gather_gates(2, q3, J, upper2[:, Q:HALF])
+        gather_gates(2, q3 + E, J, upper2[:, Q + E : HALF])
         scatter(1, 0, q1, product10[:], edge_w[:, 0:q1])
         gated30 = sbuf([P, Q], F32, "gated30")
         gather_gates(LAST, 0, q1, gated30[:])
@@ -295,19 +295,19 @@ def tile_list_msg_silu_gate_kernel(
         scatter(LAST, 0, q1, msgs[LAST, 0], gated30[:])
         rows2 = at(66 * KIB, [P, PACK, Q], BF16, "rows2")
         rows3 = at(72 * KIB, [P, PACK, Q], BF16, "rows3")
-        act2 = sbuf([P, PACK, Q], F32, "act2")
+        act2 = [sbuf([P, 2, Q], F32, f"act2_{b}") for b in range(2)]
         pairs = ((0, 1), (2, 3))
         accs2 = [sums(ts, q2, q3, b) for b, ts in enumerate(pairs)]
         accs3 = [sums(ts, q3, J, 2 + b) for b, ts in enumerate(pairs)]
-        for acc, ts in zip(accs2, pairs):
-            activate(acc, act2[:, ts[0] : ts[1] + 1, :], rows2, ts)
-        late = sbuf([P, HALF + 64 + Q], F32, "late", "act2")
-        first = HALF - 64
-        messages([(0, q1), (2, q1)], late[:, 0:HALF], 4)()
-        messages([(1, q1)], late[:, first + E : first + E + Q], 5)()
+        for acc, act, ts in zip(accs2, act2, pairs):
+            activate(acc, act[:], rows2, ts)
+        late = sbuf([P, 3 * Q], F32, "late", "act2_1")
+        first = HALF - E
+        messages([(0, q1)], late[:, 0:Q], 4)()
+        messages([(2, q1), (1, q1)], late[:, Q : 3 * Q], 5)()
         cover = bank(6, [P, 1, Q], "y_acc3_cover")
         message(LAST, q1, cover[:, 0, :])
-        gated31 = at(61 * KIB - HALF, [P, Q], F32, "gated31")
+        gated31 = sbuf([P, Q], F32, "gated31", "act2_0")
         gather_gates(LAST, q1, q2, gated31[:])
         scatter(0, q1, q2, msgs[0, q1], gated0[:, q1:q2])
         product21 = at(63 * KIB, [P, Q], F32, "product21")
@@ -319,22 +319,21 @@ def tile_list_msg_silu_gate_kernel(
 
         h_bf2 = sbuf([P, PACK * Q], BF16, "h_bf2")
         interleave(rows2, h_bf2[:])
-        msg31 = at(65 * KIB + HALF, [P, Q], F32, "msg31")
+        msg31 = at(66 * KIB + 64, [P, Q], F32, "msg31")
         empty(cover, msg31[:])
         quantise(h_bf2[:], q2, at(63 * KIB, [P, Q], U32, "h_codes2")[:], sbuf([P, Q], U8, "h_scales2")[:])
         scatter(LAST, q1, q2, msg31[:], gated31[:])
-        act3 = at(67 * KIB, [P, PACK, Q], F32, "act3")
-        for acc, ts in zip(accs3, pairs):
-            activate(acc, act3[:, ts[0] : ts[1] + 1, :], rows3, ts)
+        act3 = [at(67 * KIB + 64, [P, 2, Q], F32, "act3_0"), at(64 * KIB + 64, [P, 2, Q], F32, "act3_1")]
+        for acc, act, ts in zip(accs3, act3, pairs):
+            activate(acc, act[:], rows3, ts)
         h_bf3 = sbuf([P, PACK * Q], BF16, "h_bf3")
         interleave(rows3, h_bf3[:])
-        messages([(0, q2), (LAST, q2)], at(71 * KIB, [P, HALF], F32, "msg02")[:], 7)()
-        empty_single = messages([(1, q2)], at(73 * KIB, [P, Q], F32, "msg12")[:], 4)
+        messages([(0, q2)], at(71 * KIB + HALF, [P, Q], F32, "msg02")[:], 7)()
+        messages([(LAST, q2), (1, q2)], at(73 * KIB, [P, HALF], F32, "msg12")[:], 4)()
         last_acc = bank(1, [P, 2, Q], "y_acc_last")
         message(2, q2, last_acc[:, 0, :])
-        gated13 = at(63 * KIB, [P, Q], F32, "gated13")
+        gated13 = at(68 * KIB, [P, Q], F32, "gated13")
         gather_gates(1, q3, J, gated13[:])
-        empty_single()
         quantise(h_bf3[:], q3, sbuf([P, Q], U32, "h_codes3")[:], sbuf([P, Q], U8, "h_scales3")[:])
         scatter(0, q2, q3, msgs[0, q2], gated0[:, q2:q3])
         product32 = sbuf([P, Q], F32, "product32")

@@ -93,19 +93,25 @@ def tile_list_msg_silu_gate_kernel(
         sm_cols = sbuf([P, PACK], F32, "sm_cols")
         nc.sync.dma_start(out=sm_cols[:], in_=sm.rearrange("(p t) -> p t", t=PACK))
 
-        picked = [sbuf([P, J], U8, "picked0"), at(61 * KIB, [P, J], U8, "picked1")]
-        for half in range(2):
+        picked = {
+            0: sbuf([P, 2 * Q], U8, "picked0"),
+            HALF: at(61 * KIB, [P, 2 * HALF], U8, "picked2"),
+            Q: sbuf([P, 2 * Q], U8, "picked1"),
+        }
+        for lo, tile in picked.items():
+            width = tile.shape[1] // 2
             for i in range(2):
                 nc.vector.tensor_copy(
-                    picked[half][:, i * HALF : (i + 1) * HALF],
-                    tab_rows[:].bitcast(U8).indirect(entries(i, half * HALF, (half + 1) * HALF)),
+                    tile[:, i * width : (i + 1) * width],
+                    tab_rows[:].bitcast(U8).indirect(entries(i, lo, lo + width)),
                 )
 
-        def move_scale_rows(half):
+        def move_scale_rows(lo):
+            words = slice(2 * lo // 4, (2 * lo + picked[lo].shape[1]) // 4)
             for q in range(4):
                 nc.sync.dma_start(
-                    out=v_plane[32 * q : 32 * q + 4, half * Q : (half + 1) * Q],
-                    in_=picked[half][ROW0 + 4 * q : ROW0 + 4 * q + 4, :].bitcast(I32),
+                    out=v_plane[32 * q : 32 * q + 4, words],
+                    in_=picked[lo][ROW0 + 4 * q : ROW0 + 4 * q + 4, :].bitcast(I32),
                 )
 
         move_scale_rows(0)
@@ -115,8 +121,9 @@ def tile_list_msg_silu_gate_kernel(
             gates[n] = at(offset, [P, T], F32, f"gates{n}")
             nc.sync.dma_start(out=gates[n][:], in_=gT[n * P : (n + 1) * P, :])
 
-        for n in range(2):
-            load_gates(n, n * 8 * KIB)
+        load_gates(0, 0)
+        move_scale_rows(Q)
+        load_gates(1, 8 * KIB)
 
         edge_w = sbuf([P, J], F32, "edge_w")
         edge_view = edge_w[:].rearrange("p (m b c) -> p b m c", b=2, c=4)
@@ -146,7 +153,7 @@ def tile_list_msg_silu_gate_kernel(
                 in_=wt_raw[u][:].rearrange("p i (m t) -> p m i t", t=PACK),
             )
         load_gates(LAST, 32 * KIB)
-        move_scale_rows(1)
+        move_scale_rows(HALF)
 
         v_codes = {}
 
@@ -165,7 +172,8 @@ def tile_list_msg_silu_gate_kernel(
         def project(i, t, lo, hi, acc):
             rows = slice(t * P, (t + 1) * P)
             start = max(s for j, s in v_codes if j == i and s <= lo)
-            plane = (lo // HALF) * J + i * HALF + lo % HALF
+            group = max(s for s in picked if s <= lo)
+            plane = 2 * group + i * picked[group].shape[1] // 2 + lo - group
             nc.tensor.matmul_mx(
                 out=acc,
                 lhsT=w_codes[:, i, rows].bitcast(FP8X4),
@@ -187,9 +195,6 @@ def tile_list_msg_silu_gate_kernel(
             nc.scalar.activation(act, acc[:], ACT.Silu)
             for u, t in enumerate(ts):
                 scale(act[:, u, :], h_rows, t)
-
-        def hidden(act, h_rows, ts, lo, hi, b):
-            activate(sums(ts, lo, hi, b), act[:, ts[0] : ts[-1] + 1, :], h_rows, ts)
 
         def scale(act_row, h_rows, t):
             nc.scalar.activation(h_rows[:, t, :], act_row, ACT.Copy, scale=sm_cols[:, t : t + 1])
@@ -256,13 +261,14 @@ def tile_list_msg_silu_gate_kernel(
         for t in range(PACK):
             project(1, t, 0, Q, accs[t][:])
             nc.scalar.activation(act0[t][:], accs[t][:], ACT.Silu)
-        for t in range(PACK):
-            scale(act0[t][:], rows0, t)
-        gather_words(1, HALF, J, sbuf([P, HALF], U32, "v_dst_rest", "act0_0"))
+            if t > 0:
+                scale(act0[t - 1][:], rows0, t - 1)
+        scale(act0[LAST][:], rows0, LAST)
+        gather_words(1, HALF, J, sbuf([P, HALF], U32, "v_dst_rest", "picked1"))
         h_bf0 = at(51 * KIB, [P, PACK * Q], BF16, "h_bf0")
         interleave(rows0, h_bf0[:])
-        gated1 = sbuf([P, HALF], F32, "gated1")
-        gather_gates(1, q1, q3, gated1[:])
+        gated1 = sbuf([P, 3 * Q], F32, "gated1")
+        gather_gates(1, q1, J, gated1[:])
         quantise(h_bf0[:], 0, sbuf([P, Q], U32, "h_codes0")[:], wd_plane[:].bitcast(U8)[4:P, 0:Q])
         gated20 = sbuf([P, Q], F32, "gated20")
         gather_gates(2, 0, q1, gated20[:])
@@ -271,12 +277,13 @@ def tile_list_msg_silu_gate_kernel(
         for n in (2, LAST):
             zero_out(n, at((44 + 8 * (n - 2)) * KIB, [P, T], F32, f"out{n}"))
 
-        act1 = sbuf([P, PACK, Q], F32, "act1", "rows0_act1")
+        pairs = ((0, 1), (2, 3))
+        accs1 = [sums(ts, q1, q2, b) for b, ts in enumerate(pairs)]
         rows1 = sbuf([P, PACK, Q], BF16, "rows1")
-        hidden(act1, rows1, (0,), q1, q2, 4)
-        messages([(0, 0)], sbuf([P, Q], F32, "msg00")[:], 5)()
-        messages([(1, 0), (2, 0)], upper2[:, Q + E : 3 * Q + E], 6)()
-        empty_last = messages([(LAST, 0)], at(61 * KIB + HALF, [P, Q], F32, "msg30")[:], 7)
+        activate(accs1[0], sbuf([P, 2, Q], F32, "act1_0", "rows0_act1")[:], rows1, pairs[0])
+        messages([(0, 0)], sbuf([P, Q], F32, "msg00")[:], 4)()
+        messages([(1, 0), (2, 0)], upper2[:, Q + E : 3 * Q + E], 5)()
+        empty_last = messages([(LAST, 0)], at(61 * KIB + HALF, [P, Q], F32, "msg30")[:], 6)
         scatter(0, 0, q1, msgs[0, 0], gated0[:, 0:q1])
         product10 = sbuf([P, Q], F32, "product10")
         gather_gates(1, 0, q1, product10[:], msgs[1, 0])
@@ -286,8 +293,7 @@ def tile_list_msg_silu_gate_kernel(
         gated30 = sbuf([P, Q], F32, "gated30")
         gather_gates(LAST, 0, q1, gated30[:])
 
-        hidden(act1, rows1, (1,), q1, q2, 5)
-        hidden(act1, rows1, (2, 3), q1, q2, 6)
+        activate(accs1[1], sbuf([P, 2, Q], F32, "act1_1", "h_codes0")[:], rows1, pairs[1])
         h_bf1 = sbuf([P, PACK * Q], BF16, "h_bf1")
         interleave(rows1, h_bf1[:])
         empty_last()
@@ -296,16 +302,15 @@ def tile_list_msg_silu_gate_kernel(
         rows2 = at(66 * KIB, [P, PACK, Q], BF16, "rows2")
         rows3 = at(72 * KIB, [P, PACK, Q], BF16, "rows3")
         act2 = [sbuf([P, 2, Q], F32, f"act2_{b}") for b in range(2)]
-        pairs = ((0, 1), (2, 3))
-        accs2 = [sums(ts, q2, q3, b) for b, ts in enumerate(pairs)]
-        accs3 = [sums(ts, q3, J, 2 + b) for b, ts in enumerate(pairs)]
+        accs2 = [sums(ts, q2, q3, 2 + b) for b, ts in enumerate(pairs)]
+        accs3 = [sums(ts, q3, J, b) for b, ts in enumerate(pairs)]
         for acc, act, ts in zip(accs2, act2, pairs):
             activate(acc, act[:], rows2, ts)
         late = sbuf([P, 3 * Q], F32, "late", "act2_1")
         first = HALF - E
-        messages([(0, q1)], late[:, 0:Q], 4)()
-        messages([(2, q1), (1, q1)], late[:, Q : 3 * Q], 5)()
-        cover = bank(6, [P, 1, Q], "y_acc3_cover")
+        messages([(0, q1)], late[:, 0:Q], 7)()
+        messages([(2, q1), (1, q1)], late[:, Q : 3 * Q], 4)()
+        cover = bank(5, [P, 1, Q], "y_acc3_cover")
         message(LAST, q1, cover[:, 0, :])
         gated31 = sbuf([P, Q], F32, "gated31", "act2_0")
         gather_gates(LAST, q1, q2, gated31[:])
@@ -329,24 +334,22 @@ def tile_list_msg_silu_gate_kernel(
         h_bf3 = sbuf([P, PACK * Q], BF16, "h_bf3")
         interleave(rows3, h_bf3[:])
         messages([(0, q2)], at(71 * KIB + HALF, [P, Q], F32, "msg02")[:], 7)()
-        messages([(LAST, q2), (1, q2)], at(73 * KIB, [P, HALF], F32, "msg12")[:], 4)()
-        last_acc = bank(1, [P, 2, Q], "y_acc_last")
+        messages([(LAST, q2), (1, q2)], at(73 * KIB, [P, HALF], F32, "msg12")[:], 6)()
+        last_acc = bank(2, [P, 2, Q], "y_acc_last")
         message(2, q2, last_acc[:, 0, :])
-        gated13 = at(68 * KIB, [P, Q], F32, "gated13")
-        gather_gates(1, q3, J, gated13[:])
+        gated32 = at(68 * KIB, [P, Q], F32, "gated32")
+        gather_gates(LAST, q2, q3, gated32[:])
         quantise(h_bf3[:], q3, sbuf([P, Q], U32, "h_codes3")[:], sbuf([P, Q], U8, "h_scales3")[:])
         scatter(0, q2, q3, msgs[0, q2], gated0[:, q2:q3])
-        product32 = sbuf([P, Q], F32, "product32")
-        gather_gates(LAST, q2, q3, product32[:], msgs[LAST, q2])
 
-        messages([(0, q3), (1, q3)], sbuf([P, HALF], F32, "msg03")[:], 5)()
-        messages([(LAST, q3)], sbuf([P, Q], F32, "msg33")[:], 0)()
+        messages([(0, q3), (1, q3)], sbuf([P, HALF], F32, "msg03")[:], 4)()
+        messages([(LAST, q3)], sbuf([P, Q], F32, "msg33")[:], 3)()
         message(2, q3, last_acc[:, 1, :])
         msg22 = sbuf([P, HALF], F32, "msg22")
         empty(last_acc, msg22[:])
         scatter(1, q2, q3, msgs[1, q2], gated1[:, Q:HALF])
         scatter(0, q3, J, msgs[0, q3], gated0[:, q3:J])
-        scatter(LAST, q2, q3, product32[:], edge_w[:, q2:q3])
-        scatter(1, q3, J, msgs[1, q3], gated13[:])
+        scatter(LAST, q2, q3, msgs[LAST, q2], gated32[:])
+        scatter(1, q3, J, msgs[1, q3], gated1[:, HALF : 3 * Q])
         scatter(LAST, q3, J, msgs[LAST, q3], late[:, first : first + Q])
         scatter(2, q2, J, msg22[:], upper2[:, 0:HALF])

@@ -125,20 +125,23 @@ def tile_list_msg_silu_gate_kernel(
         move_scale_rows(Q)
         load_gates(1, 8 * KIB)
 
-        edge_w = sbuf([P, J], F32, "edge_w")
+        edge_w = at(19 * KIB, [P, J], F32, "edge_w")
         edge_view = edge_w[:].rearrange("p (m b c) -> p b m c", b=2, c=4)
+        spreads = []
         for b in range(2):
             spread = bank(6 + b, [P, 4, P], f"spread{b}")
             for c in range(4):
                 column = edge_cols[:, 4 * b + c : 4 * b + c + 1].to_broadcast([P, P])
                 nc.tensor.transpose(spread[:, c, :], column, identity[:])
-            nc.scalar.copy(out=edge_view[:, b], in_=spread[:].rearrange("p c m -> p m c"))
+            spreads.append(spread)
 
         w_bf = [sbuf([P, PACK * R], BF16, "w_bf0"), at(40 * KIB, [P, PACK * R], BF16, "w_bf1")]
         w_codes = sbuf([P, 2, R], U32, "w_codes")
         w_scales = sbuf([P, 2, R], U8, "w_scales")
         w_view = [w_bf[i][:].rearrange("p (t m i) -> p m i t", t=PACK, i=PACK) for i in range(2)]
         nc.scalar.copy(out=w_view[0], in_=ws_raw[:].rearrange("p i (m t) -> p m i t", t=PACK))
+        for b, spread in enumerate(spreads):
+            nc.scalar.copy(out=edge_view[:, b], in_=spread[:].rearrange("p c m -> p m c"))
         wd_plane = at(16 * KIB, [P, N // 4], I32, "wd_plane")
         nc.gpsimd.memset(wd_plane[:], 0)
         by_place = wd_scales[0].bitcast(I32).rearrange("(q r) w -> r q w", r=4)
@@ -269,7 +272,7 @@ def tile_list_msg_silu_gate_kernel(
         interleave(rows0, h_bf0[:])
         gated1 = sbuf([P, 3 * Q], F32, "gated1")
         gather_gates(1, q1, J, gated1[:])
-        quantise(h_bf0[:], 0, sbuf([P, Q], U32, "h_codes0")[:], wd_plane[:].bitcast(U8)[4:P, 0:Q])
+        quantise(h_bf0[:], 0, at(80 * KIB, [P, Q], U32, "h_codes0")[:], wd_plane[:].bitcast(U8)[4:P, 0:Q])
         gated20 = sbuf([P, Q], F32, "gated20")
         gather_gates(2, 0, q1, gated20[:])
         upper2 = sbuf([P, 3 * Q + E], F32, "upper2")
@@ -279,8 +282,8 @@ def tile_list_msg_silu_gate_kernel(
 
         pairs = ((0, 1), (2, 3))
         accs1 = [sums(ts, q1, q2, b) for b, ts in enumerate(pairs)]
-        rows1 = sbuf([P, PACK, Q], BF16, "rows1")
-        activate(accs1[0], sbuf([P, 2, Q], F32, "act1_0", "rows0_act1")[:], rows1, pairs[0])
+        act1 = [sbuf([P, 2, Q], F32, "act1_0", "rows0_act1"), at(80 * KIB + HALF, [P, 2, Q], F32, "act1_1")]
+        nc.scalar.activation(act1[0][:], accs1[0][:], ACT.Silu)
         messages([(0, 0)], sbuf([P, Q], F32, "msg00")[:], 4)()
         messages([(1, 0), (2, 0)], upper2[:, Q + E : 3 * Q + E], 5)()
         empty_last = messages([(LAST, 0)], at(61 * KIB + HALF, [P, Q], F32, "msg30")[:], 6)
@@ -293,7 +296,10 @@ def tile_list_msg_silu_gate_kernel(
         gated30 = sbuf([P, Q], F32, "gated30")
         gather_gates(LAST, 0, q1, gated30[:])
 
-        activate(accs1[1], sbuf([P, 2, Q], F32, "act1_1", "h_codes0")[:], rows1, pairs[1])
+        rows1 = at(78 * KIB + HALF, [P, PACK, Q], BF16, "rows1")
+        for t in pairs[0]:
+            scale(act1[0][:, t, :], rows1, t)
+        activate(accs1[1], act1[1][:], rows1, pairs[1])
         h_bf1 = sbuf([P, PACK * Q], BF16, "h_bf1")
         interleave(rows1, h_bf1[:])
         empty_last()
@@ -307,7 +313,6 @@ def tile_list_msg_silu_gate_kernel(
         for acc, act, ts in zip(accs2, act2, pairs):
             activate(acc, act[:], rows2, ts)
         late = sbuf([P, 3 * Q], F32, "late", "act2_1")
-        first = HALF - E
         messages([(0, q1)], late[:, 0:Q], 7)()
         messages([(2, q1), (1, q1)], late[:, Q : 3 * Q], 4)()
         cover = bank(5, [P, 1, Q], "y_acc3_cover")
@@ -318,9 +323,8 @@ def tile_list_msg_silu_gate_kernel(
         product21 = at(63 * KIB, [P, Q], F32, "product21")
         gather_gates(2, q1, q2, product21[:], msgs[2, q1])
         scatter(1, q1, q2, msgs[1, q1], gated1[:, 0:Q])
-        gather_gates(LAST, q3, q3 + E, late[:, first : first + E])
         scatter(2, q1, q2, product21[:], edge_w[:, q1:q2])
-        gather_gates(LAST, q3 + E, J, late[:, first + E : first + Q])
+        gather_gates(LAST, q3, J, late[:, HALF : 3 * Q])
 
         h_bf2 = sbuf([P, PACK * Q], BF16, "h_bf2")
         interleave(rows2, h_bf2[:])
@@ -351,5 +355,5 @@ def tile_list_msg_silu_gate_kernel(
         scatter(0, q3, J, msgs[0, q3], gated0[:, q3:J])
         scatter(LAST, q2, q3, msgs[LAST, q2], gated32[:])
         scatter(1, q3, J, msgs[1, q3], gated1[:, HALF : 3 * Q])
-        scatter(LAST, q3, J, msgs[LAST, q3], late[:, first : first + Q])
+        scatter(LAST, q3, J, msgs[LAST, q3], late[:, HALF : 3 * Q])
         scatter(2, q2, J, msg22[:], upper2[:, 0:HALF])

@@ -125,37 +125,34 @@ def tile_list_msg_silu_gate_kernel(
         move_scale_rows(Q)
         load_gates(1, 8 * KIB)
 
-        edge_w = at(19 * KIB, [P, J], F32, "edge_w")
+        edge_w = sbuf([P, J], F32, "edge_w")
         edge_view = edge_w[:].rearrange("p (m b c) -> p b m c", b=2, c=4)
-        spreads = []
         for b in range(2):
             spread = bank(6 + b, [P, 4, P], f"spread{b}")
             for c in range(4):
                 column = edge_cols[:, 4 * b + c : 4 * b + c + 1].to_broadcast([P, P])
                 nc.tensor.transpose(spread[:, c, :], column, identity[:])
-            spreads.append(spread)
+            nc.scalar.copy(out=edge_view[:, b], in_=spread[:].rearrange("p c m -> p m c"))
 
-        w_bf = [sbuf([P, PACK * R], BF16, "w_bf0"), at(40 * KIB, [P, PACK * R], BF16, "w_bf1")]
+        w_bf = [sbuf([P, PACK * R], BF16, "w_bf0"), sbuf([P, PACK * R], BF16, "w_bf1")]
         w_codes = sbuf([P, 2, R], U32, "w_codes")
         w_scales = sbuf([P, 2, R], U8, "w_scales")
         w_view = [w_bf[i][:].rearrange("p (t m i) -> p m i t", t=PACK, i=PACK) for i in range(2)]
         nc.scalar.copy(out=w_view[0], in_=ws_raw[:].rearrange("p i (m t) -> p m i t", t=PACK))
-        for b, spread in enumerate(spreads):
-            nc.scalar.copy(out=edge_view[:, b], in_=spread[:].rearrange("p c m -> p m c"))
-        wd_plane = at(16 * KIB, [P, N // 4], I32, "wd_plane")
-        nc.gpsimd.memset(wd_plane[:], 0)
-        by_place = wd_scales[0].bitcast(I32).rearrange("(q r) w -> r q w", r=4)
-        for r in range(4):
-            nc.sync.dma_start(out=wd_plane[r:P:32, :], in_=by_place[r])
-        load_gates(2, 24 * KIB - 64)
-        wd_codes = at(16 * KIB + N, [P, N], I32, "wd_codes")
-        nc.sync.dma_start(out=wd_codes[:], in_=wd_words[0].rearrange("p n i -> p (n i)").bitcast(I32))
         for u in range(2):
             nc.scalar.copy(
                 out=w_view[1][:, u * P // 2 : (u + 1) * P // 2],
                 in_=wt_raw[u][:].rearrange("p i (m t) -> p m i t", t=PACK),
             )
-        load_gates(LAST, 32 * KIB)
+        wd_plane = at(32 * KIB, [P, N // 4], I32, "wd_plane")
+        nc.gpsimd.memset(wd_plane[:], 0)
+        by_place = wd_scales[0].bitcast(I32).rearrange("(q r) w -> r q w", r=4)
+        for r in range(4):
+            nc.sync.dma_start(out=wd_plane[r:P:32, :], in_=by_place[r])
+        load_gates(2, 24 * KIB - 64)
+        wd_codes = at(16 * KIB, [P, N], I32, "wd_codes")
+        nc.sync.dma_start(out=wd_codes[:], in_=wd_words[0].rearrange("p n i -> p (n i)").bitcast(I32))
+        load_gates(LAST, 32 * KIB + N)
         move_scale_rows(HALF)
 
         v_codes = {}
@@ -164,13 +161,18 @@ def tile_list_msg_silu_gate_kernel(
             v_codes[i, lo] = tile
             nc.vector.tensor_copy(tile[:], tab[:].bitcast(U32).indirect(entries(i, lo, hi)))
 
-        def quantise_weight(i):
-            nc.vector.quantize_mx(out=w_codes[:, i, :].bitcast(FP8X4), scales=w_scales[:, i, :], in_=w_bf[i][:])
+        def quantise_weight(i, lo, hi):
+            nc.vector.quantize_mx(
+                out=w_codes[:, i, lo:hi].bitcast(FP8X4),
+                scales=w_scales[:, i, lo:hi],
+                in_=w_bf[i][:, PACK * lo : PACK * hi],
+            )
 
         gather_words(0, 0, J, sbuf([P, J], U32, "v_src"))
-        quantise_weight(0)
+        quantise_weight(0, 0, R)
         gather_words(1, 0, HALF, sbuf([P, HALF], U32, "v_dst_first"))
-        quantise_weight(1)
+        for lo, hi in ((0, P), (P, 2 * P), (2 * P, R)):
+            quantise_weight(1, lo, hi)
 
         def project(i, t, lo, hi, acc):
             rows = slice(t * P, (t + 1) * P)
@@ -270,13 +272,13 @@ def tile_list_msg_silu_gate_kernel(
         gather_words(1, HALF, J, sbuf([P, HALF], U32, "v_dst_rest", "picked1"))
         h_bf0 = at(51 * KIB, [P, PACK * Q], BF16, "h_bf0")
         interleave(rows0, h_bf0[:])
-        gated1 = sbuf([P, 3 * Q], F32, "gated1")
-        gather_gates(1, q1, J, gated1[:])
+        gated1 = sbuf([P, HALF], F32, "gated1")
+        gather_gates(1, q1, q3, gated1[:])
         quantise(h_bf0[:], 0, at(80 * KIB, [P, Q], U32, "h_codes0")[:], wd_plane[:].bitcast(U8)[4:P, 0:Q])
         gated20 = sbuf([P, Q], F32, "gated20")
         gather_gates(2, 0, q1, gated20[:])
-        upper2 = sbuf([P, 3 * Q + E], F32, "upper2")
-        gather_gates(2, q2, q3 + E, upper2[:, 0 : Q + E])
+        upper2 = sbuf([P, 3 * Q], F32, "upper2")
+        gather_gates(2, q2, q3, upper2[:, 0:Q])
         for n in (2, LAST):
             zero_out(n, at((44 + 8 * (n - 2)) * KIB, [P, T], F32, f"out{n}"))
 
@@ -285,13 +287,13 @@ def tile_list_msg_silu_gate_kernel(
         act1 = [sbuf([P, 2, Q], F32, "act1_0", "rows0_act1"), at(80 * KIB + HALF, [P, 2, Q], F32, "act1_1")]
         nc.scalar.activation(act1[0][:], accs1[0][:], ACT.Silu)
         messages([(0, 0)], sbuf([P, Q], F32, "msg00")[:], 4)()
-        messages([(1, 0), (2, 0)], upper2[:, Q + E : 3 * Q + E], 5)()
+        messages([(1, 0), (2, 0)], upper2[:, Q : 3 * Q], 5)()
         empty_last = messages([(LAST, 0)], at(61 * KIB + HALF, [P, Q], F32, "msg30")[:], 6)
         scatter(0, 0, q1, msgs[0, 0], gated0[:, 0:q1])
         product10 = sbuf([P, Q], F32, "product10")
         gather_gates(1, 0, q1, product10[:], msgs[1, 0])
         scatter(2, 0, q1, msgs[2, 0], gated20[:])
-        gather_gates(2, q3 + E, J, upper2[:, Q + E : HALF])
+        gather_gates(2, q3, J, upper2[:, Q:HALF])
         scatter(1, 0, q1, product10[:], edge_w[:, 0:q1])
         gated30 = sbuf([P, Q], F32, "gated30")
         gather_gates(LAST, 0, q1, gated30[:])
@@ -323,6 +325,7 @@ def tile_list_msg_silu_gate_kernel(
         product21 = at(63 * KIB, [P, Q], F32, "product21")
         gather_gates(2, q1, q2, product21[:], msgs[2, q1])
         scatter(1, q1, q2, msgs[1, q1], gated1[:, 0:Q])
+        gather_gates(1, q3, J, late[:, Q:HALF])
         scatter(2, q1, q2, product21[:], edge_w[:, q1:q2])
         gather_gates(LAST, q3, J, late[:, HALF : 3 * Q])
 
@@ -354,6 +357,6 @@ def tile_list_msg_silu_gate_kernel(
         scatter(1, q2, q3, msgs[1, q2], gated1[:, Q:HALF])
         scatter(0, q3, J, msgs[0, q3], gated0[:, q3:J])
         scatter(LAST, q2, q3, msgs[LAST, q2], gated32[:])
-        scatter(1, q3, J, msgs[1, q3], gated1[:, HALF : 3 * Q])
+        scatter(1, q3, J, msgs[1, q3], late[:, Q:HALF])
         scatter(LAST, q3, J, msgs[LAST, q3], late[:, HALF : 3 * Q])
         scatter(2, q2, J, msg22[:], upper2[:, 0:HALF])

@@ -138,12 +138,17 @@ def tile_list_msg_silu_gate_kernel(
         w_codes = sbuf([P, 2, R], U32, "w_codes")
         w_scales = sbuf([P, 2, R], U8, "w_scales")
         w_view = [w_bf[i][:].rearrange("p (t m i) -> p m i t", t=PACK, i=PACK) for i in range(2)]
-        nc.scalar.copy(out=w_view[0], in_=ws_raw[:].rearrange("p i (m t) -> p m i t", t=PACK))
-        for u in range(2):
+        slot_pairs = (slice(0, 2), slice(2, PACK))
+        for ts in slot_pairs:
             nc.scalar.copy(
-                out=w_view[1][:, u * P // 2 : (u + 1) * P // 2],
-                in_=wt_raw[u][:].rearrange("p i (m t) -> p m i t", t=PACK),
+                out=w_view[0][:, :, :, ts], in_=ws_raw[:].rearrange("p i (m t) -> p m i t", t=PACK)[:, :, :, ts]
             )
+        for u in range(2):
+            for ts in slot_pairs:
+                nc.scalar.copy(
+                    out=w_view[1][:, u * P // 2 : (u + 1) * P // 2, :, ts],
+                    in_=wt_raw[u][:].rearrange("p i (m t) -> p m i t", t=PACK)[:, :, :, ts],
+                )
         wd_plane = at(32 * KIB, [P, N // 4], I32, "wd_plane")
         nc.gpsimd.memset(wd_plane[:], 0)
         by_place = wd_scales[0].bitcast(I32).rearrange("(q r) w -> r q w", r=4)
@@ -169,7 +174,8 @@ def tile_list_msg_silu_gate_kernel(
             )
 
         gather_words(0, 0, J, sbuf([P, J], U32, "v_src"))
-        quantise_weight(0, 0, R)
+        for lo in (0, R // 2):
+            quantise_weight(0, lo, lo + R // 2)
         gather_words(1, 0, HALF, sbuf([P, HALF], U32, "v_dst_first"))
         for lo, hi in ((0, P), (P, 2 * P), (2 * P, R)):
             quantise_weight(1, lo, hi)
@@ -207,7 +213,7 @@ def tile_list_msg_silu_gate_kernel(
         def interleave(h_rows, h_bf):
             nc.scalar.copy(
                 out=h_bf.rearrange("p (c i t) -> p c t i", i=4, t=PACK),
-                in_=h_rows[:].rearrange("p t (c i) -> p c t i", i=4),
+                in_=h_rows.rearrange("p t (c i) -> p c t i", i=4),
             )
 
         h = {}
@@ -268,10 +274,13 @@ def tile_list_msg_silu_gate_kernel(
             nc.scalar.activation(act0[t][:], accs[t][:], ACT.Silu)
             if t > 0:
                 scale(act0[t - 1][:], rows0, t - 1)
-        scale(act0[LAST][:], rows0, LAST)
+        halves = (slice(0, E), slice(E, Q))
+        for cols in halves:
+            nc.scalar.activation(rows0[:, LAST, cols], act0[LAST][:, cols], ACT.Copy, scale=sm_cols[:, LAST:PACK])
         gather_words(1, HALF, J, sbuf([P, HALF], U32, "v_dst_rest", "picked1"))
         h_bf0 = at(51 * KIB, [P, PACK * Q], BF16, "h_bf0")
-        interleave(rows0, h_bf0[:])
+        for cols in halves:
+            interleave(rows0[:, :, cols], h_bf0[:, PACK * cols.start : PACK * cols.stop])
         gated1 = sbuf([P, HALF], F32, "gated1")
         gather_gates(1, q1, q3, gated1[:])
         quantise(h_bf0[:], 0, at(80 * KIB, [P, Q], U32, "h_codes0")[:], wd_plane[:].bitcast(U8)[4:P, 0:Q])
@@ -303,7 +312,7 @@ def tile_list_msg_silu_gate_kernel(
             scale(act1[0][:, t, :], rows1, t)
         activate(accs1[1], act1[1][:], rows1, pairs[1])
         h_bf1 = sbuf([P, PACK * Q], BF16, "h_bf1")
-        interleave(rows1, h_bf1[:])
+        interleave(rows1[:], h_bf1[:])
         empty_last()
         quantise(h_bf1[:], q1, at(61 * KIB - HALF, [P, Q], U32, "h_codes1")[:], sbuf([P, Q], U8, "h_scales1")[:])
         scatter(LAST, 0, q1, msgs[LAST, 0], gated30[:])
@@ -330,7 +339,7 @@ def tile_list_msg_silu_gate_kernel(
         gather_gates(LAST, q3, J, late[:, HALF : 3 * Q])
 
         h_bf2 = sbuf([P, PACK * Q], BF16, "h_bf2")
-        interleave(rows2, h_bf2[:])
+        interleave(rows2[:], h_bf2[:])
         msg31 = at(66 * KIB + 64, [P, Q], F32, "msg31")
         empty(cover, msg31[:])
         quantise(h_bf2[:], q2, at(63 * KIB, [P, Q], U32, "h_codes2")[:], sbuf([P, Q], U8, "h_scales2")[:])
@@ -339,7 +348,7 @@ def tile_list_msg_silu_gate_kernel(
         for acc, act, ts in zip(accs3, act3, pairs):
             activate(acc, act[:], rows3, ts)
         h_bf3 = sbuf([P, PACK * Q], BF16, "h_bf3")
-        interleave(rows3, h_bf3[:])
+        interleave(rows3[:], h_bf3[:])
         messages([(0, q2)], at(71 * KIB + HALF, [P, Q], F32, "msg02")[:], 7)()
         messages([(LAST, q2), (1, q2)], at(73 * KIB, [P, HALF], F32, "msg12")[:], 6)()
         last_acc = bank(2, [P, 2, Q], "y_acc_last")

@@ -38,11 +38,11 @@ def tile_list_msg_silu_gate_kernel(
         psum = ctx.enter_context(tc.psum_pool(name="psum", bufs=1))
         placed = ctx.enter_context(tc.tile_pool(name="placed", bufs=1))
 
-        def sbuf(shape, dtype, name, slot=None):
-            return keep.tile(shape, dtype, name=name, tag=slot or name, align_bytes=64)
+        def sbuf(shape, dtype, name, slot=None, align=64):
+            return keep.tile(shape, dtype, name=name, tag=slot or name, align_bytes=align)
 
         def at(offset, shape, dtype, name):
-            return placed.tile(shape, dtype, name=name, offset=offset, align_bytes=64)
+            return placed.tile(shape, dtype, name=name, offset=offset, align_bytes=64 if offset % 256 else 256)
 
         def bank(b, shape, name):
             return psum.tile(shape, F32, name=name, tag=f"bank{b}")
@@ -67,7 +67,7 @@ def tile_list_msg_silu_gate_kernel(
         nc.scalar.activation(warm_out[:], warm_in[:], ACT.Silu)
 
         identity = sbuf([P, P], F32, "identity")
-        v_plane = sbuf([P, 2 * J // 4], I32, "v_plane")
+        v_plane = sbuf([P, 2 * J // 4], I32, "v_plane", align=256)
         nc.gpsimd.memset(tab_rows[0:ROW0, :], 0)
         nc.gpsimd.memset(identity[:], 0.0)
         nc.gpsimd.memset(v_plane[:], 0)
@@ -80,13 +80,13 @@ def tile_list_msg_silu_gate_kernel(
             nc.gpsimd.memset(tile[:], 0.0)
 
         for n in range(2):
-            zero_out(n, sbuf([P, T], F32, f"out{n}"))
+            zero_out(n, sbuf([P, T], F32, f"out{n}", align=256))
 
         ws_raw = at(16 * KIB, [P, PACK, R], F32, "ws_raw")
         nc.sync.dma_start(out=ws_raw[:], in_=ws.rearrange("(p i) r -> p i r", i=PACK))
-        tab = sbuf([P, T], I32, "tab")
+        tab = sbuf([P, T], I32, "tab", align=256)
         nc.sync.dma_start(out=tab[:], in_=tab_words[0].rearrange("p t i -> p (t i)").bitcast(I32))
-        wt_raw = [at(32 * KIB, [P, PACK, R // 2], F32, "wt_raw0"), sbuf([P, PACK, R // 2], F32, "wt_raw1")]
+        wt_raw = [at(32 * KIB, [P, PACK, R // 2], F32, "wt_raw0"), sbuf([P, PACK, R // 2], F32, "wt_raw1", align=256)]
         for u in range(2):
             cols = slice(u * R // 2, (u + 1) * R // 2)
             nc.sync.dma_start(out=wt_raw[u][:], in_=wt[:, cols].rearrange("(p i) r -> p i r", i=PACK))
@@ -154,7 +154,7 @@ def tile_list_msg_silu_gate_kernel(
         by_place = wd_scales[0].bitcast(I32).rearrange("(q r) w -> r q w", r=4)
         for r in range(4):
             nc.sync.dma_start(out=wd_plane[r:P:32, :], in_=by_place[r])
-        load_gates(2, 24 * KIB - 64)
+        load_gates(2, 24 * KIB - 256)
         wd_codes = at(16 * KIB, [P, N], I32, "wd_codes")
         nc.sync.dma_start(out=wd_codes[:], in_=wd_words[0].rearrange("p n i -> p (n i)").bitcast(I32))
         load_gates(LAST, 32 * KIB + N)

@@ -58,7 +58,7 @@ def tile_list_msg_silu_gate_kernel(
         def entries(i, lo, hi):
             return lists[i][:, lo // GROUP : hi // GROUP]
 
-        edge_cols = sbuf([P, J // P], F32, "edge_cols")
+        edge_cols = at(84 * KIB, [P, J // P], F32, "edge_cols")
         nc.scalar.dma_start(out=edge_cols[:], in_=wgo[0].rearrange("(p c) -> p c", p=P))
 
         warm_in = sbuf([P, 1], F32, "warm_in")
@@ -134,7 +134,7 @@ def tile_list_msg_silu_gate_kernel(
                 nc.tensor.transpose(spread[:, c, :], column, identity[:])
             nc.scalar.copy(out=edge_view[:, b], in_=spread[:].rearrange("p c m -> p m c"))
 
-        w_bf = [sbuf([P, PACK * R], BF16, "w_bf0"), sbuf([P, PACK * R], BF16, "w_bf1")]
+        w_bf = [sbuf([P, PACK * R], BF16, "w_bf0"), at(84 * KIB, [P, PACK * R], BF16, "w_bf1")]
         w_codes = sbuf([P, 2, R], U32, "w_codes")
         w_scales = sbuf([P, 2, R], U8, "w_scales")
         w_view = [w_bf[i][:].rearrange("p (t m i) -> p m i t", t=PACK, i=PACK) for i in range(2)]

from contextlib import ExitStack

import concourse.mybir as mybir
from concourse.masks import make_identity

K, R, N, T, J = 512, 512, 512, 2048, 1024
FLOPS = 2 * J * (2 * K * R + R * N)

F32 = mybir.dt.float32
BF16 = mybir.dt.bfloat16
I32 = mybir.dt.int32
U32 = mybir.dt.uint32
U16 = mybir.dt.uint16
U8 = mybir.dt.uint8
FP8X4 = mybir.dt.float8_e4m3fn_x4
MULT = mybir.AluOpType.mult
ACT = mybir.ActivationFunctionType

P = 128
PACK = 4
GROUP = 16
HALF = J // 2
Q = J // 4
E = J // 8
N_TILES = N // P
ROW0 = P - K // 32
LAST = N_TILES - 1
KIB = 1024


def tile_list_msg_silu_gate_kernel(
    tc, tab_words, tab_scales, ws, wt, sm, wd_words, wd_scales, gT, wgo, offs, offs2, out
):
    nc = tc.nc

    with ExitStack() as ctx:
        keep = ctx.enter_context(tc.tile_pool(name="keep", bufs=1))
        psum = ctx.enter_context(tc.psum_pool(name="psum", bufs=1))
        placed = ctx.enter_context(tc.tile_pool(name="placed", bufs=1))

        def sbuf(shape, dtype, name, slot=None, align=64):
            return keep.tile(shape, dtype, name=name, tag=slot or name, align_bytes=align)

        def at(offset, shape, dtype, name):
            return placed.tile(shape, dtype, name=name, offset=offset, align_bytes=64 if offset % 256 else 256)

        def bank(b, shape, name):
            return psum.tile(shape, F32, name=name, tag=f"bank{b}")

        src_list = keep.tile([P, J // GROUP], U16, name="src_list")
        dst_list = keep.tile([P, J // GROUP], U16, name="dst_list")
        tab_rows = at(7 * KIB, [P, T // 4], I32, "tab_rows")
        nc.scalar.dma_start(out=tab_rows[ROW0:P, :], in_=tab_scales[0].bitcast(I32))
        nc.sync.dma_start(src_list[:], offs)
        nc.sync.dma_start(dst_list[:], offs2)
        lists = (src_list, dst_list)

        def entries(i, lo, hi):
            return lists[i][:, lo // GROUP : hi // GROUP]

        edge_cols = at(84 * KIB, [P, J // P], F32, "edge_cols")
        nc.scalar.dma_start(out=edge_cols[:], in_=wgo[0].rearrange("(p c) -> p c", p=P))

        warm_in = sbuf([P, 1], F32, "warm_in")
        warm_out = sbuf([P, 1], F32, "warm_out")
        nc.gpsimd.memset(warm_in[:], 0.0)
        nc.scalar.activation(warm_out[:], warm_in[:], ACT.Silu)

        identity = sbuf([P, P], F32, "identity")
        v_plane = sbuf([P, 2 * J // 4], I32, "v_plane", align=256)
        nc.gpsimd.memset(tab_rows[0:ROW0, :], 0)
        nc.gpsimd.memset(identity[:], 0.0)
        nc.gpsimd.memset(v_plane[:], 0)
        make_identity(nc, identity[:], nomemset=True)

        outs = {}

        def zero_out(n, tile):
            outs[n] = tile
            nc.gpsimd.memset(tile[:], 0.0)

        for n in range(2):
            zero_out(n, sbuf([P, T], F32, f"out{n}", align=256))

        ws_raw = at(16 * KIB, [P, PACK, R], F32, "ws_raw")
        nc.sync.dma_start(out=ws_raw[:], in_=ws.rearrange("(p i) r -> p i r", i=PACK))
        tab = sbuf([P, T], I32, "tab", align=256)
        nc.sync.dma_start(out=tab[:], in_=tab_words[0].rearrange("p t i -> p (t i)").bitcast(I32))
        wt_raw = [at(32 * KIB, [P, PACK, R // 2], F32, "wt_raw0"), sbuf([P, PACK, R // 2], F32, "wt_raw1", align=256)]
        for u in range(2):
            cols = slice(u * R // 2, (u + 1) * R // 2)
            nc.sync.dma_start(out=wt_raw[u][:], in_=wt[:, cols].rearrange("(p i) r -> p i r", i=PACK))
        sm_cols = sbuf([P, PACK], F32, "sm_cols")
        nc.sync.dma_start(out=sm_cols[:], in_=sm.rearrange("(p t) -> p t", t=PACK))

        picked = {
            0: sbuf([P, 2 * Q], U8, "picked0"),
            HALF: at(61 * KIB, [P, 2 * HALF], U8, "picked2"),
            Q: sbuf([P, 2 * Q], U8, "picked1"),
        }
        for lo, tile in picked.items():
            width = tile.shape[1] // 2
            for i in range(2):
                nc.vector.tensor_copy(
                    tile[:, i * width : (i + 1) * width],
                    tab_rows[:].bitcast(U8).indirect(entries(i, lo, lo + width)),
                )

        def move_scale_rows(lo):
            words = slice(2 * lo // 4, (2 * lo + picked[lo].shape[1]) // 4)
            for q in range(4):
                nc.sync.dma_start(
                    out=v_plane[32 * q : 32 * q + 4, words],
                    in_=picked[lo][ROW0 + 4 * q : ROW0 + 4 * q + 4, :].bitcast(I32),
                )

        move_scale_rows(0)
        gates = {}

        def load_gates(n, offset):
            gates[n] = at(offset, [P, T], F32, f"gates{n}")
            nc.sync.dma_start(out=gates[n][:], in_=gT[n * P : (n + 1) * P, :])

        load_gates(0, 0)
        move_scale_rows(Q)
        load_gates(1, 8 * KIB)

        edge_w = sbuf([P, J], F32, "edge_w")
        edge_view = edge_w[:].rearrange("p (m b c) -> p b m c", b=2, c=4)
        for b in range(2):
            spread = bank(6 + b, [P, 4, P], f"spread{b}")
            for c in range(4):
                column = edge_cols[:, 4 * b + c : 4 * b + c + 1].to_broadcast([P, P])
                nc.tensor.transpose(spread[:, c, :], column, identity[:])
            nc.scalar.copy(out=edge_view[:, b], in_=spread[:].rearrange("p c m -> p m c"))

        w_bf = [sbuf([P, PACK * R], BF16, "w_bf0"), at(84 * KIB, [P, PACK * R], BF16, "w_bf1")]
        w_codes = sbuf([P, 2, R], U32, "w_codes")
        w_scales = sbuf([P, 2, R], U8, "w_scales")
        w_view = [w_bf[i][:].rearrange("p (t m i) -> p m i t", t=PACK, i=PACK) for i in range(2)]
        slot_pairs = (slice(0, 2), slice(2, PACK))
        for ts in slot_pairs:
            nc.scalar.copy(
                out=w_view[0][:, :, :, ts], in_=ws_raw[:].rearrange("p i (m t) -> p m i t", t=PACK)[:, :, :, ts]
            )
        for u in range(2):
            for ts in slot_pairs:
                nc.scalar.copy(
                    out=w_view[1][:, u * P // 2 : (u + 1) * P // 2, :, ts],
                    in_=wt_raw[u][:].rearrange("p i (m t) -> p m i t", t=PACK)[:, :, :, ts],
                )
        wd_plane = at(32 * KIB, [P, N // 4], I32, "wd_plane")
        nc.gpsimd.memset(wd_plane[:], 0)
        by_place = wd_scales[0].bitcast(I32).rearrange("(q r) w -> r q w", r=4)
        for r in range(4):
            nc.sync.dma_start(out=wd_plane[r:P:32, :], in_=by_place[r])
        load_gates(2, 24 * KIB - 256)
        wd_codes = at(16 * KIB, [P, N], I32, "wd_codes")
        nc.sync.dma_start(out=wd_codes[:], in_=wd_words[0].rearrange("p n i -> p (n i)").bitcast(I32))
        load_gates(LAST, 32 * KIB + N)
        move_scale_rows(HALF)

        v_codes = {}

        def gather_words(i, lo, hi, tile):
            v_codes[i, lo] = tile
            nc.vector.tensor_copy(tile[:], tab[:].bitcast(U32).indirect(entries(i, lo, hi)))

        def quantise_weight(i, lo, hi):
            nc.vector.quantize_mx(
                out=w_codes[:, i, lo:hi].bitcast(FP8X4),
                scales=w_scales[:, i, lo:hi],
                in_=w_bf[i][:, PACK * lo : PACK * hi],
            )

        gather_words(0, 0, J, sbuf([P, J], U32, "v_src"))
        for lo in (0, R // 2):
            quantise_weight(0, lo, lo + R // 2)
        gather_words(1, 0, HALF, sbuf([P, HALF], U32, "v_dst_first"))
        for lo, hi in ((0, P), (P, 2 * P), (2 * P, R)):
            quantise_weight(1, lo, hi)

        def project(i, t, lo, hi, acc):
            rows = slice(t * P, (t + 1) * P)
            start = max(s for j, s in v_codes if j == i and s <= lo)
            group = max(s for s in picked if s <= lo)
            plane = 2 * group + i * picked[group].shape[1] // 2 + lo - group
            nc.tensor.matmul_mx(
                out=acc,
                lhsT=w_codes[:, i, rows].bitcast(FP8X4),
                lhsT_scale=w_scales[:, i, rows],
                rhs=v_codes[i, start][:, lo - start : hi - start].bitcast(FP8X4),
                rhs_scale=v_plane[:].bitcast(U8)[:, plane : plane + hi - lo],
                start=(i == 0),
                stop=(i == 1),
            )

        def sums(ts, lo, hi, b):
            acc = bank(b, [P, len(ts), hi - lo], f"acc{lo}_{ts[0]}")
            for u, t in enumerate(ts):
                for i in range(2):
                    project(i, t, lo, hi, acc[:, u, :])
            return acc

        def activate(acc, act, h_rows, ts):
            nc.scalar.activation(act, acc[:], ACT.Silu)
            for u, t in enumerate(ts):
                scale(act[:, u, :], h_rows, t)

        def scale(act_row, h_rows, t):
            nc.scalar.activation(h_rows[:, t, :], act_row, ACT.Copy, scale=sm_cols[:, t : t + 1])

        def interleave(h_rows, h_bf):
            nc.scalar.copy(
                out=h_bf.rearrange("p (c i t) -> p c t i", i=4, t=PACK),
                in_=h_rows.rearrange("p t (c i) -> p c t i", i=4),
            )

        h = {}

        def quantise(h_bf, lo, h_codes, h_scales):
            nc.vector.quantize_mx(out=h_codes.bitcast(FP8X4), scales=h_scales, in_=h_bf)
            h[lo] = h_codes, h_scales

        msgs, gated = {}, {}

        def message(n, lo, acc):
            h_codes, h_scales = h[lo]
            rows = slice(n * P, (n + 1) * P)
            nc.tensor.matmul_mx(
                out=acc,
                lhsT=wd_codes[:, rows].bitcast(FP8X4),
                lhsT_scale=wd_plane[:].bitcast(U8)[:, rows],
                rhs=h_codes.bitcast(FP8X4),
                rhs_scale=h_scales,
                start=True,
                stop=True,
            )

        def empty(acc, dest):
            nc.scalar.copy(out=dest, in_=acc[:].rearrange("p a w -> p (a w)"))

        def messages(parts, dest, b):
            acc = bank(b, [P, len(parts), Q], f"y_acc{parts[0][0]}_{parts[0][1]}")
            for place, (n, lo) in enumerate(parts):
                message(n, lo, acc[:, place, :])
                msgs[n, lo] = dest[:, place * Q : (place + 1) * Q]
            return lambda: empty(acc, dest)

        def gather_gates(n, lo, hi, dest, factor=None):
            factor = edge_w[:, lo:hi] if factor is None else factor
            nc.vector.tensor_tensor(dest, gates[n][:].indirect(entries(0, lo, hi)), factor, MULT)

        def scatter(n, lo, hi, a, b):
            nc.vector.tensor_tensor(outs[n][:].indirect(entries(1, lo, hi)), a, b, MULT)
            if hi == J and n != 2:
                nc.sync.dma_start(out=out[n * P : (n + 1) * P, :], in_=outs[n][:])
            elif hi == J:
                cut = 3 * T // 8
                nc.sync.dma_start(out=out[n * P : (n + 1) * P, 0:cut], in_=outs[n][:, 0:cut])
                nc.scalar.dma_start(out=out[n * P : (n + 1) * P, cut:T], in_=outs[n][:, cut:T])

        q1, q2, q3 = Q, 2 * Q, 3 * Q

        gated0 = sbuf([P, J], F32, "gated0")
        gather_gates(0, 0, J, gated0[:])
        act0 = [sbuf([P, Q], F32, f"act0_{t}") for t in range(PACK)]
        rows0 = sbuf([P, PACK, Q], BF16, "rows0", "rows0_act1")
        accs = [bank(t, [P, Q], f"acc0_{t}") for t in range(PACK)]
        for t in range(PACK):
            project(0, t, 0, Q, accs[t][:])
        for t in range(PACK):
            project(1, t, 0, Q, accs[t][:])
            nc.scalar.activation(act0[t][:], accs[t][:], ACT.Silu)
            if t > 0:
                scale(act0[t - 1][:], rows0, t - 1)
        halves = (slice(0, E), slice(E, Q))
        for cols in halves:
            nc.scalar.activation(rows0[:, LAST, cols], act0[LAST][:, cols], ACT.Copy, scale=sm_cols[:, LAST:PACK])
        gather_words(1, HALF, J, sbuf([P, HALF], U32, "v_dst_rest", "picked1"))
        h_bf0 = at(51 * KIB, [P, PACK * Q], BF16, "h_bf0")
        for cols in halves:
            interleave(rows0[:, :, cols], h_bf0[:, PACK * cols.start : PACK * cols.stop])
        gated1 = sbuf([P, HALF], F32, "gated1")
        gather_gates(1, q1, q3, gated1[:])
        quantise(h_bf0[:], 0, at(80 * KIB, [P, Q], U32, "h_codes0")[:], wd_plane[:].bitcast(U8)[4:P, 0:Q])
        gated20 = sbuf([P, Q], F32, "gated20")
        gather_gates(2, 0, q1, gated20[:])
        upper2 = sbuf([P, 3 * Q], F32, "upper2")
        gather_gates(2, q2, q3, upper2[:, 0:Q])
        for n in (2, LAST):
            zero_out(n, at((44 + 8 * (n - 2)) * KIB, [P, T], F32, f"out{n}"))

        pairs = ((0, 1), (2, 3))
        accs1 = [sums(ts, q1, q2, b) for b, ts in enumerate(pairs)]
        act1 = [sbuf([P, 2, Q], F32, "act1_0", "rows0_act1"), at(80 * KIB + HALF, [P, 2, Q], F32, "act1_1")]
        nc.scalar.activation(act1[0][:], accs1[0][:], ACT.Silu)
        messages([(0, 0)], sbuf([P, Q], F32, "msg00")[:], 4)()
        messages([(1, 0), (2, 0)], upper2[:, Q : 3 * Q], 5)()
        empty_last = messages([(LAST, 0)], at(61 * KIB + HALF, [P, Q], F32, "msg30")[:], 6)
        scatter(0, 0, q1, msgs[0, 0], gated0[:, 0:q1])
        product10 = sbuf([P, Q], F32, "product10")
        gather_gates(1, 0, q1, product10[:], msgs[1, 0])
        scatter(2, 0, q1, msgs[2, 0], gated20[:])
        gather_gates(2, q3, J, upper2[:, Q:HALF])
        scatter(1, 0, q1, product10[:], edge_w[:, 0:q1])
        gated30 = sbuf([P, Q], F32, "gated30")
        gather_gates(LAST, 0, q1, gated30[:])

        rows1 = at(78 * KIB + HALF, [P, PACK, Q], BF16, "rows1")
        for t in pairs[0]:
            scale(act1[0][:, t, :], rows1, t)
        activate(accs1[1], act1[1][:], rows1, pairs[1])
        h_bf1 = sbuf([P, PACK * Q], BF16, "h_bf1")
        interleave(rows1[:], h_bf1[:])
        empty_last()
        quantise(h_bf1[:], q1, at(61 * KIB - HALF, [P, Q], U32, "h_codes1")[:], sbuf([P, Q], U8, "h_scales1")[:])
        scatter(LAST, 0, q1, msgs[LAST, 0], gated30[:])
        rows2 = at(66 * KIB, [P, PACK, Q], BF16, "rows2")
        rows3 = at(72 * KIB, [P, PACK, Q], BF16, "rows3")
        act2 = [sbuf([P, 2, Q], F32, f"act2_{b}") for b in range(2)]
        accs2 = [sums(ts, q2, q3, 2 + b) for b, ts in enumerate(pairs)]
        accs3 = [sums(ts, q3, J, b) for b, ts in enumerate(pairs)]
        for acc, act, ts in zip(accs2, act2, pairs):
            activate(acc, act[:], rows2, ts)
        late = sbuf([P, 3 * Q], F32, "late", "act2_1")
        messages([(0, q1)], late[:, 0:Q], 7)()
        messages([(2, q1), (1, q1)], late[:, Q : 3 * Q], 4)()
        cover = bank(5, [P, 1, Q], "y_acc3_cover")
        message(LAST, q1, cover[:, 0, :])
        gated31 = sbuf([P, Q], F32, "gated31", "act2_0")
        gather_gates(LAST, q1, q2, gated31[:])
        scatter(0, q1, q2, msgs[0, q1], gated0[:, q1:q2])
        product21 = at(63 * KIB, [P, Q], F32, "product21")
        gather_gates(2, q1, q2, product21[:], msgs[2, q1])
        scatter(1, q1, q2, msgs[1, q1], gated1[:, 0:Q])
        gather_gates(1, q3, J, late[:, Q:HALF])
        scatter(2, q1, q2, product21[:], edge_w[:, q1:q2])
        gather_gates(LAST, q3, J, late[:, HALF : 3 * Q])

        h_bf2 = sbuf([P, PACK * Q], BF16, "h_bf2")
        interleave(rows2[:], h_bf2[:])
        msg31 = at(66 * KIB + 64, [P, Q], F32, "msg31")
        empty(cover, msg31[:])
        quantise(h_bf2[:], q2, at(63 * KIB, [P, Q], U32, "h_codes2")[:], sbuf([P, Q], U8, "h_scales2")[:])
        scatter(LAST, q1, q2, msg31[:], gated31[:])
        act3 = [at(67 * KIB + 64, [P, 2, Q], F32, "act3_0"), at(64 * KIB + 64, [P, 2, Q], F32, "act3_1")]
        for acc, act, ts in zip(accs3, act3, pairs):
            activate(acc, act[:], rows3, ts)
        h_bf3 = sbuf([P, PACK * Q], BF16, "h_bf3")
        interleave(rows3[:], h_bf3[:])
        messages([(0, q2)], at(71 * KIB + HALF, [P, Q], F32, "msg02")[:], 7)()
        messages([(LAST, q2), (1, q2)], at(73 * KIB, [P, HALF], F32, "msg12")[:], 6)()
        last_acc = bank(2, [P, 2, Q], "y_acc_last")
        message(2, q2, last_acc[:, 0, :])
        gated32 = at(68 * KIB, [P, Q], F32, "gated32")
        gather_gates(LAST, q2, q3, gated32[:])
        quantise(h_bf3[:], q3, sbuf([P, Q], U32, "h_codes3")[:], sbuf([P, Q], U8, "h_scales3")[:])
        scatter(0, q2, q3, msgs[0, q2], gated0[:, q2:q3])

        messages([(0, q3), (1, q3)], sbuf([P, HALF], F32, "msg03")[:], 4)()
        messages([(LAST, q3)], sbuf([P, Q], F32, "msg33")[:], 3)()
        message(2, q3, last_acc[:, 1, :])
        msg22 = sbuf([P, HALF], F32, "msg22")
        empty(last_acc, msg22[:])
        scatter(1, q2, q3, msgs[1, q2], gated1[:, Q:HALF])
        scatter(0, q3, J, msgs[0, q3], gated0[:, q3:J])
        scatter(LAST, q2, q3, msgs[LAST, q2], gated32[:])
        scatter(1, q3, J, msgs[1, q3], late[:, Q:HALF])
        scatter(LAST, q3, J, msgs[LAST, q3], late[:, HALF : 3 * Q])
        scatter(2, q2, J, msg22[:], upper2[:, 0:HALF])
